import numpy as np, ml_dtypes
CORES = [1,5,17,21,33,37,49,53]
N = 8
BF = ml_dtypes.bfloat16
W, V, L, S, T, E = 4096, 1024, 128, 32, 5, 2
def parts(rng):
    x = (64 * rng.random((N, 8, 16, W)) * (0.5 + 0.5 * rng.random((N, 8, 1, W)))).astype(np.int64)
    im = (64 * rng.random((N, 8, 16, V)) * (0.25 + 0.75 * rng.random((N, 8, 1, V)))).astype(np.int64)
    z = (64 * rng.random((N, 8, 16, 2, L)) * (0.5 + 0.5 * rng.random((N, 8, 1, 2, L)))).astype(np.int64)
    b = rng.integers(0, W, (N, 8, 16, V)); q = np.minimum((8 * rng.random((N, 8, 16, V)) ** 0.6).astype(np.int64), 7)
    return x, im, b, q, z, rng.integers(1, 4096, (N, 8, 16))
def pack(x, im, b, q, z, w):
    return {"geno": x.reshape(N, 128, W).astype(np.float32).astype(BF), "immun": im.reshape(N, 128, V).astype(np.float32).astype(BF),
            "bank": (b + W * q).reshape(N, 128, V).astype(np.int32), "bites": z.reshape(N, 128, 2 * L).astype(np.float32).astype(BF), "wt": w.reshape(N, 128, 1).astype(np.int32)}
def first(z, w):
    u = np.sum(w[:, :, :, None] * z[:, :, :, 0], axis=2) & 4095
    return ((u * u >> 5) + 37 * u) & (V - 1)
def setup_inputs(rng):
    return pack(*parts(rng))
def setup_inputs_corners(rng):
    x, im, b, q, z, w = parts(rng); w[:, :, 0] = 4095; w[:, :, 1] = 2048
    kind = rng.integers(0, 4, (N, 8, 1, V)); im = np.where(kind == 0, 0, np.where(kind == 1, 63, im))
    mode = rng.integers(0, 7, (N, 8, 1, V)); pos = np.argsort(rng.random((N, 8, 16, V)), axis=2); near = E - 1 + rng.integers(0, 3, q.shape)
    q = np.where(mode == 5, q[:, :, :1], q); q = np.where(mode == 4, near, q); q = np.where(mode == 3, 7 * (pos < 2), q)
    q = np.where(mode == 2, 7 * (pos < 1), q); q = np.where(mode == 1, 0, q); q = np.where(mode == 0, 7, q)
    edge = rng.integers(0, 4, (N, 8, 1, V)); b = np.where(edge == 0, (W - 1) * rng.integers(0, 2, b.shape), b); b = np.where(edge == 1, b[:, :, :1], b)
    z[:, :, :, 0, 4:L - 1] = np.maximum(z[:, :, :, 0, 4:L - 1], 1)
    z[:, :, :, :, 0] = 0; z[:, :, :, :, 1] = 63; z[:, :, :, :, 2] = 0; z[:, :, 1, :, 2] = 1; z[:, :, :, :, L - 1] = 0; z[:, :, 0, :, L - 1] = 1
    v = first(z, w); n = L // 2; m = L // 8
    for a in range(N):
        for g in range(8):
            lanes = (4 + rng.permutation(L - 5))[:n]; zz = z[a, g, :, 0][:, lanes]
            po = np.argsort(rng.random((16, n)), axis=0); cnt = 8 + np.arange(n) % 3
            im[a, g][:, v[a, g, lanes]] = zz - (po < cnt)
            own = lanes[:m]; k = rng.integers(0, 16, m); h = v[a, g, own]
            b[a, g, k, h] = S * own; q[a, g, k, h] = 7
            x[a, g][:, S * own] = np.where(zz[:, :m] < 32, 63, 0)
    return pack(x, im, b, q, z, w)
def setup_inputs_crowd(rng):
    x, im, b, q, z, w = parts(rng); w = np.repeat(rng.integers(1, 4096, (N, 8, 1)), 16, axis=2)
    for a in range(N):
        for g in range(8):
            for c in range(2):
                n = int(rng.choice(np.array([1, 2, 5, 17, 30])))
                if g == a % 8 and c == 0: n = 1
                if g == (a + 3) % 8 and c == 0: continue
                base = z[a, g, :, c, :n].copy()[:, rng.integers(0, n, L)]
                z[a, g, :, c] = np.take_along_axis(base, np.argsort(rng.random((16, L)), axis=0), 0)
        g = (a + 3) % 8; w[a, g] = rng.integers(1, 4096, 16); w[a, g, 0] = 1; w[a, g, 15] = 64
        u = rng.permutation(4096); u = u[np.unique(((u * u >> 5) + 37 * u) & (V - 1), return_index=True)[1]]
        need = (rng.permutation(u)[:L] - np.sum(w[a, g, 1:15, None] * z[a, g, 1:15, 0], axis=0)) & 4095
        z[a, g, 0, 0] = need & 63; z[a, g, 15, 0] = need >> 6
    return pack(x, im, b, q, z, w)
def setup_inputs_ends(rng):
    def rec(n):
        k = rng.integers(0, 3, (N, 8, 1, n)); return 63 * np.where(k == 2, rng.integers(0, 2, (N, 8, 16, n)), k)
    x = rec(W); im = rec(V); z = rec(2 * L).reshape(N, 8, 16, 2, L); w = np.where(rng.integers(0, 2, (N, 8, 16)) == 1, 4095, 1); w[N - 1, 7] = 4095
    x[:, 1::2, :, W - 1] = 0; x[:, ::2, :, W - 1] = 63 * rng.integers(0, 2, (N, 4, 16))
    nz = rng.integers(0, 8, (8, 1, L)) * rng.integers(0, 2, (8, 1, L)); nz[:, :, 0] = 0; nz[:, :, L - 1] = 0
    nz[0, 0, ::2] = 0; nz[0, 0, 1] = 1; nz[0, 0, L - 1] = 0
    z[N - 1, :, :, 0] = 63 * (np.argsort(rng.random((8, 16, L)), axis=1) >= nz)
    z[1, :, :, 0] = 63 * (np.argsort(rng.random((8, 16, L)), axis=1) >= rng.integers(0, 8, (8, 1, L)))
    v = first(z, w); r = np.arange(16)[None, None, :, None]; mode = rng.integers(0, 5, (N, 8, 1, V))
    fl = (mode == 0) | ((mode == 1) & (r >= 14)) | ((mode == 2) & ((r == 0) | (r == 15))) | ((mode == 4) & (rng.random((N, 8, 16, V)) < 0.5))
    anyb = (rng.random((N, 8, 1, V)) < 0.5) & fl
    for g in range(8):
        for a in (1, N - 1):
            h = v[a, g]; fl[a, g, 14:][:, h] = True; anyb[a, g][:, h] = False; im[a, g][:, h] = 0
        im[0, g][:, v[0, g]] = 63
    im[N - 1, 0][:, v[N - 1, 0, 1]] = 63
    woke = 16 * L - 2 * int(np.sum(v[N - 1, 0] == v[N - 1, 0, 1])); assert woke > 15 * L and woke & (V - 1) != 0
    b = np.where(fl, np.where(anyb, rng.integers(0, W, fl.shape), W - 1), 0); q = 7 * fl
    for g, ks in ((1, (2, 5, 9)), (3, (0, 1, 15)), (5, (13, 14, 15))):
        h = v[N - 1, g, 0]; x[N - 1, g, :, W - 2] = 0; x[N - 1, g, rng.integers(0, 16), W - 2] = 1
        b[N - 1, g, :, h] = 0; q[N - 1, g, :, h] = 0
        for k, c in zip(ks, (W - 2, W - 2, W - 1)):
            b[N - 1, g, k, h] = c; q[N - 1, g, k, h] = 7
    return pack(x, im, b, q, z, w)
def setup_inputs_spread(rng):
    x, im, b, q, z, w = parts(rng)
    def pw(*s): return rng.random(s) ** np.exp2(rng.integers(-2, 4, s[:2] + (1,) + s[3:]))
    x = np.minimum((64 * pw(N, 8, 16, W)).astype(np.int64), 63); im = np.minimum((64 * pw(N, 8, 16, V)).astype(np.int64), 63)
    z = np.minimum((64 * pw(N, 8, 16, 2, L)).astype(np.int64), 63); b = np.minimum((W * pw(N, 8, 16, V)).astype(np.int64), W - 1)
    q = np.minimum((8 * rng.random((N, 8, 16, V)) ** np.exp2(rng.integers(-2, 2, (N, 8, 1, V)))).astype(np.int64), 7)
    w = np.minimum(np.exp2(12 * rng.random((N, 8, 16))).astype(np.int64), 4095)
    return pack(x, im, b, q, z, np.maximum(w, 1))
def setup_inputs_ties(rng):
    lv = rng.integers(0, 3, (N, 8, 1, W)); x = lv + rng.integers(0, 3, (N, 8, 16, W)); im = rng.integers(0, 3, (N, 8, 16, V))
    z = rng.integers(0, 3, (N, 8, 1, 2, L)) + rng.integers(0, 3, (N, 8, 16, 2, L)); w = rng.integers(1, 4096, (N, 8, 16)); b = rng.integers(0, W, (N, 8, 16, V))
    q = np.where(rng.random((N, 8, 16, V)) < 0.5, rng.integers(0, 8, (N, 8, 1, V)), rng.integers(4, 8, (N, 8, 1, V)))
    x[:, ::2, :, W // 2:] = x[:, ::2, :, :W // 2]; b[:, :, 8:, ::2] = b[:, :, :8, ::2]
    z[:, :, :, 0, ::4] = np.take_along_axis(x, rng.integers(0, W, (N, 8, 1, L // 4)), 3)
    x[:, 1::2] += 59; im[:, 1::2] += 59; z[:, 1::2] += 59
    r = np.arange(16)[:, None]; x[:, 2] = (r + np.arange(W)) % 3; z[:, 2, :, 0] = (r + np.arange(L)) % 3; im[:, 2] = 0
    same = ((4, 0, [15]), (6, L // 2, [2, 15]), (7, L - 1, [15])); cz = rng.integers(0, W, (N, 8))
    for a in range(N):
        for g, j, ks in same:
            e = 59 * (g % 2) + rng.integers(1, 3, 16); z[a, g, :, 0, j] = e; x[a, g, :, cz[a, g]] = e
    v = first(z, w)
    for a in range(N):
        for j in range(3):
            h = v[a, 2, j]; q[a, 2, :, h] = 0; q[a, 2, 3, h] = 7; q[a, 2, 12, h] = 7
            b[a, 2, 3, h] = 3 * rng.integers(0, W // 3) + (j + 1) % 3; b[a, 2, 12, h] = 3 * rng.integers(0, W // 3) + (j + 2) % 3
        for g, j, ks in same:
            h = v[a, g, j]; im[a, g, :, h] = 0; q[a, g, :, h] = 0; b[a, g, 15, h] = cz[a, g]
            for k in ks: q[a, g, k, h] = 7
    return pack(x, im, b, q, z, w)
def check_inputs(d):
    bad = []
    for k, lo, hi in (("geno", 0, 63), ("immun", 0, 63), ("bank", 0, 8 * W - 1), ("bites", 0, 63), ("wt", 1, 4095)):
        a = np.asarray(d[k]).astype(np.float64)
        if not np.all((a >= lo) & (a <= hi)): bad.append("range of " + k)
        elif np.any(a != np.floor(a)): bad.append("whole numbers of " + k)
    return bad
def beats(a, c):
    return (np.sum(a > c, axis=2) >= 9).astype(np.int64)
def reference(geno, immun, bank, bites, wt):
    X = geno.astype(np.float32).astype(np.int64).reshape(N, 8, 16, W); im = immun.astype(np.float32).astype(np.int64).reshape(N, 8, 16, V)
    bk = bank.astype(np.int64).reshape(N, 8, 16, V); z = bites.astype(np.float32).astype(np.int64).reshape(N, 8, 16, 2, L); w = wt.astype(np.int64).reshape(N, 8, 16, 1)
    todo = [z[:, :, :, 0], np.roll(z[:, :, :, 1], 1, axis=0)]
    A = np.zeros(N, np.int64); row = np.arange(16)[None, None, :, None]; lane = np.arange(L)[None, None, None, :]
    for t in range(T):
        s = todo[t]
        u = np.sum(w * s, axis=2) & 4095; v = ((u * u >> 5) + 37 * u + A[:, None, None]) & (V - 1)
        e = np.take_along_axis(bk, v[:, :, None, :], 3); b = e & (W - 1); q = e // W
        iv = np.take_along_axis(im, v[:, :, None, :], 3)
        c = np.take_along_axis(X, b.reshape(N, 8, 1, 16 * L), 3).reshape(N, 8, 16, 16, L)
        D = np.sum(np.abs(c - s[:, :, :, None, :]), axis=2)
        sick = np.sum(s > iv, axis=2) >= 9
        key = np.where((q >= t + E) & sick[:, :, None, :], D * 16 + 15 - row, -1)
        k1 = np.argmax(key, axis=2); h1 = (np.max(key, axis=2) >= 0).astype(np.int64)
        key = np.where(row == k1[:, :, None, :], -1, key)
        k2 = np.argmax(key, axis=2); h2 = (np.max(key, axis=2) >= 0).astype(np.int64)
        a1 = np.take_along_axis(c, k1[:, :, None, None, :], 3)[:, :, :, 0]; a2 = np.take_along_axis(c, k2[:, :, None, None, :], 3)[:, :, :, 0]
        n0 = h1 * beats(a1, s) + h2 * beats(a2, s); n1 = beats(s, a1) + h2 * beats(a2, a1); n2 = beats(s, a2) + beats(a1, a2)
        o = np.argsort(np.stack([n0 * 4, np.where(h1 == 1, n1 * 4 + 1, 97), np.where(h2 == 1, n2 * 4 + 2, 98)]), axis=0)
        st = np.stack([s, a1, a2]); second = np.where(h1 == 1, o[1], 0)
        f = np.take_along_axis(st, o[0][None, :, :, None, :], 0)[0]; m = np.take_along_axis(st, second[None, :, :, None, :], 0)[0]
        todo.append(np.roll(np.where((u[:, :, None, :] >> (row & 7)) & 1 == 1, f, m), 2, axis=0))
        wake = ((row == k1[:, :, None, :]) & (h1[:, :, None, :] == 1)) | ((row == k2[:, :, None, :]) & (h2[:, :, None, :] == 1))
        q = np.where(wake, 0, q); slot = np.argmin(q * 16 + row, axis=2)
        e = np.where(row == slot[:, :, None, :], S * lane + t + W * (8 + t), b + W * q); iv = np.maximum(iv - 1, f)
        for a in range(N):
            for g in range(8):
                hv, fi = np.unique(v[a, g], return_index=True)
                bk[a, g][:, hv] = e[a, g][:, fi]; im[a, g][:, hv] = iv[a, g][:, fi]
        X[:, :, :, t::S] = s
        A = np.sum(h1 + h2, axis=(1, 2))
    return {"ybank": bk.reshape(N, 128, V).astype(np.float32), "yimm": im.reshape(N, 128, V).astype(np.float32).astype(BF), "ygeno": X.reshape(N, 128, W).astype(np.float32).astype(BF)}

@@ -1,0 +1,648 @@
+import numpy as np
+from concourse.mybir import AluOpType as OP, AxisListType, ActivationFunctionType as AF
+
+NST = 5
+XS = 257
+THR = 16384.0
+DIST = ((0, 0), (0, 64), (64, 96), (96, 128))
+BIG = 2.0 ** 20
+ON_DVE = (0, 2, 4, 6)
+
+SCRATCH = {
+    "G": ("sbuf", [128, 4096], "bfloat16"), "BKI": ("sbuf", [128, 1024], "int32"),
+    "BK": ("sbuf", [128, 1152], "float32"), "IM": ("sbuf", [128, 1152], "bfloat16"),
+    "ZB": ("sbuf", [128, 256], "bfloat16"), "WI": ("sbuf", [128, 1], "int32"),
+    "Z1": ("sbuf", [128, 128], "bfloat16"), "Z2": ("sbuf", [128, 128], "bfloat16"),
+    "Z3": ("sbuf", [128, 128], "bfloat16"), "Z4": ("sbuf", [128, 128], "bfloat16"),
+    "CR": ("sbuf", [128, 384], "bfloat16"), "HI": ("sbuf", [128, 640], "bfloat16"), "TI": ("sbuf", [128, 640], "bfloat16"),
+    "X0": ("sbuf", [128, 8 * XS], "bfloat16"), "X1": ("sbuf", [128, 8 * XS], "bfloat16"),
+    "AB": ("sbuf", [128, 2048], "bfloat16"), "EQ": ("sbuf", [128, 1024], "bfloat16"),
+    "SEL": ("sbuf", [128, 512], "bfloat16"), "MK2": ("sbuf", [128, 128], "bfloat16"),
+    "cI": ("sbuf", [128, 128], "int32"), "cg": ("sbuf", [128, 640], "int32"), "cm": ("sbuf", [128, 128], "int32"),
+    "pc": ("sbuf", [128, 32], "int32"), "pf": ("sbuf", [128, 64], "float32"),
+    "tw": ("sbuf", [128, 128], "float32"), "tf": ("sbuf", [128, 128], "float32"), "tf2": ("sbuf", [128, 128], "float32"),
+    "rows": ("sbuf", [128, 1024], "bfloat16"),
+    "oXA": ("sbuf", [128, 16], "uint16"),
+    "P0": ("psum", [128, 512], "float32"), "P1": ("psum", [128, 512], "float32"), "P2": ("psum", [128, 512], "float32"),
+    "P3": ("psum", [128, 512], "float32"), "P4": ("psum", [128, 512], "float32"), "P5": ("psum", [128, 512], "float32"),
+    "P6": ("psum", [128, 512], "float32"), "P7": ("psum", [128, 512], "float32"),
+}
+for _n in ("I", "nI", "BO", "cap", "KF", "KC", "ONES", "HALF", "I16", "nI16", "nI256", "D32", "Kc", "Kn", "CO1", "CO2",
+           "WH", "WL", "VH", "VL",
+           "zT0", "zT1", "BE", "BD", "DM", "qt", "ivm", "Fs", "Sg", "W", "E1", "wq", "S", "nim"):
+    SCRATCH[_n] = ("sbuf", [128, 128], "bfloat16")
+for _n in ("R8", "G16", "hv"):
+    SCRATCH[_n] = ("sbuf", [128, 8], "bfloat16")
+for _n in ("Ui", "u", "sq", "s5", "bb", "bbm", "ub", "ubm", "bi", "bm"):
+    SCRATCH[_n] = ("sbuf", [128, 128], "int32")
+for _n in ("mb", "sw0", "sw1", "c", "h3", "e2", "s3", "t1", "nb"):
+    SCRATCH[_n] = ("sbuf", [128, 128], "float32")
+for _n in ("goff0", "goff1", "soff0", "soff1"):
+    SCRATCH[_n] = ("sbuf", [128, 8], "uint16")
+SCRATCH["b16"] = ("sbuf", [128, 128], "uint16")
+for _n in ("vi", "so"):
+    SCRATCH[_n] = ("sbuf", [128, 8], "int32")
+SCRATCH["vm"] = ("sbuf", [128, 16], "int32")
+for _n in ("nwi0", "nwi1", "dmin", "hm", "sk"):
+    SCRATCH[_n] = ("sbuf", [128, 8], "float32")
+for _n in ("zr0", "zr1"):
+    SCRATCH[_n] = ("sbuf", [128, 1024], "bfloat16")
+for _n in ("MK", "zr4", "BT0", "BT1", "WE", "A12", "F", "FD", "C", "CD", "L"):
+    SCRATCH[_n] = ("sbuf", [128, 256], "bfloat16")
+for _n in ("Ps", "Ns"):
+    SCRATCH[_n] = ("sbuf", [128, 384], "bfloat16")
+SCRATCH["B"] = ("sbuf", [128, 128], "bfloat16")
+for _n in ("ab", "h12", "hb12"):
+    SCRATCH[_n] = ("sbuf", [128, 256], "float32")
+SCRATCH["RS"] = ("sbuf", [128, 256], "bfloat16")
+SCRATCH["SM"] = ("sbuf", [128, 128], "bfloat16")
+SCRATCH["XT"] = ("sbuf", [128, 128], "bfloat16")
+
+SEMAPHORES = ["sv", "sa", "st", "sg", "ls"] + ["dm%d" % i for i in range(8)] + ["rz%d" % t for t in range(1, 5)]
+CNT = {"v": "sv", "a": "sa", "t": "st", "g": "sg"}
+
+
+def build(g, T, topo, core):
+    ops = []
+
+    def op(q, dur, reads, writes, *fns, banks=(), sem=None):
+        ops.append({"q": q, "dur": dur, "r": tuple(reads), "w": tuple(writes), "f": fns, "b": tuple(banks), "sem": sem})
+
+    V, S, PE = g.vector, g.scalar, g.tensor
+
+    def dv(n, x=1.0):
+        return 35 + max(64.0, n * x) * 0.83 * 1.2
+
+    def ac(n):
+        return 60 + max(64.0, n) * 0.83 * 1.2
+
+    def pe(n):
+        return 60 + n * 0.6
+
+    def copy(out, in_, n, r, w, banks=(), x=1.0):
+        op("v", dv(n, x), r, w, lambda: V.tensor_copy(out, in_), banks=banks)
+
+    def tt(out, in0, in1, o, n, r, w, banks=(), x=2.0):
+        op("v", dv(n, x), r, w, lambda: V.tensor_tensor(out, in0, in1, o), banks=banks)
+
+    def ts(out, in0, s1, o1, n, r, w, s2=None, o2=None, banks=(), x=1.0):
+        if o2 is None:
+            op("v", dv(n, x), r, w, lambda: V.tensor_scalar(out, in0, s1, None, o1), banks=banks)
+        else:
+            op("v", dv(n, x), r, w, lambda: V.tensor_scalar(out, in0, s1, s2, o1, o2), banks=banks)
+
+    def scan(out, d0, d1, o0, o1, n, r, w, banks=()):
+        op("v", dv(n), r, w, lambda: V.tensor_tensor_scan(out, d0, d1, 0.0, o0, o1), banks=banks)
+
+    def act(out, in_, f, n, r, w, bias=0.0, scale=1.0, banks=(), x=1.0):
+        op("a", ac(n * x), r, w, lambda: S.activation(out, in_, f, bias, scale), banks=banks)
+
+    def mm(n, r, bank, *calls, grp=(), hard=False):
+        def one(a):
+            return lambda: PE.matmul(*a)
+        op("t", pe(n), r, grp, *[one(a) for a in calls], banks=(bank,))
+        ops[-1]["hard"] = hard
+
+    def pcopy(out, in_, r, w, n=128):
+        op("g", 230 + 2 * n, r, w, lambda: g.affine_select(out, in_, [[1, n]], OP.is_ge, 0.0, 0, 0))
+
+    def memset(ap, val, n, w):
+        op("v", dv(n, 0.5), (), w, lambda: V.memset(ap, val))
+
+    nd = [0]
+
+    def load(out, in_, w, dur, r=()):
+        s = "dm%d" % nd[0]
+        nd[0] += 1
+        op("s", dur, r, w, lambda: g.sync.dma_start(out, in_), sem=(s, 16))
+
+    load(T.WI[:], T.wt[:], ("WI",), 2000)
+    load(T.ZB[:], T.bites[:], ("ZB",), 2200)
+    load(T.BKI[:], T.bank[:], ("BKI",), 4000)
+    load(T.IM[:, 0:1024], T.immun[:], ("IM",), 5000)
+    load(T.G[:], T.geno[:], ("G",), 8500)
+
+    rank = T.rank_of(core)
+    cores = list(T.cores)
+    nr = len(cores)
+
+    def engs(src, dst):
+        return topo.engines(src, dst)[:8]
+
+    def send(src_ap, key, dst, t):
+        e = engs(core, dst)
+        m = 0
+        for x in e:
+            m |= 1 << x
+        a = topo.addr(dst)
+        zt = T["Z%d" % t]
+        op("g", 300, (key,), ("sent%d" % t,), lambda: g.remote_dma(zt[:], src_ap, T.sem["rz%d" % t], T.sem.ls, a[1], a[0], m),
+           sem=("ls", len(e)))
+        frm = cores[(rank - (1 if t == 1 else 2)) % nr]
+        op("n", 3500, ("sent%d" % t,), ("Z%d" % t,), sem=("rz%d" % t, len(engs(frm, core))))
+
+    op("g", 180, (), ("pI",), lambda: g.iota(T.pc[:, 0:1], [[1, 1]], 0, 1))
+    op("g", 380, (), ("cg",), lambda: g.iota(T.cg[:, 0:128], [[1, 8], [0, 16]], 0, 0))
+    op("g", 380, (), ("cm",), lambda: g.iota(T.cm[:], [[0, 8], [1, 16]], 0, 0))
+    op("g", 380, (), ("cI",), lambda: g.iota(T.cI[:], [[1, 128]], 0, 0))
+    memset(T.ONES[:], 1.0, 128, ("ONES",))
+    memset(T.HALF[:], 0.5, 128, ("HALF",))
+    memset(T.rows[:, 0:128], -2080.0, 128, ("rowA",))
+    memset(T.rows[:, 128:256], 2336.0, 128, ("rowB",))
+    memset(T.c[:], 0.0, 128, ("c",))
+    memset(T.h12[:], 0.0, 512, ("h12",))
+    memset(T.h3[:], 0.0, 256, ("h3",))
+    pc, pf = T.pc, T.pf
+    pi = pc[:, 0:1]
+    copy(pf[:, 0:1], pi, 1, ("pI",), ("f0",))
+    ts(pc[:, 1:2], pi, 4, OP.logical_shift_right, 1, ("pI",), ("i1",))
+    ts(pc[:, 2:3], pi, 15, OP.bitwise_and, 1, ("pI",), ("i2",))
+    copy(pf[:, 1:2], pc[:, 1:2], 1, ("i1",), ("f1",))
+    copy(pf[:, 2:3], pc[:, 2:3], 1, ("i2",), ("f2",))
+    cI = T.cI[:]
+    op("g", 1050, (), ("cg5",), lambda: g.iota(T.cg[:, 128:640], [[1, 32], [0, 16]], 0, 0))
+    cg, cm = T.cg[:, 0:128], T.cm[:]
+    ts(T.BO[:], cg, pf[:, 1:2], OP.is_equal, 128, ("cg", "f1"), ("BO",))
+    ts(pc[:, 8:9], T.WI[:], 4032, OP.bitwise_and, 1, ("WI",), ("i8",))
+    ts(pc[:, 9:10], T.WI[:], 63, OP.bitwise_and, 1, ("WI",), ("i9",))
+    copy(pf[:, 8:9], pc[:, 8:9], 1, ("i8",), ("f8",))
+    copy(pf[:, 9:10], pc[:, 9:10], 1, ("i9",), ("f9",))
+    ts(T.WH[:], T.BO[:], pf[:, 8:9], OP.mult, 128, ("BO", "f8"), ("WH",))
+    ts(T.WL[:], T.BO[:], pf[:, 9:10], OP.mult, 128, ("BO", "f9"), ("WL",))
+    ts(pc[:, 10:11], T.WI[:], 37, OP.mult, 1, ("WI",), ("i10",))
+    ts(pc[:, 11:12], pc[:, 10:11], 992, OP.bitwise_and, 1, ("i10",), ("i11",))
+    ts(pc[:, 12:13], pc[:, 10:11], 31, OP.bitwise_and, 1, ("i10",), ("i12",))
+    copy(pf[:, 11:12], pc[:, 11:12], 1, ("i11",), ("f11",))
+    copy(pf[:, 12:13], pc[:, 12:13], 1, ("i12",), ("f12",))
+    act(T.VH[:], T.BO[:], AF.Copy, 128, ("BO", "f11"), ("VH",), scale=pf[:, 11:12])
+    act(T.VL[:], T.BO[:], AF.Copy, 128, ("BO", "f12"), ("VL",), scale=pf[:, 12:13])
+    ts(T.MK[:, 0:128], cm, pf[:, 2:3], OP.is_equal, 128, ("cm", "f2"), ("MKa",))
+    act(T.MK[:, 128:256], T.MK[:, 0:128], AF.Copy, 128, ("MKa",), ("MK",))
+    ts(T.RS[:, 0:128], cm, 0.0, OP.is_gt, 128, ("cm",), ("RSa",))
+    act(T.RS[:, 128:256], T.RS[:, 0:128], AF.Copy, 128, ("RSa",), ("RS",))
+    ts(T.I[:], cI, pf[:, 0:1], OP.is_equal, 128, ("cI", "f0"), ("I",))
+    ts(T.R8[:], T.cI[:, 0:8], pf[:, 1:2], OP.is_equal, 8, ("cI", "f1"), ("R8",))
+    ts(T.tf[:], T.RS[:, 0:128], 0.5, OP.mult, 128, ("RSa",), ("tf",))
+    ts(T.tf2[:], T.RS[:, 0:128], -512.0, OP.mult, 128, ("RSa",), ("tf2",), s2=512.0, o2=OP.add)
+    scan(T.mb[:], T.tf[:], T.tf2[:], OP.mult, OP.add, 128, ("tf", "tf2"), ("mb",))
+    tt(T.tf[:], T.mb[:], T.I[:], OP.mult, 128, ("mb", "I"), ("tf",))
+    op("v", dv(128), ("tf",), ("f5",), lambda: V.tensor_reduce(pf[:, 5:6], T.tf[:], AxisListType.X, OP.add))
+    ts(pf[:, 6:7], pf[:, 2:3], 8.0, OP.is_ge, 1, ("f2",), ("f6",))
+    ts(pf[:, 7:8], pf[:, 6:7], 63.75, OP.mult, 1, ("f6",), ("f7",), s2=0.25, o2=OP.add)
+    tt(pf[:, 10:11], pf[:, 7:8], pf[:, 5:6], OP.mult, 1, ("f7", "f5"), ("f10",))
+    ts(pc[:, 13:14], pc[:, 1:2], 1, OP.bitwise_and, 1, ("i1",), ("i13",))
+    ts(pf[:, 13:14], pf[:, 2:3], 10.0, OP.is_lt, 1, ("f2",), ("f13",))
+    tt(pf[:, 14:15], pf[:, 13:14], pc[:, 13:14], OP.mult, 1, ("f13", "i13"), ("f14",))
+    tt(pf[:, 15:16], pf[:, 13:14], pf[:, 14:15], OP.subtract, 1, ("f13", "f14"), ("f15",))
+    ts(pf[:, 16:18], pf[:, 14:16], 1.0 / 256, OP.mult, 2, ("f14", "f15"), ("f16",))
+    ts(pf[:, 18:20], pf[:, 14:16], -1.0, OP.mult, 2, ("f14", "f15"), ("f18",))
+    ts(T.tf[:, 0:8], T.cI[:, 0:8], 16.0, OP.mult, 8, ("cI", "tf"), ("tf",), s2=1024.0, o2=OP.add)
+    ts(pf[:, 48:56], T.tf[:, 0:8], pf[:, 2:3], OP.add, 8, ("tf", "f2"), ("iw",))
+    ts(pc[:, 3:4], pi, 31, OP.bitwise_and, 1, ("pI",), ("i3",))
+    copy(pf[:, 3:4], pc[:, 3:4], 1, ("i3",), ("f3",))
+    ts(pf[:, 4:5], pf[:, 0:1], 32.0, OP.mult, 1, ("f0",), ("f4",))
+    ts(T.SEL[:], T.cg[:, 128:640], pf[:, 3:4], OP.is_equal, 512, ("cg5", "f3"), ("SEL",), s2=-1.0, o2=OP.mult)
+    act(T.G16[:], T.R8[:], AF.Copy, 8, ("R8",), ("G16",), scale=16.0)
+    act(T.KC[:], T.BO[:], AF.Copy, 128, ("BO",), ("KC",), scale=128.0)
+    ts(T.rows[:, 512:640], cm, -1.0, OP.mult, 128, ("cm",), ("rowR",), s2=15.0, o2=OP.add)
+    ts(T.rows[:, 672:688], T.cI[:, 0:16], 8.0, OP.is_ge, 16, ("cI",), ("rowZ",), s2=-8.0, o2=OP.mult)
+    tt(T.rows[:, 656:672], T.cI[:, 0:16], T.rows[:, 672:688], OP.add, 16, ("cI", "rowZ"), ("rowY",))
+    ts(T.rows[:, 640:656], T.rows[:, 656:672], 256.0, OP.mult, 16, ("rowY",), ("rowX",))
+
+    def cst(name, t):
+        return T[name][:, 128 * t:128 * t + 128]
+
+    def scaled(name, val, t=None):
+        out = T[name][:] if t is None else cst(name, t)
+        act(out, T.I[:], AF.Copy, 128, ("I",), (name if t is None else name + str(t),), scale=val)
+
+    for name, val in (("KF", THR), ("I16", 16.0), ("nI16", -16.0), ("nI", -1.0), ("nI256", -256.0)):
+        scaled(name, val)
+    act(T.D32[:], T.I[:], AF.Copy, 128, ("I", "f4"), ("D32",), scale=pf[:, 4:5])
+    for t in range(NST):
+        scaled("HI", 4096.0 * (8 + t), t)
+        if t:
+            scaled("TI", float(t), t)
+    for j in range(2):
+        memset(T["X%d" % j][:, 0:4 * XS:XS], -64.0, 4, ["Xs%d" % j])
+        memset(T["X%d" % j][:, 4 * XS::XS], -1.0, 4, ["Xt%d" % j])
+    tw = T.tw
+    ts(tw[:, 64:72], T.cI[:, 0:8], 0.0, OP.is_equal, 8, ("cI",), ("d1",))
+    for nm_, base_, o in (("n", 1.0 / 64, 0), ("p", 64.0, 24)):
+        memset(tw[:, 72 + o:80 + o], base_, 8, ("d0" + nm_,))
+        scan(tw[:, 80 + o:88 + o], tw[:, 72 + o:80 + o], tw[:, 64:72], OP.mult, OP.add, 8, ("d0" + nm_, "d1"), ("pw" + nm_,))
+        tt(tw[:, 88 + o:96 + o], tw[:, 80 + o:88 + o], T.R8[:], OP.mult, 8, ("pw" + nm_, "R8"), ("px" + nm_,))
+    op("v", dv(8), ("pxn",), ("f57",), lambda: V.tensor_reduce(pf[:, 57:58], tw[:, 88:96], AxisListType.X, OP.add))
+    op("v", dv(8), ("pxp",), ("f58",), lambda: V.tensor_reduce(pf[:, 58:59], tw[:, 112:120], AxisListType.X, OP.add))
+    ts(tw[:, 8:24], T.cm[:, 0:16], pf[:, 2:3], OP.is_gt, 16, ("cm", "f2"), ("wt0",), s2=1.9375, o2=OP.mult)
+    ts(T.rows[:, 900:916], tw[:, 8:24], 0.0625, OP.add, 16, ("wt0", "f57"), ("WT",), s2=pf[:, 57:58], o2=OP.mult)
+    act(T.MK2[:], T.MK[:, 0:128], AF.Copy, 128, ("MKa", "f58"), ("MK2",), scale=pf[:, 58:59])
+    ts(pf[:, 20:21], pf[:, 2:3], 1.0, OP.add, 1, ("f2",), ("f20",))
+    ts(T.tf2[:], cm, 16.0, OP.mult, 128, ("cm", "f20"), ("tf2",), s2=pf[:, 20:21], o2=OP.add)
+    tt(T.Kc[:], T.tf2[:], T.BO[:], OP.mult, 128, ("tf2", "BO"), ("Kc",))
+    act(T.Kn[:], T.Kc[:], AF.Copy, 128, ("Kc",), ("Kn",), scale=-1.0)
+    ts(pc[:, 4:5], pi, 3, OP.logical_shift_right, 1, ("pI",), ("i4",))
+    ts(pc[:, 5:6], pi, 7, OP.bitwise_and, 1, ("pI",), ("i5",))
+    copy(pf[:, 21:22], pc[:, 5:6], 1, ("i5",), ("f21",))
+    for j in range(6):
+        ts(pf[:, 22 + j:23 + j], pc[:, 4:5], float(j), OP.is_equal, 1, ("i4",), ("f%d" % (22 + j),))
+    tt(pf[:, 32:35], pf[:, 22:25], pf[:, 25:28], OP.add, 3, ["f%d" % j for j in range(22, 28)], ("f32",))
+    tt(pf[:, 35:37], pf[:, 32:34], pf[:, 33:35], OP.subtract, 2, ("f32",), ("f35",))
+    tt(pf[:, 37:38], pf[:, 32:33], pf[:, 34:35], OP.subtract, 1, ("f32",), ("f37",))
+    for j in range(3):
+        ts(T.SM[:, 8 * j:8 * j + 8], T.cI[:, 0:8], pf[:, 21:22], OP.is_equal, 8, ("cI", "f21", "f35", "f37"), ("M1%d" % j,),
+           s2=pf[:, 35 + j:36 + j], o2=OP.mult)
+    memset(T.SM[:, 24:32], 0.0, 8, ("M13",))
+    memset(T.SM[:, 32:120], 0.0, 88, ("RB",))
+    copy(T.SM[:, 72:80], T.R8[:], 8, ("R8",), ("RB",), x=0.5)
+    ts(pf[:, 38:44], pf[:, 22:28], 0.5, OP.mult, 6, ["f%d" % j for j in range(22, 28)], ("f38",))
+    tt(pf[:, 46:47], pf[:, 25:26], pf[:, 26:27], OP.add, 1, ("f25", "f26"), ("f46",))
+    ts(pf[:, 29:30], pf[:, 46:47], -2.0, OP.mult, 1, ("f46",), ("f29",))
+    tt(pf[:, 44:45], pf[:, 39:40], pf[:, 38:39], OP.subtract, 1, ("f38",), ("f44",))
+    tt(pf[:, 28:29], pf[:, 44:45], pf[:, 29:30], OP.add, 1, ("f44", "f29"), ("f28",))
+    tt(pf[:, 45:46], pf[:, 39:40], pf[:, 40:41], OP.add, 1, ("f38",), ("f45",))
+    tt(pf[:, 30:31], pf[:, 29:30], pf[:, 45:46], OP.subtract, 1, ("f29", "f45"), ("f30",))
+    ts(T.CO1[:], cg, pf[:, 21:22], OP.is_equal, 128, ("cg", "f21", "f28"), ("CO1",), s2=pf[:, 28:29], o2=OP.mult)
+    ts(T.CO2[:], cg, pf[:, 21:22], OP.is_equal, 128, ("cg", "f21", "f30"), ("CO2",), s2=pf[:, 30:31], o2=OP.mult)
+
+    P0, P1, P2, P3, P4, P5, P6, P7 = [T["P%d" % i] for i in range(8)]
+    one1 = T.ONES[0:1, :]
+
+    def zap(t):
+        return T.ZB[:, 0:128] if t == 0 else T["Z%d" % t][:]
+
+    def zk(t):
+        return "ZB" if t == 0 else "Z%d" % t
+
+    def prep(t):
+        z, k, d = zap(t), zk(t), t % 2
+        for j in range(4):
+            pcopy(T.zr4[:, j::4], z[:, 0:64], (k,), ("zr4%d" % j,), 64)
+        for j in range(4):
+            pcopy(T["zr%d" % d][:, j::4], T.zr4[:], ["zr4%d" % i for i in range(4)], ("zr%d" % d,) if j == 3 else ("zq%d%d" % (d, j),), 256)
+        mm(256, (k, "WH", "WL"), "P6", (P6[:, 0:128], T.WH[:], z, True, False), (P6[:, 0:128], T.WL[:], z, False, True))
+        mm(256, (k, "VH", "VL"), "P6", (P6[:, 128:256], T.VH[:], z, True, False), (P6[:, 128:256], T.VL[:], z, False, True))
+        copy(T.Ui[:], P6[:, 0:128], 128, (), ("Ui",), banks=("P6",))
+        ts(T.u[:], T.Ui[:], 4095, OP.bitwise_and, 128, ("Ui",), ("u",))
+        tt(T.sq[:], T.u[:], T.u[:], OP.mult, 128, ("u",), ("sq",))
+        ts(T.s5[:], T.sq[:], 5, OP.logical_shift_right, 128, ("sq",), ("s5",))
+        tt(P6[:, 256:384], T.s5[:], P6[:, 128:256], OP.add, 128, ("s5",), ("base",), banks=("P6",), x=1.0)
+        sw = T["sw%d" % d]
+        tt(T.mb[:], P6[:, 256:384], T.MK[:, 0:128], OP.mult, 128, ("base", "MKa"), ("mb",), banks=("P6",), x=1.0)
+        scan(sw[:], T.RS[:, 0:128], T.mb[:], OP.mult, OP.add, 128, ("RSa", "mb"), ("sw%d" % d,))
+        mm(128, (k, "I"), "P6", (P6[:, 384:512], z, T.I[:], True, True))
+        act(T["zT%d" % d][:], P6[:, 384:512], AF.Copy, 128, (), ("zT%d" % d,), banks=("P6",))
+
+    def dups(t):
+        z, k, d = zap(t), zk(t), t % 2
+        ts(T.bb[:], P6[:, 256:384], pf[:, 5:6], OP.mult, 128, ("base", "f5"), ("bb",), banks=("P6",))
+        if t <= NST - 3:
+            ts(T.ub[:], P6[:, 0:128], pf[:, 10:11], OP.mult, 128, ("f10",), ("ub",), banks=("P6",))
+            ts(T.ubm[:], T.ub[:], 128, OP.bitwise_and, 128, ("ub",), ("ubm",))
+            bt = T["BT%d" % d]
+            ts(bt[:, 0:128], T.ubm[:], -1.0 / 128, OP.mult, 128, ("ubm",), ("bta%d" % d,))
+            pcopy(bt[:, 128:256], bt[:, 0:128], ("bta%d" % d,), ("BT%d" % d,))
+        ts(T.bbm[:], T.bb[:], 512, OP.bitwise_and, 128, ("bb",), ("bbm",))
+        ts(T.BD[:], T.bbm[:], pf[:, 16:17], OP.mult, 128, ("bbm", "f16", "f18"), ("BD",), s2=pf[:, 18:19], o2=OP.add)
+        ts(T.BE[:], T.bbm[:], pf[:, 17:18], OP.mult, 128, ("bbm", "f16", "f18"), ("BE",), s2=pf[:, 19:20], o2=OP.add)
+        for h in range(2):
+            for j in range(2):
+                calls = []
+                for i in range(2):
+                    bx = (T.BD if i else T.BE)[64 * h + 32 * j:64 * h + 32 * j + 32, :]
+                    calls.append((P0[:, 256 * j + 128 * i:256 * j + 128 * i + 128], bx, bx, True, True))
+                mm(256, ("BD", "BE"), "P0", *calls, grp=("gdup",), hard=bool(j))
+            act(T.EQ[:, 512 * h:512 * h + 512], P0[:], AF.Relu, 512, (), ("EQ%d" % h,), bias=-9.0, banks=("P0",))
+        mm(512, ("EQ0", "EQ1", "WT"), "P0",
+           *[(P0[:, 16 * j:16 * j + 16], T.EQ[:, 128 * j:128 * j + 128], T.rows[:, 900:916], True, True) for j in range(8)])
+        tt(T.DM[:], P0[:, 0:128], T.MK2[:], OP.mult, 128, ("MK2",), ("DM",), banks=("P0",), x=1.0)
+        mm(64, ("DM", "R8"), "P0", (P0[:, 128:136], T.DM[:], T.R8[:], True, True))
+        act(T.dmin[:], P0[:, 128:136], AF.Sign, 8, (), ("dmin",), bias=-1.75, banks=("P0",))
+        tt(T["nwi%d" % d][:], T.dmin[:], pf[:, 48:56], OP.mult, 8, ("dmin", "iw"), ("nwi%d" % d,))
+
+    def voff(t):
+        d = t % 2
+        if t == 0:
+            copy(T.vi[:], T.sw0[:, 15::16], 8, ("sw0",), ("vi",))
+        else:
+            ts(T.vi[:], T["sw%d" % d][:, 15::16], pf[:, 63:64], OP.add, 8, ("sw%d" % d, "A"), ("vi",))
+        ts(T.vm[:, 8 * d:8 * d + 8], T.vi[:], 1023, OP.bitwise_and, 8, ("vi",), ("vm%d" % d,))
+        copy(T["goff%d" % d][:], T.vm[:, 8 * d:8 * d + 8], 8, ("vm%d" % d,), ("goff%d" % d,))
+
+    def soff(t):
+        d = t % 2
+        tt(T.so[:], T.vm[:, 8 * d:8 * d + 8], T["nwi%d" % d][:], OP.max, 8, ("vm%d" % d, "nwi%d" % d), ("so",))
+        copy(T["soff%d" % d][:], T.so[:], 8, ("so",), ("soff%d" % d,))
+
+    def main(t):
+        d = t % 2
+        z, k = zap(t), zk(t)
+        last = t == NST - 1
+        go, gk = T["goff%d" % d][:, 0:8], "goff%d" % d
+        X, xk = T["X%d" % d], "X%d" % d
+        win = T.BK[:, 0:1024]
+        qb = {"bias": 129.5 + 2.0 ** -14, "scale": 1.0 / 4096}
+        if t == 0:
+            copy(T.bi[:], T.BKI[:].indirect(go), 128, ("BKI", gk), ("bi",), x=1.6)
+            copy(T.nb[:], T.bi[:], 128, ("bi",), ("nb",))
+            act(T.qt[:], T.nb[:], AF.Identity, 128, ("nb",), ("qt",), **qb)
+            copy(T.BK[:, 0:1024], T.BKI[:], 1024, ("BKI",), ("BK",))
+        else:
+            copy(T.bi[:], win.indirect(go), 128, ("BK", gk), ("bi",), x=1.6)
+            act(T.qt[:], win.indirect(go), AF.Identity, 128, ("BK", gk), ("qt",), x=1.6, **qb)
+        ts(T.bm[:], T.bi[:], 4095, OP.bitwise_and, 128, ("bi",), ("bm",))
+        copy(T.b16[:], T.bm[:], 128, ("bm",), ("b16",))
+        act(T.Fs[:], T.qt[:], AF.Sign, 128, ("qt",), ("Fs",), bias=-(131.5 + t))
+        for c in range(8):
+            off = T.b16[:, 16 * c:16 * c + 16]
+            out = X[:, XS * c + 1:XS * c + 257]
+            if c < 4:
+                tt(out, T.G[:].indirect(off), T["zr%d" % d][:, 256 * c:256 * c + 256], OP.subtract, 256,
+                   ("G", "b16", "zr%d" % d) + tuple("zq%d%d" % (d, j) for j in range(3)), (xk + str(c),), x=1.6)
+            else:
+                act(out, T.G[:].indirect(off), AF.Copy, 256, ("G", "b16"), (xk + str(c),), x=1.6)
+        mm(256, ("qt", "I16", "ONES", "rowA"), "P7", (P7[:, 128:256], one1, T.rows[0:1, 0:128], True, False),
+           (P7[:, 128:256], T.qt[:], T.I16[:], False, True))
+        mm(384, ("qt", "nI16", "ONES", "rowB", "rowR"), "P7", (P7[:, 256:384], one1, T.rows[0:1, 128:256], True, False),
+           (P7[:, 256:384], one1, T.rows[0:1, 512:640], False, False), (P7[:, 256:384], T.qt[:], T.nI16[:], False, True))
+        if True:
+            mm(64, ("Fs", "R8"), "P7", (P7[:, 384:392], T.Fs[:], T.R8[:], True, True))
+        act(T.ivm[:], T.IM[:, 0:1024].indirect(go), AF.Identity, 128, ("IM", gk), ("ivm",), bias=-1.0, x=1.6)
+        mm(256, (k, "ivm", "I", "nI"), "P7", (P7[:, 0:128], T.I[:], z, True, False), (P7[:, 0:128], T.nI[:], T.ivm[:], False, True))
+        act(T.Sg[:], P7[:, 0:128], AF.Sign, 128, (), ("Sg",), bias=-1.5, banks=("P7",))
+        mm(256, ("Fs", "KF", "rowR", "ONES"), "P5", (P5[:, 0:128], one1, T.rows[0:1, 512:640], True, False),
+           (P5[:, 0:128], T.Fs[:], T.KF[:], False, False), grp=("gkey",))
+        def dist(e):
+            lo, hi = DIST[e]
+            if hi > lo:
+                mm(16 * max(hi - lo, 8), ["AB%d%d" % (i, j) for i in range(lo // 32, hi // 32) for j in range(2)] + ["G16"], "P5",
+                   *[(P5[lo:hi, kk:128:16], T.AB[:, 16 * lo + kk:16 * hi:16], T.G16[:], False, kk == 15) for kk in range(16)],
+                   grp=("gkey",))
+        for e in range(4):
+            if e < 2:
+                for c in (2 * e, 2 * e + 1):
+                    act(T.AB[:, 256 * c:256 * c + 256], X[:, XS * c + 1:XS * c + 257], AF.Abs, 256, (xk + str(c),), ("AB%d%d" % (e, c % 2),))
+                dist(e)
+                continue
+            bank = "P%d" % (1 + e % 2)
+            pb = T[bank]
+            zt = T["zT%d" % d][32 * e:32 * e + 32, :]
+            mm(512, ("zT%d" % d, "SEL"), bank, (pb[:], zt, T.SEL[32 * e:32 * e + 32, :], True, False), grp=("g" + bank,))
+            for j in range(2):
+                c = 2 * e + j
+                mm(256, (xk + str(c), "I"), bank, (pb[:, 256 * j:256 * j + 256], T.I[:], X[:, XS * c + 1:XS * c + 257], False, j == 1), grp=("g" + bank,))
+            act(T.AB[:, 512 * e:512 * e + 512], pb[:], AF.Abs, 512, (), ("AB%d0" % e, "AB%d1" % e), banks=(bank,))
+            dist(e)
+        dups(t)
+        soff(t)
+        pcopy(T.G[:, t::32], z, (k,), ("G",))
+        mm(192, ("Sg", "KC", "R8"), "P7", (P7[:, 0:128], T.Sg[:], T.KC[:], True, True), (P7[:, 392:400], T.Sg[:], T.R8[:], True, True))
+        act(T.cap[:], P7[:, 0:128], AF.Relu, 128, (), ("cap",), banks=("P7",))
+        ts(T.sk[:], P7[:, 392:400], 1.0, OP.is_ge, 8, (), ("sk",), banks=("P7",))
+        tt(P7[:, 128:256], P7[:, 128:256], T.cap[:], OP.min, 128, ("cap",), ("q16s",), banks=("P7",), x=1.0)
+        ts(T.hm[:], P7[:, 384:392], -12.0, OP.min, 8, (), ("hm",), s2=16.0, o2=OP.add, banks=("P7",))
+        tt(T.hv[:], T.hm[:], T.sk[:], OP.mult, 8, ("hm", "sk"), ("hv",))
+        if last:
+            load(T.ygeno[:], T.G[:], ("yg",), 7000, r=("G",))
+        else:
+            mm(64, ("hv", "HALF"), "P7", (P7[:, 400:408], T.HALF[:], T.hv[:], True, True))
+            op("v", dv(8), (), ("A",), lambda: V.tensor_reduce(pf[:, 63:64], P7[:, 400:408], AxisListType.X, OP.add), banks=("P7",))
+            prep(t + 1)
+            voff(t + 1)
+        key = P5[:, 0:128]
+        RS = T.RS[:, 0:128]
+        scan(T.ab[:, 0:128], RS, key, OP.mult, OP.max, 128, ("RSa",), ("a",), banks=("P5",))
+        tt(T.c[:, 1:128], T.ab[:, 0:127], P5[:, 1:128], OP.min, 128, ("a",), ("c",), banks=("P5",), x=1.0)
+        scan(T.ab[:, 128:256], T.c[:], RS, OP.max, OP.mult, 128, ("c", "RSa"), ("b",))
+        ts(T.h12[:, 0::16], T.ab[:, 15::16], THR, OP.max, 16, ("a", "b"), ("h12",))
+        scan(T.hb12[:], T.RS[:], T.h12[:], OP.mult, OP.add, 256, ("h12", "RS"), ("hb12",))
+        tt(T.W[:], key, T.hb12[:, 128:256], OP.is_ge, 128, ("hb12",), ("W",), banks=("P5",), x=1.0)
+        tt(T.E1[:], key, T.hb12[:, 0:128], OP.is_ge, 128, ("hb12",), ("E1",), banks=("P5",), x=1.0)
+        tt(T.wq[:], P7[:, 128:256], T.W[:], OP.mult, 128, ("W", "q16s"), ("wq",), banks=("P7",), x=1.0)
+        tt(T.e2[:], P7[:, 256:384], T.wq[:], OP.add, 128, ("wq",), ("e2",), banks=("P7",), x=1.0)
+        scan(T.s3[:], RS, T.e2[:], OP.mult, OP.max, 128, ("e2", "RSa"), ("s3",))
+        copy(T.h3[:, 0::16], T.s3[:, 15::16], 8, ("s3",), ("h3",))
+        scan(P5[:, 384:512], RS, T.h3[:], OP.mult, OP.add, 128, ("h3", "RSa"), ("hb3",), banks=("P5",))
+        tt(T.S[:], T.e2[:], P5[:, 384:512], OP.is_equal, 128, ("e2", "hb3"), ("S",), banks=("P5",), x=1.0)
+        mm(128, ("wq", "nI256"), "P7", (P7[:, 0:128], T.wq[:], T.nI256[:], True, True))
+        calls = [(P5[:, 256:384], T.S[:], T.D32[:], True, False)]
+        if t:
+            calls.append((P5[:, 256:384], T.S[:], cst("TI", t), False, False))
+        calls.append((P5[:, 256:384], T.S[:], cst("HI", t), False, True))
+        tt(T.t1[:], T.bi[:], P7[:, 0:128], OP.add, 128, ("bi",), ("t1",), banks=("P7",), x=1.0)
+        mm(384, ("S", "D32", "HI%d" % t) + (("TI%d" % t,) if t else ()), "P5", *calls)
+        tt(T.nb[:], T.t1[:], P5[:, 256:384], OP.max, 128, ("t1",), ("nb",), banks=("P5",), x=1.0)
+        so, sk_ = T["soff%d" % d][:, 0:8], "soff%d" % d
+        copy(T.BK[:, 0:1152].indirect(so), T.nb[:], 128, ("nb", sk_), ("BK",), x=3.5)
+        if last:
+            load(T.ybank[:], T.BK[:, 0:1024], ("yb",), 4000, r=("BK",))
+        mm(256, ("W", "E1", "I"), "P3", (P3[:, 0:128], T.E1[:], T.I[:], True, True), (P3[:, 128:256], T.W[:], T.I[:], True, True))
+        act(T.WE[:], P3[:, 0:256], AF.Copy, 256, (), ("WE",), banks=("P3",))
+        mm(384, ("WE", "Kc", "Kn"), "P3", (P3[:, 256:384], T.WE[:, 0:128], T.Kc[:], True, True),
+           (P3[:, 384:512], T.WE[:, 128:256], T.Kc[:], True, False), (P3[:, 384:512], T.WE[:, 0:128], T.Kn[:], False, True))
+        tt(T.L[:], P3[:, 256:512], T.MK[:], OP.mult, 256, ("MK",), ("L",), banks=("P3",), x=1.0)
+        mm(256, ("L", "R8", "ONES", "rowX", "rowY"), "P3", (P3[:, 0:16], one1, T.rows[0:1, 640:656], True, False),
+           (P3[:, 0:16], one1, T.rows[0:1, 656:672], False, False),
+           (P3[:, 0:8], T.L[:, 0:128], T.R8[:], False, False), (P3[:, 8:16], T.L[:, 128:256], T.R8[:], False, True))
+        copy(T.oXA[:], P3[:, 0:16], 16, (), ("oXA",), banks=("P3",))
+        act(T.A12[:], X[:].indirect(T.oXA[:, 0:16]), AF.Copy, 256, ["oXA", "Xs%d" % d, "Xt%d" % d] + [xk + str(c) for c in range(8)], ("A12",), x=1.6)
+        mm(384, ("A12", k, "I", "nI"), "P4", (P4[:, 0:256], T.I[:], T.A12[:], True, False),
+           (P4[:, 64:128], T.nI[:], z[:, 64:128], False, False), (P4[:, 192:256], T.nI[:], z[:, 64:128], False, True))
+        mm(256, ("A12", "I", "nI"), "P4", (P4[:, 256:384], T.I[:], T.A12[:, 128:256], True, False),
+           (P4[:, 256:384], T.nI[:], T.A12[:, 0:128], False, True))
+        act(T.Ps[:], P4[:, 0:384], AF.Sign, 384, (), ("Ps",), bias=-0.5, banks=("P4",))
+        act(T.Ns[:], P4[:, 0:384], AF.Sign, 384, (), ("Ns",), bias=-0.5, scale=-1.0, banks=("P4",))
+
+        def cnt(j, buf, i, first=False, last_=False):
+            return (P4[0:48, 384:512], T.SM[:, 72 - 8 * j:120 - 8 * j], buf[:, 128 * i:128 * i + 128], first, last_)
+        mm(384, ("Ps", "RB"), "P4", cnt(0, T.Ps, 0, True), cnt(3, T.Ps, 1), cnt(4, T.Ps, 2), grp=("gcnt",))
+        mm(384, ("Ns", "RB"), "P4", cnt(1, T.Ns, 0), cnt(2, T.Ns, 1), cnt(5, T.Ns, 2, False, True), grp=("gcnt",))
+        act(T.B[0:48, :], P4[0:48, 384:512], AF.Sign, 128, (), ("B",), bias=-1.0, banks=("P4",))
+        mm(192, ("B", "M10", "M11", "M12", "M13", "hv", "I"), "P3", (P3[0:32, 0:128], T.SM[0:48, 0:32], T.B[0:48, :], True, True),
+           (P3[32:40, 0:128], T.hv[:], T.I[:], True, True))
+        act(T.XT[0:40, :], P3[0:40, 0:128], AF.Sign, 128, (), ("XT",), bias=-1.0, banks=("P3",))
+        mm(256, ("XT", "CO1", "CO2"), "P0", (P0[:, 0:128], T.CO1[0:40, :], T.XT[0:40, :], True, True),
+           (P0[:, 128:256], T.CO2[0:40, :], T.XT[0:40, :], True, True))
+        bt = "BT%d" % d
+        if t <= NST - 3:
+            tt(T.C[:], P0[:, 0:256], T[bt][:], OP.is_equal, 256, (bt,), ("C",), banks=("P0",), x=1.0)
+            tt(T.CD[:], T.C[:], P4[:, 0:256], OP.mult, 256, ("C",), ("CD",), banks=("P4",), x=1.0)
+        act(T.F[:], P0[:, 0:256], AF.Relu, 256, (), ("F",), scale=-1.0, banks=("P0",))
+        tt(T.FD[:], T.F[:], P4[:, 0:256], OP.mult, 256, ("F",), ("FD",), banks=("P4",), x=1.0)
+        mm(384, ("FD", k, "I"), "P0", (P0[:, 256:384], T.I[:], z, True, False), (P0[:, 256:384], T.I[:], T.FD[:, 0:128], False, False),
+           (P0[:, 256:384], T.I[:], T.FD[:, 128:256], False, True))
+        tt(T.nim[:], T.ivm[:], P0[:, 256:384], OP.max, 128, ("ivm",), ("nim",), banks=("P0",), x=1.0)
+        copy(T.IM[:, 0:1152].indirect(so), T.nim[:], 128, ("nim", sk_), ("IM",), x=3.5)
+        if last:
+            load(T.yimm[:], T.IM[:, 0:1024], ("yi",), 3500, r=("IM",))
+        if t <= NST - 3:
+            mm(384, ("CD", k, "I"), "P3", (P3[:, 256:384], T.I[:], z, True, False), (P3[:, 256:384], T.I[:], T.CD[:, 0:128], False, False),
+               (P3[:, 256:384], T.I[:], T.CD[:, 128:256], False, True))
+            cr = "CR%d" % t
+            act(cst("CR", t), P3[:, 256:384], AF.Copy, 128, (), (cr,), banks=("P3",))
+            send(cst("CR", t), cr, cores[(rank + 2) % nr], t + 2)
+
+    send(T.ZB[:, 128:256], "ZB", cores[(rank + 1) % nr], 1)
+    prep(0)
+    voff(0)
+    for t in range(NST):
+        main(t)
+    return ops
+
+
+def depend(ops):
+    lw, rd, bank, rdy, prev = {}, {}, {}, [], []
+    lastq = {}
+    for i, o in enumerate(ops):
+        need, order = set(), set()
+        for k in o["r"]:
+            if k in lw:
+                need |= lw[k]
+            rd.setdefault(k, []).append(i)
+        for k in o["w"]:
+            if k in lw:
+                need |= lw[k]
+            need |= set(rd.get(k, ()))
+        for k in o["w"]:
+            lw[k] = {i}
+            rd[k] = []
+        for k in o["b"]:
+            h = bank.setdefault(k, [None, set(), set()])
+            if h[0] != o["q"]:
+                h[0], h[1], h[2] = o["q"], h[2], set()
+            need |= h[1]
+            h[2].add(i)
+        if o["q"] == "s":
+            if o["q"] in lastq:
+                order.add(lastq[o["q"]])
+            lastq[o["q"]] = i
+        need.discard(i)
+        order.discard(i)
+        rdy.append(need)
+        prev.append(order)
+    return rdy, prev
+
+
+def schedule(q, dur, nxt, cnt, key):
+    n = len(q)
+    left = cnt[:]
+    avail, start, fin, seq = [0.0] * n, [0.0] * n, [0.0] * n, []
+    ready = {k: [] for k in "vatgsn"}
+    free = dict.fromkeys("vatgsn", 0.0)
+    for i in range(n):
+        if left[i] == 0:
+            ready[q[i]].append(i)
+    best, dirty = {}, list("vatgsn")
+    while len(seq) < n:
+        for k in dirty:
+            r = ready[k]
+            if not r:
+                best.pop(k, None)
+                continue
+            f = free[k]
+            t0 = max(f, min([avail[i] for i in r]))
+            bi, bp = -1, -1e18
+            for i in r:
+                if avail[i] <= t0 and key[i] > bp:
+                    bp, bi = key[i], i
+            best[k] = (t0, bi)
+        k = min(best, key=lambda x: best[x])
+        st, i = best[k]
+        ready[k].remove(i)
+        seq.append(i)
+        start[i], fin[i] = st, st + dur[i]
+        free[k] = st + 60 if k == "s" else (0.0 if k == "n" else fin[i])
+        dirty = [k]
+        for j, lag in nxt[i]:
+            av = fin[i] + lag
+            if av > avail[j]:
+                avail[j] = av
+            left[j] -= 1
+            if left[j] == 0:
+                ready[q[j]].append(j)
+                if q[j] not in dirty:
+                    dirty.append(q[j])
+    return max(fin), seq, start, fin
+
+
+TRIES = 1500
+
+
+def improve(ops, need, order):
+    rnd = np.random.RandomState(3)
+    n = len(ops)
+    q, dur = [o["q"] for o in ops], [o["dur"] for o in ops]
+    nxt, prv = [[] for _ in range(n)], [[] for _ in range(n)]
+    for i in range(n):
+        for j in sorted(need[i] | order[i]):
+            lag = (40 if q[i] == q[j] else 80) if j in need[i] else 60 - dur[j]
+            nxt[j].append((i, lag))
+            prv[i].append((j, lag))
+    cur = [0.0] * n
+    for i in range(n - 1, -1, -1):
+        cur[i] = dur[i] + max([cur[j] + 40 for j, _ in nxt[i]], default=0.0)
+    best = None
+    for _ in range(TRIES):
+        r = schedule(q, dur, nxt, [len(x) for x in prv], cur)
+        for _ in range(4):
+            key = schedule(q, dur, prv, [len(x) for x in nxt], r[3])[3]
+            r2 = schedule(q, dur, nxt, [len(x) for x in prv], key)
+            if best is None or min(r, r2)[0] < best[0]:
+                best = r2 if r2[0] < r[0] else r
+            if r2[0] >= r[0] - 1:
+                break
+            r = r2
+        key = schedule(q, dur, prv, [len(x) for x in nxt], best[3])[3]
+        sg = (100.0, 400.0, 1500.0)[int(rnd.randint(3))]
+        cur = [key[i] + sg * float(x) for i, x in enumerate(rnd.normal(size=n))]
+    return best
+
+
+PLAN = {}
+
+
+def rank_program(g, core, T, topo):
+    rank = T.rank_of(core)
+    if rank is None:
+        return
+    ops = build(g, T, topo, core)
+    if "seq" not in PLAN:
+        need, order = depend(ops)
+        PLAN["need"] = need
+        PLAN["end"], PLAN["seq"], PLAN["start"], PLAN["fin"] = improve(ops, need, order)
+    need, seq = PLAN["need"], PLAN["seq"]
+    queue = {"v": g.vector, "a": g.scalar, "t": g.tensor, "g": g, "s": g.sync}
+    count, done, known, clock = {}, {}, {}, {}
+    for i in seq:
+        o = ops[i]
+        q = o["q"]
+        kn = known.setdefault(q, {}) if q != "n" else {}
+        for j in sorted(need[i], key=lambda x: -x):
+            s, v = done[j]
+            if q == "t" and ops[j]["q"] == "t" and not o["hard"]:
+                continue
+            if kn.get(s, 0) >= v:
+                continue
+            if q != "n":
+                queue[q].wait_ge(T.sem[s], v)
+            for s2, v2 in clock[j].items():
+                kn[s2] = max(kn.get(s2, 0), v2)
+            kn[s] = max(kn.get(s, 0), v)
+        ins = None
+        for f in o["f"]:
+            ins = f()
+        if o["sem"] is None:
+            s = CNT[q]
+            count[s] = count.get(s, 0) + 1
+            ins.then_inc(T.sem[s], 1)
+        else:
+            s, v = o["sem"]
+            count[s] = count.get(s, 0) + v
+            if q == "s":
+                ins.then_inc(T.sem[s], v)
+        done[i] = (s, count[s])
+        clock[i] = {} if q == "n" else dict(kn)
+    kn = known["g"]
+    for s in count:
+        if kn.get(s, 0) < count[s]:
+            g.wait_ge(T.sem[s], count[s])

@@ -1,126 +1,132 @@
 import numpy as np
+from concourse.bass import DstId, RemoteDMATransfer
 from concourse.mybir import AluOpType as OP, AxisListType, ActivationFunctionType as AF
 
 NST = 5
-XS = 257
-THR = 16384.0
-DIST = ((0, 0), (0, 64), (64, 96), (96, 128))
+ND = 64
+TW = 1280
 BIG = 2.0 ** 20
-ON_DVE = (0, 2, 4, 6)
 
-SCRATCH = {
-    "G": ("sbuf", [128, 4096], "bfloat16"), "BKI": ("sbuf", [128, 1024], "int32"),
-    "BK": ("sbuf", [128, 1152], "float32"), "IM": ("sbuf", [128, 1152], "bfloat16"),
-    "ZB": ("sbuf", [128, 256], "bfloat16"), "WI": ("sbuf", [128, 1], "int32"),
-    "Z1": ("sbuf", [128, 128], "bfloat16"), "Z2": ("sbuf", [128, 128], "bfloat16"),
-    "Z3": ("sbuf", [128, 128], "bfloat16"), "Z4": ("sbuf", [128, 128], "bfloat16"),
-    "CR": ("sbuf", [128, 384], "bfloat16"), "HI": ("sbuf", [128, 640], "bfloat16"), "TI": ("sbuf", [128, 640], "bfloat16"),
-    "X0": ("sbuf", [128, 8 * XS], "bfloat16"), "X1": ("sbuf", [128, 8 * XS], "bfloat16"),
-    "AB": ("sbuf", [128, 2048], "bfloat16"), "EQ": ("sbuf", [128, 1024], "bfloat16"),
-    "SEL": ("sbuf", [128, 512], "bfloat16"), "MK2": ("sbuf", [128, 128], "bfloat16"),
-    "cI": ("sbuf", [128, 128], "int32"), "cg": ("sbuf", [128, 640], "int32"), "cm": ("sbuf", [128, 128], "int32"),
-    "pc": ("sbuf", [128, 32], "int32"), "pf": ("sbuf", [128, 64], "float32"),
-    "tw": ("sbuf", [128, 128], "float32"), "tf": ("sbuf", [128, 128], "float32"), "tf2": ("sbuf", [128, 128], "float32"),
-    "rows": ("sbuf", [128, 1024], "bfloat16"),
-    "oXA": ("sbuf", [128, 16], "uint16"),
-    "P0": ("psum", [128, 512], "float32"), "P1": ("psum", [128, 512], "float32"), "P2": ("psum", [128, 512], "float32"),
-    "P3": ("psum", [128, 512], "float32"), "P4": ("psum", [128, 512], "float32"), "P5": ("psum", [128, 512], "float32"),
-    "P6": ("psum", [128, 512], "float32"), "P7": ("psum", [128, 512], "float32"),
-}
-for _n in ("I", "nI", "BO", "cap", "KF", "KC", "ONES", "HALF", "I16", "nI16", "nI256", "D32", "Kc", "Kn", "CO1", "CO2",
-           "WH", "WL", "VH", "VL",
-           "zT0", "zT1", "BE", "BD", "DM", "qt", "ivm", "Fs", "Sg", "W", "E1", "wq", "S", "nim"):
-    SCRATCH[_n] = ("sbuf", [128, 128], "bfloat16")
-for _n in ("R8", "G16", "hv"):
-    SCRATCH[_n] = ("sbuf", [128, 8], "bfloat16")
-for _n in ("Ui", "u", "sq", "s5", "bb", "bbm", "ub", "ubm", "bi", "bm"):
-    SCRATCH[_n] = ("sbuf", [128, 128], "int32")
-for _n in ("mb", "sw0", "sw1", "c", "h3", "e2", "s3", "t1", "nb"):
-    SCRATCH[_n] = ("sbuf", [128, 128], "float32")
-for _n in ("goff0", "goff1", "soff0", "soff1"):
-    SCRATCH[_n] = ("sbuf", [128, 8], "uint16")
-SCRATCH["b16"] = ("sbuf", [128, 128], "uint16")
-for _n in ("vi", "so"):
-    SCRATCH[_n] = ("sbuf", [128, 8], "int32")
-SCRATCH["vm"] = ("sbuf", [128, 16], "int32")
-for _n in ("nwi0", "nwi1", "dmin", "hm", "sk"):
-    SCRATCH[_n] = ("sbuf", [128, 8], "float32")
-for _n in ("zr0", "zr1"):
-    SCRATCH[_n] = ("sbuf", [128, 1024], "bfloat16")
-for _n in ("MK", "zr4", "BT0", "BT1", "WE", "A12", "F", "FD", "C", "CD", "L"):
-    SCRATCH[_n] = ("sbuf", [128, 256], "bfloat16")
-for _n in ("Ps", "Ns"):
-    SCRATCH[_n] = ("sbuf", [128, 384], "bfloat16")
-SCRATCH["B"] = ("sbuf", [128, 128], "bfloat16")
-for _n in ("ab", "h12", "hb12"):
-    SCRATCH[_n] = ("sbuf", [128, 256], "float32")
-SCRATCH["RS"] = ("sbuf", [128, 256], "bfloat16")
-SCRATCH["SM"] = ("sbuf", [128, 128], "bfloat16")
-SCRATCH["XT"] = ("sbuf", [128, 128], "bfloat16")
+SCRATCH = {}
+
+
+def _bufs(names, cols, dtype, where="sbuf"):
+    for n in names.split():
+        SCRATCH[n] = (where, [128, cols], dtype)
+
+
+_bufs("G", 4096, "bfloat16")
+_bufs("X0 X1 AB", 2048, "bfloat16")
+_bufs("BKI bti", 1024, "int32")
+_bufs("BK", TW, "float32")
+_bufs("IM", TW, "bfloat16")
+_bufs("BT EQ", 1024, "bfloat16")
+_bufs("zr0 zr1", 16 * ND, "bfloat16")
+_bufs("zr4", 4 * ND, "bfloat16")
+_bufs("CO", 512, "bfloat16")
+_bufs("SEL", 2048 - 16 * ND, "bfloat16")
+_bufs("CR", 768, "bfloat16")
+_bufs("THR", 272, "bfloat16")
+_bufs("ZB ROWS WE D12 P12 N12 S21 TD FD zz0 zz1", 256, "bfloat16")
+_bufs("KB", 144, "bfloat16")
+_bufs("GM", 56, "bfloat16")
+_bufs("Z1 Z2 Z3 Z4 ONES I nI hI KF D4 nI16 nI256 BO MK MK2 RS D8W BO8 REP nREP WH WL SM sm zT0 zT1 BD BE Bu0 Bu1 DM "
+      "qt Fs ivm Sg sk H W E1 wq S B XT r", 128, "bfloat16")
+_bufs("R8 G16 nG16", 8, "bfloat16")
+_bufs("ab", 288, "float32")
+_bufs("hb", 272, "float32")
+_bufs("s3", 144, "float32")
+_bufs("c e2 t1 ns mU AL", 128, "float32")
+_bufs("pf tw", 64, "float32")
+_bufs("R8f iw y sq nwi hc", 8, "float32")
+_bufs("cg cm c8 bi bm", 128, "int32")
+_bufs("c7", 56, "int32")
+_bufs("pc vi vm0 vm1", 16, "int32")
+_bufs("WI", 1, "int32")
+_bufs("Ui u so", 8, "int32")
+_bufs("b16", 128, "uint16")
+_bufs("go0 go1 oX", 16, "uint16")
+_bufs("sf0 sf1", 8, "uint16")
+_bufs("PK PQ PA PB PS PW PR PD", 512, "float32", "psum")
 
 SEMAPHORES = ["sv", "sa", "st", "sg", "ls"] + ["dm%d" % i for i in range(8)] + ["rz%d" % t for t in range(1, 5)]
 CNT = {"v": "sv", "a": "sa", "t": "st", "g": "sg"}
+CY, GATH, SCAT = 0.83, 1.56, 3.8
 
 
 def build(g, T, topo, core):
     ops = []
-
-    def op(q, dur, reads, writes, *fns, banks=(), sem=None):
-        ops.append({"q": q, "dur": dur, "r": tuple(reads), "w": tuple(writes), "f": fns, "b": tuple(banks), "sem": sem})
-
     V, S, PE = g.vector, g.scalar, g.tensor
 
-    def dv(n, x=1.0):
-        return 35 + max(64.0, n * x) * 0.83 * 1.2
+    def op(q, dur, reads, writes, *fns, bank=None, sem=None, hard=False):
+        ops.append({"q": q, "dur": dur, "r": reads.split(), "w": writes.split(), "f": fns, "b": bank, "sem": sem, "hard": hard})
 
-    def ac(n):
-        return 60 + max(64.0, n) * 0.83 * 1.2
+    def dv(ap, x):
+        return 50 + max(64.0, ap.shape[1] * x) * CY
 
-    def pe(n):
-        return 60 + n * 0.6
+    def copy(out, in_, r, w, bank=None, x=1.0):
+        op("v", dv(in_, x), r, w, lambda: V.tensor_copy(out, in_), bank=bank)
 
-    def copy(out, in_, n, r, w, banks=(), x=1.0):
-        op("v", dv(n, x), r, w, lambda: V.tensor_copy(out, in_), banks=banks)
+    def tt(out, in0, in1, o, r, w, bank=None, x=None):
+        op("v", dv(in1, x or (1.0 if bank else 2.0)), r, w, lambda: V.tensor_tensor(out, in0, in1, o), bank=bank)
 
-    def tt(out, in0, in1, o, n, r, w, banks=(), x=2.0):
-        op("v", dv(n, x), r, w, lambda: V.tensor_tensor(out, in0, in1, o), banks=banks)
-
-    def ts(out, in0, s1, o1, n, r, w, s2=None, o2=None, banks=(), x=1.0):
+    def ts(out, in0, s1, o1, r, w, s2=None, o2=None, bank=None, x=1.0):
         if o2 is None:
-            op("v", dv(n, x), r, w, lambda: V.tensor_scalar(out, in0, s1, None, o1), banks=banks)
+            op("v", dv(out, x), r, w, lambda: V.tensor_scalar(out, in0, s1, None, o1), bank=bank)
         else:
-            op("v", dv(n, x), r, w, lambda: V.tensor_scalar(out, in0, s1, s2, o1, o2), banks=banks)
+            op("v", dv(out, x), r, w, lambda: V.tensor_scalar(out, in0, s1, s2, o1, o2), bank=bank)
 
-    def scan(out, d0, d1, o0, o1, n, r, w, banks=()):
-        op("v", dv(n), r, w, lambda: V.tensor_tensor_scan(out, d0, d1, 0.0, o0, o1), banks=banks)
+    def scan(out, d0, d1, init, o0, o1, r, w, bank=None):
+        op("v", dv(out, 1.0), r, w, lambda: V.tensor_tensor_scan(out, d0, d1, init, o0, o1), bank=bank)
 
-    def act(out, in_, f, n, r, w, bias=0.0, scale=1.0, banks=(), x=1.0):
-        op("a", ac(n * x), r, w, lambda: S.activation(out, in_, f, bias, scale), banks=banks)
+    def reduce_(out, in_, r, w):
+        op("v", dv(in_, 1.0), r, w, lambda: V.tensor_reduce(out, in_, AxisListType.X, OP.add))
 
-    def mm(n, r, bank, *calls, grp=(), hard=False):
+    def memset(ap, val, w):
+        op("v", dv(ap, 0.5), "", w, lambda: V.memset(ap, val))
+
+    def act(out, in_, f, r, w, bias=0.0, scale=1.0, bank=None, x=1.0, accum=None):
+        d = 70 + max(64.0, out.shape[1] * x) * CY
+        if accum is None:
+            op("a", d, r, w, lambda: S.activation(out, in_, f, bias, scale), bank=bank)
+        else:
+            op("a", d + 20, r, w, lambda: S.activation(out, in_, f, bias, scale, accum_out=accum), bank=bank)
+
+    def mm(r, bank, calls, grp="", hard=False, x=1):
         def one(a):
             return lambda: PE.matmul(*a)
-        op("t", pe(n), r, grp, *[one(a) for a in calls], banks=(bank,))
-        ops[-1]["hard"] = hard
+        d = sum(10 + 0.45 * x * max(min(64, a[1].shape[1]), a[2].shape[1]) for a in calls)
+        op("t", d, r, grp, *[one(a) for a in calls], bank=bank, hard=hard)
 
-    def pcopy(out, in_, r, w, n=128):
-        op("g", 230 + 2 * n, r, w, lambda: g.affine_select(out, in_, [[1, n]], OP.is_ge, 0.0, 0, 0))
+    def acc(out, *terms, start=True, stop=True):
+        n = len(terms)
+        return [(out, a, b, start and i == 0, stop and i == n - 1) for i, (a, b) in enumerate(terms)]
 
-    def memset(ap, val, n, w):
-        op("v", dv(n, 0.5), (), w, lambda: V.memset(ap, val))
+    def select(out, in_, pattern, cmp_, base, cm, r, w):
+        op("g", 170 + 2 * CY * out.shape[1], r, w, lambda: g.affine_select(out, in_, pattern, cmp_, 0.0, base, cm))
+
+    def pcopy(out, in_, r, w):
+        select(out, in_, [[1, in_.shape[1]]], OP.is_ge, 0, 0, r, w)
+
+    def iota(out, pattern, base, cm, w, r="", cast=False):
+        d = 130 + 2 * CY * out.shape[1]
+        if cast:
+            op("g", d, r, w, lambda: g.iota(out, pattern, base, cm, allow_small_or_imprecise_dtypes=True))
+        else:
+            op("g", d, r, w, lambda: g.iota(out, pattern, base, cm))
 
     nd = [0]
 
-    def load(out, in_, w, dur, r=()):
+    def dma(out, in_, r, w, dur):
         s = "dm%d" % nd[0]
         nd[0] += 1
         op("s", dur, r, w, lambda: g.sync.dma_start(out, in_), sem=(s, 16))
 
-    load(T.WI[:], T.wt[:], ("WI",), 2000)
-    load(T.ZB[:], T.bites[:], ("ZB",), 2200)
-    load(T.BKI[:], T.bank[:], ("BKI",), 4000)
-    load(T.IM[:, 0:1024], T.immun[:], ("IM",), 5000)
-    load(T.G[:], T.geno[:], ("G",), 8500)
+    dma(T.WI[:], T.wt[:], "", "WI", 1900)
+    dma(T.ZB[:], T.bites[:], "", "ZB", 2200)
+    dma(T.BKI[:], T.bank[:], "", "BKI", 4500)
+    dma(T.G[:], T.geno[:], "", "G", 8000)
+    dma(T.IM[:, 0:1024], T.immun[:], "", "IM", 9000)
 
     rank = T.rank_of(core)
     cores = list(T.cores)
@@ -129,144 +135,142 @@ def build(g, T, topo, core):
     def engs(src, dst):
         return topo.engines(src, dst)[:8]
 
-    def send(src_ap, key, dst, t):
+    def send(srcs, key, hop, t):
+        dst = cores[(rank + hop) % nr]
         e = engs(core, dst)
-        m = 0
-        for x in e:
-            m |= 1 << x
+        m = sum(1 << x for x in e)
         a = topo.addr(dst)
-        zt = T["Z%d" % t]
-        op("g", 300, (key,), ("sent%d" % t,), lambda: g.remote_dma(zt[:], src_ap, T.sem["rz%d" % t], T.sem.ls, a[1], a[0], m),
-           sem=("ls", len(e)))
-        frm = cores[(rank - (1 if t == 1 else 2)) % nr]
-        op("n", 3500, ("sent%d" % t,), ("Z%d" % t,), sem=("rz%d" % t, len(engs(frm, core))))
+        zt, rs = T["Z%d" % t], T.sem["rz%d" % t]
+        if len(srcs) == 1:
+            f = lambda: g.remote_dma(zt[:], srcs[0], rs, T.sem.ls, a[1], a[0], m)
+        else:
+            f = lambda: g.remote_dma_fused([RemoteDMATransfer(dst_ids=[DstId(rid=a[0], pnc=a[1])], dma_engine_mask=m, remote_sem=rs,
+                                                              srcs=list(srcs), dsts=[zt[:]], alu_op=2)], local_sem=T.sem.ls)
+        op("g", 300, key, "sent%d" % t, f, sem=("ls", len(e)))
+        op("n", 2300, "sent%d" % t, "Z%d" % t, sem=("rz%d" % t, len(engs(cores[(rank - hop) % nr], core))))
 
-    op("g", 180, (), ("pI",), lambda: g.iota(T.pc[:, 0:1], [[1, 1]], 0, 1))
-    op("g", 380, (), ("cg",), lambda: g.iota(T.cg[:, 0:128], [[1, 8], [0, 16]], 0, 0))
-    op("g", 380, (), ("cm",), lambda: g.iota(T.cm[:], [[0, 8], [1, 16]], 0, 0))
-    op("g", 380, (), ("cI",), lambda: g.iota(T.cI[:], [[1, 128]], 0, 0))
-    memset(T.ONES[:], 1.0, 128, ("ONES",))
-    memset(T.HALF[:], 0.5, 128, ("HALF",))
-    memset(T.rows[:, 0:128], -2080.0, 128, ("rowA",))
-    memset(T.rows[:, 128:256], 2336.0, 128, ("rowB",))
-    memset(T.c[:], 0.0, 128, ("c",))
-    memset(T.h12[:], 0.0, 512, ("h12",))
-    memset(T.h3[:], 0.0, 256, ("h3",))
-    pc, pf = T.pc, T.pf
-    pi = pc[:, 0:1]
-    copy(pf[:, 0:1], pi, 1, ("pI",), ("f0",))
-    ts(pc[:, 1:2], pi, 4, OP.logical_shift_right, 1, ("pI",), ("i1",))
-    ts(pc[:, 2:3], pi, 15, OP.bitwise_and, 1, ("pI",), ("i2",))
-    copy(pf[:, 1:2], pc[:, 1:2], 1, ("i1",), ("f1",))
-    copy(pf[:, 2:3], pc[:, 2:3], 1, ("i2",), ("f2",))
-    cI = T.cI[:]
-    op("g", 1050, (), ("cg5",), lambda: g.iota(T.cg[:, 128:640], [[1, 32], [0, 16]], 0, 0))
-    cg, cm = T.cg[:, 0:128], T.cm[:]
-    ts(T.BO[:], cg, pf[:, 1:2], OP.is_equal, 128, ("cg", "f1"), ("BO",))
-    ts(pc[:, 8:9], T.WI[:], 4032, OP.bitwise_and, 1, ("WI",), ("i8",))
-    ts(pc[:, 9:10], T.WI[:], 63, OP.bitwise_and, 1, ("WI",), ("i9",))
-    copy(pf[:, 8:9], pc[:, 8:9], 1, ("i8",), ("f8",))
-    copy(pf[:, 9:10], pc[:, 9:10], 1, ("i9",), ("f9",))
-    ts(T.WH[:], T.BO[:], pf[:, 8:9], OP.mult, 128, ("BO", "f8"), ("WH",))
-    ts(T.WL[:], T.BO[:], pf[:, 9:10], OP.mult, 128, ("BO", "f9"), ("WL",))
-    ts(pc[:, 10:11], T.WI[:], 37, OP.mult, 1, ("WI",), ("i10",))
-    ts(pc[:, 11:12], pc[:, 10:11], 992, OP.bitwise_and, 1, ("i10",), ("i11",))
-    ts(pc[:, 12:13], pc[:, 10:11], 31, OP.bitwise_and, 1, ("i10",), ("i12",))
-    copy(pf[:, 11:12], pc[:, 11:12], 1, ("i11",), ("f11",))
-    copy(pf[:, 12:13], pc[:, 12:13], 1, ("i12",), ("f12",))
-    act(T.VH[:], T.BO[:], AF.Copy, 128, ("BO", "f11"), ("VH",), scale=pf[:, 11:12])
-    act(T.VL[:], T.BO[:], AF.Copy, 128, ("BO", "f12"), ("VL",), scale=pf[:, 12:13])
-    ts(T.MK[:, 0:128], cm, pf[:, 2:3], OP.is_equal, 128, ("cm", "f2"), ("MKa",))
-    act(T.MK[:, 128:256], T.MK[:, 0:128], AF.Copy, 128, ("MKa",), ("MK",))
-    ts(T.RS[:, 0:128], cm, 0.0, OP.is_gt, 128, ("cm",), ("RSa",))
-    act(T.RS[:, 128:256], T.RS[:, 0:128], AF.Copy, 128, ("RSa",), ("RS",))
-    ts(T.I[:], cI, pf[:, 0:1], OP.is_equal, 128, ("cI", "f0"), ("I",))
-    ts(T.R8[:], T.cI[:, 0:8], pf[:, 1:2], OP.is_equal, 8, ("cI", "f1"), ("R8",))
-    ts(T.tf[:], T.RS[:, 0:128], 0.5, OP.mult, 128, ("RSa",), ("tf",))
-    ts(T.tf2[:], T.RS[:, 0:128], -512.0, OP.mult, 128, ("RSa",), ("tf2",), s2=512.0, o2=OP.add)
-    scan(T.mb[:], T.tf[:], T.tf2[:], OP.mult, OP.add, 128, ("tf", "tf2"), ("mb",))
-    tt(T.tf[:], T.mb[:], T.I[:], OP.mult, 128, ("mb", "I"), ("tf",))
-    op("v", dv(128), ("tf",), ("f5",), lambda: V.tensor_reduce(pf[:, 5:6], T.tf[:], AxisListType.X, OP.add))
-    ts(pf[:, 6:7], pf[:, 2:3], 8.0, OP.is_ge, 1, ("f2",), ("f6",))
-    ts(pf[:, 7:8], pf[:, 6:7], 63.75, OP.mult, 1, ("f6",), ("f7",), s2=0.25, o2=OP.add)
-    tt(pf[:, 10:11], pf[:, 7:8], pf[:, 5:6], OP.mult, 1, ("f7", "f5"), ("f10",))
-    ts(pc[:, 13:14], pc[:, 1:2], 1, OP.bitwise_and, 1, ("i1",), ("i13",))
-    ts(pf[:, 13:14], pf[:, 2:3], 10.0, OP.is_lt, 1, ("f2",), ("f13",))
-    tt(pf[:, 14:15], pf[:, 13:14], pc[:, 13:14], OP.mult, 1, ("f13", "i13"), ("f14",))
-    tt(pf[:, 15:16], pf[:, 13:14], pf[:, 14:15], OP.subtract, 1, ("f13", "f14"), ("f15",))
-    ts(pf[:, 16:18], pf[:, 14:16], 1.0 / 256, OP.mult, 2, ("f14", "f15"), ("f16",))
-    ts(pf[:, 18:20], pf[:, 14:16], -1.0, OP.mult, 2, ("f14", "f15"), ("f18",))
-    ts(T.tf[:, 0:8], T.cI[:, 0:8], 16.0, OP.mult, 8, ("cI", "tf"), ("tf",), s2=1024.0, o2=OP.add)
-    ts(pf[:, 48:56], T.tf[:, 0:8], pf[:, 2:3], OP.add, 8, ("tf", "f2"), ("iw",))
-    ts(pc[:, 3:4], pi, 31, OP.bitwise_and, 1, ("pI",), ("i3",))
-    copy(pf[:, 3:4], pc[:, 3:4], 1, ("i3",), ("f3",))
-    ts(pf[:, 4:5], pf[:, 0:1], 32.0, OP.mult, 1, ("f0",), ("f4",))
-    ts(T.SEL[:], T.cg[:, 128:640], pf[:, 3:4], OP.is_equal, 512, ("cg5", "f3"), ("SEL",), s2=-1.0, o2=OP.mult)
-    act(T.G16[:], T.R8[:], AF.Copy, 8, ("R8",), ("G16",), scale=16.0)
-    act(T.KC[:], T.BO[:], AF.Copy, 128, ("BO",), ("KC",), scale=128.0)
-    ts(T.rows[:, 512:640], cm, -1.0, OP.mult, 128, ("cm",), ("rowR",), s2=15.0, o2=OP.add)
-    ts(T.rows[:, 672:688], T.cI[:, 0:16], 8.0, OP.is_ge, 16, ("cI",), ("rowZ",), s2=-8.0, o2=OP.mult)
-    tt(T.rows[:, 656:672], T.cI[:, 0:16], T.rows[:, 672:688], OP.add, 16, ("cI", "rowZ"), ("rowY",))
-    ts(T.rows[:, 640:656], T.rows[:, 656:672], 256.0, OP.mult, 16, ("rowY",), ("rowX",))
+    pc, pf, tw = T.pc, T.pf, T.tw
 
-    def cst(name, t):
-        return T[name][:, 128 * t:128 * t + 128]
+    def col(i, n=1):
+        return pf[:, i:i + n]
 
-    def scaled(name, val, t=None):
-        out = T[name][:] if t is None else cst(name, t)
-        act(out, T.I[:], AF.Copy, 128, ("I",), (name if t is None else name + str(t),), scale=val)
+    memset(T.ONES[:], 1.0, "ONES")
+    iota(pc[:, 0:1], [[1, 1]], 0, 1, "pI")
+    iota(T.cm[:], [[0, 8], [1, 16]], 0, 0, "cm")
+    for j, (s, o) in enumerate(((15, OP.bitwise_and), (7, OP.bitwise_and), (3, OP.logical_shift_right), (16, OP.bitwise_and))):
+        ts(pc[:, 1 + j:2 + j], pc[:, 0:1], s, o, "pI", "i%d" % j)
+    copy(col(0, 4), pc[:, 1:5], "i0 i1 i2 i3", "fp")
+    select(T.BO[:], T.ONES[:], [[-16, 8], [0, 16]], OP.is_ge, 0, 1, "ONES", "BO")
+    select(T.BO[:], T.BO[:], [[16, 8], [0, 16]], OP.is_ge, 15, -1, "BO", "BO")
+    R8 = T.R8[:]
+    act(R8, T.BO[:, 0::16], AF.Copy, "BO", "R8")
+    act(T.R8f[:], T.BO[:, 0::16], AF.Copy, "BO", "R8f")
+    ts(T.MK[:], T.cm[:], col(0), OP.is_equal, "cm fp", "MK")
+    ts(pc[:, 8:9], T.WI[:], 4032, OP.bitwise_and, "WI", "i8")
+    ts(pc[:, 9:10], T.WI[:], 63, OP.bitwise_and, "WI", "i9")
+    copy(col(8, 2), pc[:, 8:10], "i8 i9", "fw")
+    act(T.WH[:], T.BO[:], AF.Copy, "BO fw", "WH", scale=col(8))
+    act(T.WL[:], T.BO[:], AF.Copy, "BO fw", "WL", scale=col(9))
+    select(T.I[:], T.ONES[:], [[-1, 128]], OP.is_equal, 0, 1, "ONES", "I")
+    for name, val in (("nI", -1.0), ("KF", 8192.0), ("nI16", -16.0), ("nI256", -256.0), ("hI", 0.5)):
+        act(T[name][:], T.I[:], AF.Copy, "I", name, scale=val)
+    act(T.G16[:], R8, AF.Copy, "R8", "G16", scale=16.0)
+    act(T.nG16[:], R8, AF.Copy, "R8", "nG16", scale=-16.0)
+    memset(T.SEL[:], -1.0, "SEL")
 
-    for name, val in (("KF", THR), ("I16", 16.0), ("nI16", -16.0), ("nI", -1.0), ("nI256", -256.0)):
-        scaled(name, val)
-    act(T.D32[:], T.I[:], AF.Copy, 128, ("I", "f4"), ("D32",), scale=pf[:, 4:5])
-    for t in range(NST):
-        scaled("HI", 4096.0 * (8 + t), t)
-        if t:
-            scaled("TI", float(t), t)
+    def sel(e, lo=0, hi=128):
+        return T.SEL[lo:hi, 512 * e - 16 * ND:512 * e - 16 * ND + 512]
+    for e in range(ND // 32, 4):
+        select(sel(e), sel(e), [[-1, 32], [0, 16]], OP.is_equal, -32 * e, 1, "SEL", "SEL%d" % e)
+    select(T.RS[:], T.ONES[:], [[0, 8], [1, 16]], OP.is_gt, 0, 0, "ONES", "RS")
+    iota(T.ROWS[0:2, 0:128], [[-32768, 8], [0, 16]], 8192 + 7 * 32768, 0, "row1", "", True)
+    iota(T.ROWS[0:2, 128:256], [[-512, 8], [0, 16]], 2336 + 7 * 512, 0, "row2", "", True)
+    iota(T.ROWS[0:1, :], [[0, 16], [-1, 16]], 15, 0, "row1 row2", "", True)
+    memset(T.THR[:], BIG, "THR")
+    for o in (0, 144):
+        iota(T.THR[:, o:o + 128:16], [[-32768, 8]], 16384 + 7 * 32768, 0, "THR%d" % o, "THR", True)
+    memset(T.ab[:, 128:288], 0.0, "abp")
+    memset(T.ab[:, 143:144], BIG, "abp")
+    memset(T.c[:, 0:1], 0.0, "c")
+    memset(T.s3[:, 128:144], 0.0, "s3p")
+    for d in range(2):
+        memset(T["zz%d" % d][:], 0.0, "zz%d" % d)
+    iota(T.tw[:, 63:64], [[1, 1]], 0, 4, "p4", cast=True)
+    act(T.D4[:], T.I[:], AF.Copy, "I p4", "D4", scale=tw[:, 63:64])
+    memset(tw[:, 0:16], 0.5, "tw0")
+    memset(tw[:, 16:32], 0.0, "tw1")
+    scan(tw[:, 32:48], tw[:, 0:16], tw[:, 16:32], 1024.0, OP.mult, OP.add, "tw0 tw1", "tw2")
+    tt(tw[:, 0:16], tw[:, 32:48], T.MK[:, 0:16], OP.mult, "tw2 MK", "tw0")
+    reduce_(col(10), tw[:, 0:16], "tw0", "f10")
+    iota(T.bti[:], [[1, 1024]], 0, 0, "bti")
+    ts(T.bti[:], T.bti[:], col(10), OP.mult, "bti f10", "bti")
+    ts(T.bti[:], T.bti[:], 512, OP.bitwise_and, "bti", "bti")
+    ts(T.BT[:], T.bti[:], 1.0 / 256, OP.mult, "bti", "BT", s2=-1.0, o2=OP.add)
+    ts(col(11), col(3), 1.0 / 16, OP.mult, "fp", "odd")
+    ts(col(12), col(3), 0.0, OP.is_equal, "fp", "even")
+    memset(tw[:, 48:56], 1.0 / 64, "tw3")
+    scan(tw[:, 32:40], tw[:, 48:56], tw[:, 16:24], 64.0, OP.mult, OP.add, "tw3 tw1", "tw2")
+    tt(tw[:, 48:56], tw[:, 32:40], R8, OP.mult, "tw2 R8", "tw3")
+    reduce_(col(13), tw[:, 48:56], "tw3", "f13")
+    op("v", 250, "f13", "f14", lambda: V.reciprocal(col(14), col(13)))
+    ts(col(15), col(14), 8192.0, OP.mult, "f14", "f15")
+    ts(tw[:, 0:16], T.cm[:, 0:16], col(0), OP.is_gt, "cm fp", "tw0", s2=1.9375, o2=OP.mult)
+    WT, rowC, rowN = T.sm[:, 0:16], T.sm[0:1, 16:32], T.sm[0:1, 32:40]
+    ts(WT, tw[:, 0:16], 0.0625, OP.add, "tw0 f13", "WT", s2=col(13), o2=OP.mult)
+    act(T.MK2[:], T.MK[:], AF.Copy, "MK f15", "MK2", scale=col(15))
+    memset(rowN, -14336.0, "rowN")
+    iota(T.iw[:], [[16, 8]], 1024, 1, "iw", cast=True)
+    iota(rowC, [[0, 2], [256, 8]], 0, 0, "rowC", cast=True)
+    ts(col(16), col(0), 16.0, OP.mult, "fp", "f16")
+    memset(T.KB[:], 0.0, "KB")
+    act(T.KB[:, 15:143:16], R8, AF.Copy, "R8 fp KB", "KB", scale=col(0))
+    iota(T.cg[:], [[1, 8], [0, 16]], 0, 0, "cg")
+    iota(T.c7[:], [[0, 7], [1, 8]], 0, 0, "c7")
+    iota(T.c8[:], [[0, 16], [1, 8]], 0, 0, "c8")
+    ts(T.D8W[:], T.cg[:], col(1), OP.is_equal, "cg fp", "D8W")
+    ts(col(17), col(2), 0.0, OP.is_equal, "fp", "f17", s2=2.0, o2=OP.mult)
+    ts(col(18), col(17), -1.0, OP.add, "f17", "f18")
+    D16, L1, L2, GM, M1 = T.sm[:, 40:56], T.sm[:, 56:72], T.sm[0:8, 72:88], T.GM[0:16, :], T.sm[0:56, 88:128]
+    ts(D16, T.c7[:, 0:16], col(1), OP.is_equal, "c7 fp f18", "D16", s2=col(18), o2=OP.mult)
     for j in range(2):
-        memset(T["X%d" % j][:, 0:4 * XS:XS], -64.0, 4, ["Xs%d" % j])
-        memset(T["X%d" % j][:, 4 * XS::XS], -1.0, 4, ["Xt%d" % j])
-    tw = T.tw
-    ts(tw[:, 64:72], T.cI[:, 0:8], 0.0, OP.is_equal, 8, ("cI",), ("d1",))
-    for nm_, base_, o in (("n", 1.0 / 64, 0), ("p", 64.0, 24)):
-        memset(tw[:, 72 + o:80 + o], base_, 8, ("d0" + nm_,))
-        scan(tw[:, 80 + o:88 + o], tw[:, 72 + o:80 + o], tw[:, 64:72], OP.mult, OP.add, 8, ("d0" + nm_, "d1"), ("pw" + nm_,))
-        tt(tw[:, 88 + o:96 + o], tw[:, 80 + o:88 + o], T.R8[:], OP.mult, 8, ("pw" + nm_, "R8"), ("px" + nm_,))
-    op("v", dv(8), ("pxn",), ("f57",), lambda: V.tensor_reduce(pf[:, 57:58], tw[:, 88:96], AxisListType.X, OP.add))
-    op("v", dv(8), ("pxp",), ("f58",), lambda: V.tensor_reduce(pf[:, 58:59], tw[:, 112:120], AxisListType.X, OP.add))
-    ts(tw[:, 8:24], T.cm[:, 0:16], pf[:, 2:3], OP.is_gt, 16, ("cm", "f2"), ("wt0",), s2=1.9375, o2=OP.mult)
-    ts(T.rows[:, 900:916], tw[:, 8:24], 0.0625, OP.add, 16, ("wt0", "f57"), ("WT",), s2=pf[:, 57:58], o2=OP.mult)
-    act(T.MK2[:], T.MK[:, 0:128], AF.Copy, 128, ("MKa", "f58"), ("MK2",), scale=pf[:, 58:59])
-    ts(pf[:, 20:21], pf[:, 2:3], 1.0, OP.add, 1, ("f2",), ("f20",))
-    ts(T.tf2[:], cm, 16.0, OP.mult, 128, ("cm", "f20"), ("tf2",), s2=pf[:, 20:21], o2=OP.add)
-    tt(T.Kc[:], T.tf2[:], T.BO[:], OP.mult, 128, ("tf2", "BO"), ("Kc",))
-    act(T.Kn[:], T.Kc[:], AF.Copy, 128, ("Kc",), ("Kn",), scale=-1.0)
-    ts(pc[:, 4:5], pi, 3, OP.logical_shift_right, 1, ("pI",), ("i4",))
-    ts(pc[:, 5:6], pi, 7, OP.bitwise_and, 1, ("pI",), ("i5",))
-    copy(pf[:, 21:22], pc[:, 5:6], 1, ("i5",), ("f21",))
-    for j in range(6):
-        ts(pf[:, 22 + j:23 + j], pc[:, 4:5], float(j), OP.is_equal, 1, ("i4",), ("f%d" % (22 + j),))
-    tt(pf[:, 32:35], pf[:, 22:25], pf[:, 25:28], OP.add, 3, ["f%d" % j for j in range(22, 28)], ("f32",))
-    tt(pf[:, 35:37], pf[:, 32:34], pf[:, 33:35], OP.subtract, 2, ("f32",), ("f35",))
-    tt(pf[:, 37:38], pf[:, 32:33], pf[:, 34:35], OP.subtract, 1, ("f32",), ("f37",))
-    for j in range(3):
-        ts(T.SM[:, 8 * j:8 * j + 8], T.cI[:, 0:8], pf[:, 21:22], OP.is_equal, 8, ("cI", "f21", "f35", "f37"), ("M1%d" % j,),
-           s2=pf[:, 35 + j:36 + j], o2=OP.mult)
-    memset(T.SM[:, 24:32], 0.0, 8, ("M13",))
-    memset(T.SM[:, 32:120], 0.0, 88, ("RB",))
-    copy(T.SM[:, 72:80], T.R8[:], 8, ("R8",), ("RB",), x=0.5)
-    ts(pf[:, 38:44], pf[:, 22:28], 0.5, OP.mult, 6, ["f%d" % j for j in range(22, 28)], ("f38",))
-    tt(pf[:, 46:47], pf[:, 25:26], pf[:, 26:27], OP.add, 1, ("f25", "f26"), ("f46",))
-    ts(pf[:, 29:30], pf[:, 46:47], -2.0, OP.mult, 1, ("f46",), ("f29",))
-    tt(pf[:, 44:45], pf[:, 39:40], pf[:, 38:39], OP.subtract, 1, ("f38",), ("f44",))
-    tt(pf[:, 28:29], pf[:, 44:45], pf[:, 29:30], OP.add, 1, ("f44", "f29"), ("f28",))
-    tt(pf[:, 45:46], pf[:, 39:40], pf[:, 40:41], OP.add, 1, ("f38",), ("f45",))
-    tt(pf[:, 30:31], pf[:, 29:30], pf[:, 45:46], OP.subtract, 1, ("f29", "f45"), ("f30",))
-    ts(T.CO1[:], cg, pf[:, 21:22], OP.is_equal, 128, ("cg", "f21", "f28"), ("CO1",), s2=pf[:, 28:29], o2=OP.mult)
-    ts(T.CO2[:], cg, pf[:, 21:22], OP.is_equal, 128, ("cg", "f21", "f30"), ("CO2",), s2=pf[:, 30:31], o2=OP.mult)
+        act(T.sm[:, 56 + 8 * j:64 + 8 * j], R8, AF.Copy, "R8", "L1%d" % j, scale=-0.5)
+    act(L2, T.sm[0:8, 40:56], AF.Copy, "D16", "L2", scale=-8.0)
+    act(T.BO8[0:8, :], T.D8W[0:8, :], AF.Copy, "D8W", "BO8", scale=-256.0)
+    ts(T.AL[0:16, :], T.ONES[0:16, :], pf[0:16, 18:19], OP.mult, "ONES f18", "AL", s2=-32.0, o2=OP.mult)
+    memset(T.SM[:], 0.0, "SM")
+    act(T.SM[:, 48:56], R8, AF.Copy, "R8 SM", "SM")
+    memset(T.GM[0:16, 0:16], 0.0, "GM0")
+    act(T.GM[0:16, 16:32], T.sm[0:16, 40:56], AF.Copy, "D16", "GM1", scale=-32.0)
+    act(T.GM[0:16, 32:48], T.sm[0:16, 40:56], AF.Copy, "D16", "GM2", scale=32.0)
+    act(T.GM[0:16, 48:56], T.sm[0:16, 40:48], AF.Copy, "D16", "GM3", scale=0.375)
+    E = 20
+    ts(col(E, 7), T.c7[:, 0:7], col(2), OP.is_equal, "c7 fp", "E")
+    tt(col(28, 2), col(E, 2), col(E + 2, 2), OP.add, "E", "n01")
+    tt(col(30), col(E + 4), col(E + 5), OP.add, "E", "n2")
+    ts(col(31), col(E + 6), 4.0, OP.mult, "E", "g4")
+    ts(col(32, 2), col(29, 2), col(31), OP.add, "n01 n2 g4", "ng")
+    ts(col(34, 2), col(32, 2), -1.0, OP.mult, "ng n01", "s01", s2=col(28), o2=OP.add)
+    tt(col(36), col(29), col(33), OP.subtract, "n01 ng", "s2")
+    ts(col(37), col(E + 6), 8.0, OP.mult, "E", "s3c")
+    for j in range(4):
+        act(T.sm[:, 88 + 8 * j:96 + 8 * j], T.D8W[:, 0::16], AF.Copy, "D8W s01 s2 s3c", "M1%d" % j, scale=col(34 + j))
+    memset(T.sm[:, 120:128], 0.0, "M14")
+    tt(col(38), col(E + 2), col(E + 3), OP.add, "E", "k0")
+    tt(col(39), col(E), col(38), OP.subtract, "E k0", "k1")
+    tt(col(40), col(E + 1), col(E + 2), OP.add, "E", "k2")
+    ts(col(41), col(39), col(E + 4), OP.subtract, "k1 E", "co0", s2=0.5, o2=OP.mult)
+    ts(col(42), col(40), 0.5, OP.mult, "k2 E", "co1", s2=col(E + 4), o2=OP.subtract)
+    ts(col(43), col(39), col(E + 4), OP.add, "k1 E", "co2", s2=0.5, o2=OP.mult)
+    ts(col(44), col(40), 0.5, OP.mult, "k2", "co3")
+    for j in range(4):
+        act(T.CO[:, 128 * j:128 * j + 128], T.D8W[:], AF.Copy, "D8W co%d" % j, "CO%d" % j, scale=col(41 + j))
+    ts(T.nREP[:], T.c8[:], col(0), OP.is_equal, "c8 fp", "nREP", s2=32.0, o2=OP.mult)
+    tt(T.REP[:], T.nREP[:], T.BO[:], OP.mult, "nREP BO", "REP")
+    act(T.nREP[:], T.REP[:], AF.Copy, "REP", "nREP", scale=-1.0)
 
-    P0, P1, P2, P3, P4, P5, P6, P7 = [T["P%d" % i] for i in range(8)]
-    one1 = T.ONES[0:1, :]
+    PK, PQ, PS, PW, PR, PD = T.PK, T.PQ, T.PS, T.PW, T.PR, T.PD
+    I, nI, RS = T.I[:], T.nI[:], T.RS[:]
+    one1, one2 = T.ONES[0:1, :], T.ONES[0:2, :]
 
     def zap(t):
         return T.ZB[:, 0:128] if t == 0 else T["Z%d" % t][:]
@@ -276,215 +280,178 @@ def build(g, T, topo, core):
 
     def prep(t):
         z, k, d = zap(t), zk(t), t % 2
+        mm(k + " WH WL", "PD", acc(PD[:, 0:128], (z, T.WH[:]), (z, T.WL[:])))
+        tt(T.mU[:], PD[:, 0:128], T.MK[:], OP.mult, "MK", "mU", bank="PD")
+        mm("mU R8f", "PD", acc(PD[:, 128:136], (T.mU[:], T.R8f[:])), x=4)
+        copy(T.Ui[:], PD[:, 128:136], "", "Ui", bank="PD")
+        mm(k + " I", "PD", acc(PD[ND:128, 256:384], (z[:, ND:128], I)))
+        act(T["zT%d" % d][ND:128, :], PD[ND:128, 256:384], AF.Copy, "", "zT%d" % d, bank="PD")
+        ts(T.u[:], T.Ui[:], 4095, OP.bitwise_and, "Ui", "u")
+        ts(T.y[:], T.u[:], 1184.0, OP.add, "u", "y")
+        tt(T.vi[:, 0:8] if t == 0 else T.sq[:], T.u[:], T.y[:], OP.mult, "u y", "vi" if t == 0 else "sq")
+        if t <= NST - 3:
+            ts(T.vi[:, 8:16], T.u[:], 32.0, OP.mult, "u", "vu")
         for j in range(4):
-            pcopy(T.zr4[:, j::4], z[:, 0:64], (k,), ("zr4%d" % j,), 64)
-        for j in range(4):
-            pcopy(T["zr%d" % d][:, j::4], T.zr4[:], ["zr4%d" % i for i in range(4)], ("zr%d" % d,) if j == 3 else ("zq%d%d" % (d, j),), 256)
-        mm(256, (k, "WH", "WL"), "P6", (P6[:, 0:128], T.WH[:], z, True, False), (P6[:, 0:128], T.WL[:], z, False, True))
-        mm(256, (k, "VH", "VL"), "P6", (P6[:, 128:256], T.VH[:], z, True, False), (P6[:, 128:256], T.VL[:], z, False, True))
-        copy(T.Ui[:], P6[:, 0:128], 128, (), ("Ui",), banks=("P6",))
-        ts(T.u[:], T.Ui[:], 4095, OP.bitwise_and, 128, ("Ui",), ("u",))
-        tt(T.sq[:], T.u[:], T.u[:], OP.mult, 128, ("u",), ("sq",))
-        ts(T.s5[:], T.sq[:], 5, OP.logical_shift_right, 128, ("sq",), ("s5",))
-        tt(P6[:, 256:384], T.s5[:], P6[:, 128:256], OP.add, 128, ("s5",), ("base",), banks=("P6",), x=1.0)
-        sw = T["sw%d" % d]
-        tt(T.mb[:], P6[:, 256:384], T.MK[:, 0:128], OP.mult, 128, ("base", "MKa"), ("mb",), banks=("P6",), x=1.0)
-        scan(sw[:], T.RS[:, 0:128], T.mb[:], OP.mult, OP.add, 128, ("RSa", "mb"), ("sw%d" % d,))
-        mm(128, (k, "I"), "P6", (P6[:, 384:512], z, T.I[:], True, True))
-        act(T["zT%d" % d][:], P6[:, 384:512], AF.Copy, 128, (), ("zT%d" % d,), banks=("P6",))
+            pcopy(T.zr4[:, j::4], z[:, 0:ND], k, "zr4%d" % j)
+        for h in range(ND // 32):
+            for j in range(4):
+                pcopy(T["zr%d" % d][:, 512 * h + j:512 * h + 512:4], T.zr4[:, 128 * h:128 * h + 128], "zr40 zr41 zr42 zr43", "zr%d%d%d" % (d, h, j))
+        for j in range(2):
+            pcopy(T["zz%d" % d][:, 128 * j + ND:128 * j + 128], z[:, ND:128], k + " zz%d" % d, "zz%d%d" % (d, j))
+
+    def hosts(t):
+        d, n = t % 2, 16 if t <= NST - 3 else 8
+        if t:
+            ts(T.vi[:, 0:8], T.sq[:], PS[:, 384:385], OP.add, "sq", "vi", s2=65536.0, o2=OP.add, bank="PS")
+        ts(T["vm%d" % d][:, 0:n], T.vi[:, 0:n], 5, OP.logical_shift_right, "vi vu", "vm%d" % d, s2=1023, o2=OP.bitwise_and)
+        copy(T["go%d" % d][:, 0:n], T["vm%d" % d][:, 0:n], "vm%d" % d, "go%d" % d)
 
     def dups(t):
-        z, k, d = zap(t), zk(t), t % 2
-        ts(T.bb[:], P6[:, 256:384], pf[:, 5:6], OP.mult, 128, ("base", "f5"), ("bb",), banks=("P6",))
-        if t <= NST - 3:
-            ts(T.ub[:], P6[:, 0:128], pf[:, 10:11], OP.mult, 128, ("f10",), ("ub",), banks=("P6",))
-            ts(T.ubm[:], T.ub[:], 128, OP.bitwise_and, 128, ("ub",), ("ubm",))
-            bt = T["BT%d" % d]
-            ts(bt[:, 0:128], T.ubm[:], -1.0 / 128, OP.mult, 128, ("ubm",), ("bta%d" % d,))
-            pcopy(bt[:, 128:256], bt[:, 0:128], ("bta%d" % d,), ("BT%d" % d,))
-        ts(T.bbm[:], T.bb[:], 512, OP.bitwise_and, 128, ("bb",), ("bbm",))
-        ts(T.BD[:], T.bbm[:], pf[:, 16:17], OP.mult, 128, ("bbm", "f16", "f18"), ("BD",), s2=pf[:, 18:19], o2=OP.add)
-        ts(T.BE[:], T.bbm[:], pf[:, 17:18], OP.mult, 128, ("bbm", "f16", "f18"), ("BE",), s2=pf[:, 19:20], o2=OP.add)
+        d = t % 2
+        go, gk = T["go%d" % d][:, 0:8], "go%d" % d
+        act(T.BD[:], T.BT[:].indirect(go), AF.Copy, "BT odd " + gk, "BD", scale=col(11), x=GATH)
+        act(T.BE[:], T.BT[:].indirect(go), AF.Copy, "BT even " + gk, "BE", scale=col(12), x=GATH)
         for h in range(2):
             for j in range(2):
                 calls = []
                 for i in range(2):
                     bx = (T.BD if i else T.BE)[64 * h + 32 * j:64 * h + 32 * j + 32, :]
-                    calls.append((P0[:, 256 * j + 128 * i:256 * j + 128 * i + 128], bx, bx, True, True))
-                mm(256, ("BD", "BE"), "P0", *calls, grp=("gdup",), hard=bool(j))
-            act(T.EQ[:, 512 * h:512 * h + 512], P0[:], AF.Relu, 512, (), ("EQ%d" % h,), bias=-9.0, banks=("P0",))
-        mm(512, ("EQ0", "EQ1", "WT"), "P0",
-           *[(P0[:, 16 * j:16 * j + 16], T.EQ[:, 128 * j:128 * j + 128], T.rows[:, 900:916], True, True) for j in range(8)])
-        tt(T.DM[:], P0[:, 0:128], T.MK2[:], OP.mult, 128, ("MK2",), ("DM",), banks=("P0",), x=1.0)
-        mm(64, ("DM", "R8"), "P0", (P0[:, 128:136], T.DM[:], T.R8[:], True, True))
-        act(T.dmin[:], P0[:, 128:136], AF.Sign, 8, (), ("dmin",), bias=-1.75, banks=("P0",))
-        tt(T["nwi%d" % d][:], T.dmin[:], pf[:, 48:56], OP.mult, 8, ("dmin", "iw"), ("nwi%d" % d,))
-
-    def voff(t):
-        d = t % 2
-        if t == 0:
-            copy(T.vi[:], T.sw0[:, 15::16], 8, ("sw0",), ("vi",))
-        else:
-            ts(T.vi[:], T["sw%d" % d][:, 15::16], pf[:, 63:64], OP.add, 8, ("sw%d" % d, "A"), ("vi",))
-        ts(T.vm[:, 8 * d:8 * d + 8], T.vi[:], 1023, OP.bitwise_and, 8, ("vi",), ("vm%d" % d,))
-        copy(T["goff%d" % d][:], T.vm[:, 8 * d:8 * d + 8], 8, ("vm%d" % d,), ("goff%d" % d,))
-
-    def soff(t):
-        d = t % 2
-        tt(T.so[:], T.vm[:, 8 * d:8 * d + 8], T["nwi%d" % d][:], OP.max, 8, ("vm%d" % d, "nwi%d" % d), ("so",))
-        copy(T["soff%d" % d][:], T.so[:], 8, ("so",), ("soff%d" % d,))
+                    calls.append((PD[:, 256 * j + 128 * i:256 * j + 128 * i + 128], bx, bx, True, True))
+                mm("BD BE", "PD", calls, grp="gdup", hard=bool(j))
+            act(T.EQ[:, 512 * h:512 * h + 512], PD[:], AF.Relu, "", "EQ%d" % h, bias=-15.0, bank="PD")
+        mm("EQ0 EQ1 WT", "PD", [(PD[:, 16 * j:16 * j + 16], T.EQ[:, 128 * j:128 * j + 128], WT, True, True) for j in range(8)])
+        tt(T.DM[:], PD[:, 0:128], T.MK2[:], OP.mult, "MK2", "DM", bank="PD")
+        mm("DM R8 ONES rowN", "PD", acc(PD[:, 128:136], (one1, rowN), (T.DM[:], R8)))
+        tt(T.nwi[:], PD[:, 128:136], T.iw[:], OP.min, "iw", "nwi", bank="PD")
+        tt(T.so[:], T["vm%d" % d][:, 0:8], T.nwi[:], OP.max, "nwi vm%d" % d, "so")
+        copy(T["sf%d" % d][:], T.so[:], "so", "sf%d" % d)
+        if t <= NST - 3:
+            act(T["Bu%d" % d][:], T.BT[:].indirect(T["go%d" % d][:, 8:16]), AF.Copy, "BT " + gk, "Bu%d" % d, x=GATH)
 
     def main(t):
         d = t % 2
         z, k = zap(t), zk(t)
         last = t == NST - 1
-        go, gk = T["goff%d" % d][:, 0:8], "goff%d" % d
+        go, gk = T["go%d" % d][:, 0:8], "go%d" % d
         X, xk = T["X%d" % d], "X%d" % d
         win = T.BK[:, 0:1024]
-        qb = {"bias": 129.5 + 2.0 ** -14, "scale": 1.0 / 4096}
         if t == 0:
-            copy(T.bi[:], T.BKI[:].indirect(go), 128, ("BKI", gk), ("bi",), x=1.6)
-            copy(T.nb[:], T.bi[:], 128, ("bi",), ("nb",))
-            act(T.qt[:], T.nb[:], AF.Identity, 128, ("nb",), ("qt",), **qb)
-            copy(T.BK[:, 0:1024], T.BKI[:], 1024, ("BKI",), ("BK",))
+            copy(T.bi[:], T.BKI[:].indirect(go), "BKI " + gk, "bi", x=GATH)
+            copy(win, T.BKI[:], "BKI", "BK")
         else:
-            copy(T.bi[:], win.indirect(go), 128, ("BK", gk), ("bi",), x=1.6)
-            act(T.qt[:], win.indirect(go), AF.Identity, 128, ("BK", gk), ("qt",), x=1.6, **qb)
-        ts(T.bm[:], T.bi[:], 4095, OP.bitwise_and, 128, ("bi",), ("bm",))
-        copy(T.b16[:], T.bm[:], 128, ("bm",), ("b16",))
-        act(T.Fs[:], T.qt[:], AF.Sign, 128, ("qt",), ("Fs",), bias=-(131.5 + t))
-        for c in range(8):
-            off = T.b16[:, 16 * c:16 * c + 16]
-            out = X[:, XS * c + 1:XS * c + 257]
-            if c < 4:
-                tt(out, T.G[:].indirect(off), T["zr%d" % d][:, 256 * c:256 * c + 256], OP.subtract, 256,
-                   ("G", "b16", "zr%d" % d) + tuple("zq%d%d" % (d, j) for j in range(3)), (xk + str(c),), x=1.6)
-            else:
-                act(out, T.G[:].indirect(off), AF.Copy, 256, ("G", "b16"), (xk + str(c),), x=1.6)
-        mm(256, ("qt", "I16", "ONES", "rowA"), "P7", (P7[:, 128:256], one1, T.rows[0:1, 0:128], True, False),
-           (P7[:, 128:256], T.qt[:], T.I16[:], False, True))
-        mm(384, ("qt", "nI16", "ONES", "rowB", "rowR"), "P7", (P7[:, 256:384], one1, T.rows[0:1, 128:256], True, False),
-           (P7[:, 256:384], one1, T.rows[0:1, 512:640], False, False), (P7[:, 256:384], T.qt[:], T.nI16[:], False, True))
-        if True:
-            mm(64, ("Fs", "R8"), "P7", (P7[:, 384:392], T.Fs[:], T.R8[:], True, True))
-        act(T.ivm[:], T.IM[:, 0:1024].indirect(go), AF.Identity, 128, ("IM", gk), ("ivm",), bias=-1.0, x=1.6)
-        mm(256, (k, "ivm", "I", "nI"), "P7", (P7[:, 0:128], T.I[:], z, True, False), (P7[:, 0:128], T.nI[:], T.ivm[:], False, True))
-        act(T.Sg[:], P7[:, 0:128], AF.Sign, 128, (), ("Sg",), bias=-1.5, banks=("P7",))
-        mm(256, ("Fs", "KF", "rowR", "ONES"), "P5", (P5[:, 0:128], one1, T.rows[0:1, 512:640], True, False),
-           (P5[:, 0:128], T.Fs[:], T.KF[:], False, False), grp=("gkey",))
-        def dist(e):
-            lo, hi = DIST[e]
-            if hi > lo:
-                mm(16 * max(hi - lo, 8), ["AB%d%d" % (i, j) for i in range(lo // 32, hi // 32) for j in range(2)] + ["G16"], "P5",
-                   *[(P5[lo:hi, kk:128:16], T.AB[:, 16 * lo + kk:16 * hi:16], T.G16[:], False, kk == 15) for kk in range(16)],
-                   grp=("gkey",))
+            copy(T.bi[:], win.indirect(go), "BK " + gk, "bi", x=GATH)
+        ts(T.bm[:], T.bi[:], 4095, OP.bitwise_and, "bi", "bm")
+        copy(T.b16[:], T.bm[:], "bm", "b16")
+        act(T.qt[:], win.indirect(go), AF.Identity, "BK " + gk, "qt", bias=129.5 + 2.0 ** -14, scale=1.0 / 4096, x=GATH)
+        nv = ND // 32
         for e in range(4):
-            if e < 2:
-                for c in (2 * e, 2 * e + 1):
-                    act(T.AB[:, 256 * c:256 * c + 256], X[:, XS * c + 1:XS * c + 257], AF.Abs, 256, (xk + str(c),), ("AB%d%d" % (e, c % 2),))
-                dist(e)
-                continue
-            bank = "P%d" % (1 + e % 2)
-            pb = T[bank]
-            zt = T["zT%d" % d][32 * e:32 * e + 32, :]
-            mm(512, ("zT%d" % d, "SEL"), bank, (pb[:], zt, T.SEL[32 * e:32 * e + 32, :], True, False), grp=("g" + bank,))
-            for j in range(2):
-                c = 2 * e + j
-                mm(256, (xk + str(c), "I"), bank, (pb[:, 256 * j:256 * j + 256], T.I[:], X[:, XS * c + 1:XS * c + 257], False, j == 1), grp=("g" + bank,))
-            act(T.AB[:, 512 * e:512 * e + 512], pb[:], AF.Abs, 512, (), ("AB%d0" % e, "AB%d1" % e), banks=(bank,))
-            dist(e)
+            off, out = T.b16[:, 32 * e:32 * e + 32], X[:, 512 * e:512 * e + 512]
+            if e < nv:
+                tt(out, T.G[:].indirect(off), T["zr%d" % d][:, 512 * e:512 * e + 512], OP.subtract,
+                   "G b16 " + " ".join("zr%d%d%d" % (d, e, j) for j in range(4)), xk + str(e), x=GATH)
+                ts(T.AB[:, 512 * e:512 * e + 512], out, 0.0, OP.max, xk + str(e), "AB%d" % e, s2=2.0, o2=OP.mult, x=0.5)
+            else:
+                act(out, T.G[:].indirect(off), AF.Copy, "G b16", xk + str(e), x=GATH)
+        act(T.Fs[:], T.qt[:], AF.Sign, "qt", "Fs", bias=-(131.5 + t))
+        key = PK[:, 0:128]
+        mm("Fs KF row1 ONES", "PK", acc(key, (one2, T.ROWS[0:2, 0:128]), (T.Fs[:], T.KF[:]), stop=False), grp="gkey")
+        mm("qt nI16 row2 ONES", "PQ", acc(PQ[:, 128:256], (one2, T.ROWS[0:2, 128:256]), (T.qt[:], T.nI16[:])))
+
+        def dist(src, lo, hi, rhs, r, stop):
+            mm(r, "PK", [(PK[lo:hi, kk:128:16], src[:, 16 * lo + kk:16 * hi:16], rhs, False, stop and kk == 15) for kk in range(16)], grp="gkey")
+
+        def scalar_lanes(e):
+            bank = "PA" if e % 2 else "PB"
+            mm("zT%d SEL%d" % (d, e), bank, acc(T[bank][:], (T["zT%d" % d][32 * e:32 * e + 32, :], sel(e, 32 * e, 32 * e + 32)), stop=False), grp="g" + bank)
+            mm(xk + str(e) + " I", bank, acc(T[bank][:], (I, X[:, 512 * e:512 * e + 512]), start=False), grp="g" + bank)
+            act(T.AB[:, 512 * e:512 * e + 512], T[bank][:], AF.Abs, "", "AB%d" % e, bank=bank)
+            dist(T.AB, 32 * e, 32 * e + 32, T.G16[:], "G16 AB%d" % e, True)
+        dist(X, 0, ND, T.nG16[:], "nG16 " + " ".join(xk + str(e) for e in range(nv)), False)
+        scalar_lanes(nv)
+        dist(T.AB, 0, ND, T.G16[:], "G16 " + " ".join("AB%d" % e for e in range(nv)), True)
+        for e in range(nv + 1, 4):
+            scalar_lanes(e)
+        pcopy(T.G[:, t::32], z, k, "G")
+        if last:
+            dma(T.ygeno[:], T.G[:], "G", "yg", 7000)
         dups(t)
-        soff(t)
-        pcopy(T.G[:, t::32], z, (k,), ("G",))
-        mm(192, ("Sg", "KC", "R8"), "P7", (P7[:, 0:128], T.Sg[:], T.KC[:], True, True), (P7[:, 392:400], T.Sg[:], T.R8[:], True, True))
-        act(T.cap[:], P7[:, 0:128], AF.Relu, 128, (), ("cap",), banks=("P7",))
-        ts(T.sk[:], P7[:, 392:400], 1.0, OP.is_ge, 8, (), ("sk",), banks=("P7",))
-        tt(P7[:, 128:256], P7[:, 128:256], T.cap[:], OP.min, 128, ("cap",), ("q16s",), banks=("P7",), x=1.0)
-        ts(T.hm[:], P7[:, 384:392], -12.0, OP.min, 8, (), ("hm",), s2=16.0, o2=OP.add, banks=("P7",))
-        tt(T.hv[:], T.hm[:], T.sk[:], OP.mult, 8, ("hm", "sk"), ("hv",))
-        if last:
-            load(T.ygeno[:], T.G[:], ("yg",), 7000, r=("G",))
-        else:
-            mm(64, ("hv", "HALF"), "P7", (P7[:, 400:408], T.HALF[:], T.hv[:], True, True))
-            op("v", dv(8), (), ("A",), lambda: V.tensor_reduce(pf[:, 63:64], P7[:, 400:408], AxisListType.X, OP.add), banks=("P7",))
+        act(T.ivm[:], T.IM[:, 0:1024].indirect(go), AF.Identity, "IM " + gk, "ivm", bias=-1.0, x=GATH)
+        mm(k + " ivm I nI", "PS", acc(PS[:, 0:128], (I, z), (nI, T.ivm[:])))
+        act(T.Sg[:], PS[:, 0:128], AF.Sign, "", "Sg", bias=-1.5, bank="PS")
+        mm("Sg R8", "PS", acc(PS[0:8, 128:256], (R8, T.Sg[:])))
+        act(T.sk[0:8, :], PS[0:8, 128:256], AF.Sign, "", "sk", bias=-1.0, bank="PS")
+        mm("Fs sk L10 L11 L2", "PS", acc(PS[0:16, 256:384], (L1, T.Fs[:]), (L2, T.sk[0:8, :])))
+        act(T.H[0:16, :], PS[0:16, 256:384], AF.Relu, "f17", "H hc", bias=pf[0:16, 17:18], bank="PS", accum=None if last else T.hc[0:16, 0:1])
+        if not last:
+            mm("hc AL", "PS", acc(PS[:, 384:385], (T.AL[0:16, :], T.hc[0:16, 0:1])), x=4)
             prep(t + 1)
-            voff(t + 1)
-        key = P5[:, 0:128]
-        RS = T.RS[:, 0:128]
-        scan(T.ab[:, 0:128], RS, key, OP.mult, OP.max, 128, ("RSa",), ("a",), banks=("P5",))
-        tt(T.c[:, 1:128], T.ab[:, 0:127], P5[:, 1:128], OP.min, 128, ("a",), ("c",), banks=("P5",), x=1.0)
-        scan(T.ab[:, 128:256], T.c[:], RS, OP.max, OP.mult, 128, ("c", "RSa"), ("b",))
-        ts(T.h12[:, 0::16], T.ab[:, 15::16], THR, OP.max, 16, ("a", "b"), ("h12",))
-        scan(T.hb12[:], T.RS[:], T.h12[:], OP.mult, OP.add, 256, ("h12", "RS"), ("hb12",))
-        tt(T.W[:], key, T.hb12[:, 128:256], OP.is_ge, 128, ("hb12",), ("W",), banks=("P5",), x=1.0)
-        tt(T.E1[:], key, T.hb12[:, 0:128], OP.is_ge, 128, ("hb12",), ("E1",), banks=("P5",), x=1.0)
-        tt(T.wq[:], P7[:, 128:256], T.W[:], OP.mult, 128, ("W", "q16s"), ("wq",), banks=("P7",), x=1.0)
-        tt(T.e2[:], P7[:, 256:384], T.wq[:], OP.add, 128, ("wq",), ("e2",), banks=("P7",), x=1.0)
-        scan(T.s3[:], RS, T.e2[:], OP.mult, OP.max, 128, ("e2", "RSa"), ("s3",))
-        copy(T.h3[:, 0::16], T.s3[:, 15::16], 8, ("s3",), ("h3",))
-        scan(P5[:, 384:512], RS, T.h3[:], OP.mult, OP.add, 128, ("h3", "RSa"), ("hb3",), banks=("P5",))
-        tt(T.S[:], T.e2[:], P5[:, 384:512], OP.is_equal, 128, ("e2", "hb3"), ("S",), banks=("P5",), x=1.0)
-        mm(128, ("wq", "nI256"), "P7", (P7[:, 0:128], T.wq[:], T.nI256[:], True, True))
-        calls = [(P5[:, 256:384], T.S[:], T.D32[:], True, False)]
-        if t:
-            calls.append((P5[:, 256:384], T.S[:], cst("TI", t), False, False))
-        calls.append((P5[:, 256:384], T.S[:], cst("HI", t), False, True))
-        tt(T.t1[:], T.bi[:], P7[:, 0:128], OP.add, 128, ("bi",), ("t1",), banks=("P7",), x=1.0)
-        mm(384, ("S", "D32", "HI%d" % t) + (("TI%d" % t,) if t else ()), "P5", *calls)
-        tt(T.nb[:], T.t1[:], P5[:, 256:384], OP.max, 128, ("t1",), ("nb",), banks=("P5",), x=1.0)
-        so, sk_ = T["soff%d" % d][:, 0:8], "soff%d" % d
-        copy(T.BK[:, 0:1152].indirect(so), T.nb[:], 128, ("nb", sk_), ("BK",), x=3.5)
+            hosts(t + 1)
+        mm("qt sk nI16 BO8", "PQ", acc(PQ[:, 0:128], (T.qt[:], T.nI16[:]), (T.sk[0:8, :], T.BO8[0:8, :])))
+        act(PQ[:, 0:128], PQ[:, 0:128], AF.Relu, "", "", bias=-2336.0, scale=-1.0, bank="PQ")
+        ab, hb = T.ab, T.hb
+        scan(ab[:, 0:128], RS, key, 0.0, OP.mult, OP.max, "RS", "a", bank="PK")
+        tt(T.c[:, 1:128], ab[:, 0:127], PK[:, 1:128], OP.min, "a", "c", bank="PK")
+        scan(ab[:, 144:272], T.c[:], RS, 0.0, OP.max, OP.mult, "c RS", "b")
+        scan(hb[:], T.THR[:], ab[:, 15:287], BIG, OP.min, OP.max, "a b abp THR THR0 THR144", "hb")
+        tt(T.W[:], key, hb[:, 144:272], OP.is_ge, "hb", "W", bank="PK")
+        tt(T.E1[:], key, hb[:, 0:128], OP.is_ge, "hb", "E1", bank="PK")
+        tt(T.wq[:], PQ[:, 0:128], T.W[:], OP.mult, "W", "wq", bank="PQ")
+        tt(T.e2[:], PQ[:, 128:256], T.wq[:], OP.add, "wq", "e2", bank="PQ")
+        scan(T.s3[:, 0:128], RS, T.e2[:], 0.0, OP.mult, OP.max, "e2 RS", "s3")
+        scan(PK[:, 128:256], RS, T.s3[:, 15:143], 0.0, OP.mult, OP.max, "s3 s3p RS", "hb3", bank="PK")
+        tt(T.S[:], T.e2[:], PK[:, 128:256], OP.is_equal, "e2 hb3", "S", bank="PK")
+        mm("wq nI256", "PQ", acc(PQ[:, 256:384], (T.wq[:], T.nI256[:])))
+        tt(T.t1[:], T.bi[:], PQ[:, 256:384], OP.add, "bi", "t1", bank="PQ")
+        mm("S D4 KF", "PK", acc(PK[:, 256:384], (T.S[:], T.D4[:]), (T.S[:], T.KF[:])))
+        act(T.ns[:], PK[:, 256:384], AF.Identity, "", "ns", scale=8.0, bias=float(t + 4096 * (8 + t) - 65536), bank="PK")
+        so, sk_ = T["sf%d" % d][:], "sf%d" % d
+        tt(T.BK[:].indirect(so), T.t1[:], T.ns[:], OP.max, "t1 ns " + sk_, "BK", x=SCAT)
         if last:
-            load(T.ybank[:], T.BK[:, 0:1024], ("yb",), 4000, r=("BK",))
-        mm(256, ("W", "E1", "I"), "P3", (P3[:, 0:128], T.E1[:], T.I[:], True, True), (P3[:, 128:256], T.W[:], T.I[:], True, True))
-        act(T.WE[:], P3[:, 0:256], AF.Copy, 256, (), ("WE",), banks=("P3",))
-        mm(384, ("WE", "Kc", "Kn"), "P3", (P3[:, 256:384], T.WE[:, 0:128], T.Kc[:], True, True),
-           (P3[:, 384:512], T.WE[:, 128:256], T.Kc[:], True, False), (P3[:, 384:512], T.WE[:, 0:128], T.Kn[:], False, True))
-        tt(T.L[:], P3[:, 256:512], T.MK[:], OP.mult, 256, ("MK",), ("L",), banks=("P3",), x=1.0)
-        mm(256, ("L", "R8", "ONES", "rowX", "rowY"), "P3", (P3[:, 0:16], one1, T.rows[0:1, 640:656], True, False),
-           (P3[:, 0:16], one1, T.rows[0:1, 656:672], False, False),
-           (P3[:, 0:8], T.L[:, 0:128], T.R8[:], False, False), (P3[:, 8:16], T.L[:, 128:256], T.R8[:], False, True))
-        copy(T.oXA[:], P3[:, 0:16], 16, (), ("oXA",), banks=("P3",))
-        act(T.A12[:], X[:].indirect(T.oXA[:, 0:16]), AF.Copy, 256, ["oXA", "Xs%d" % d, "Xt%d" % d] + [xk + str(c) for c in range(8)], ("A12",), x=1.6)
-        mm(384, ("A12", k, "I", "nI"), "P4", (P4[:, 0:256], T.I[:], T.A12[:], True, False),
-           (P4[:, 64:128], T.nI[:], z[:, 64:128], False, False), (P4[:, 192:256], T.nI[:], z[:, 64:128], False, True))
-        mm(256, ("A12", "I", "nI"), "P4", (P4[:, 256:384], T.I[:], T.A12[:, 128:256], True, False),
-           (P4[:, 256:384], T.nI[:], T.A12[:, 0:128], False, True))
-        act(T.Ps[:], P4[:, 0:384], AF.Sign, 384, (), ("Ps",), bias=-0.5, banks=("P4",))
-        act(T.Ns[:], P4[:, 0:384], AF.Sign, 384, (), ("Ns",), bias=-0.5, scale=-1.0, banks=("P4",))
+            dma(T.ybank[:], win, "BK", "yb", 4000)
+        mm("W E1 I nI", "PW", acc(PW[:, 0:128], (T.E1[:], I)) + acc(PW[:, 128:256], (T.W[:], I), (T.E1[:], nI)))
+        act(T.WE[:], PW[:, 0:256], AF.Copy, "", "WE", bank="PW")
+        mm("WE KB ONES rowC", "PW", acc(PW[:, 256:272], (one1, rowC), *[(T.KB[:, 15 - j:143 - j], T.WE[:, j::16]) for j in range(16)]))
+        ts(T.oX[:], PW[:, 256:272], col(16), OP.add, "f16", "oX", bank="PW")
+        D12 = T.D12
+        tt(D12[:], X[:].indirect(T.oX[:]), T["zz%d" % d][:], OP.subtract,
+           "oX zz%d0 zz%d1 " % (d, d) + " ".join(xk + str(e) for e in range(4)), "D12", x=GATH)
+        d1, d2 = D12[:, 0:128], D12[:, 128:256]
+        mm("D12 I nI", "PW", acc(PW[:, 0:128], (I, d2), (nI, d1)) + acc(PW[:, 128:256], (I, d1), (nI, d2)))
+        ts(T.P12[:], D12[:], 0.0, OP.is_gt, "D12", "P12", s2=0.5, o2=OP.subtract, x=0.5)
+        ts(T.N12[:], D12[:], 0.0, OP.is_lt, "D12", "N12", s2=0.5, o2=OP.subtract, x=0.5)
+        act(T.S21[:], PW[:, 0:256], AF.Sign, "", "S21", bias=-0.5, bank="PW")
+        cnt = PW[0:56, 256:384]
 
-        def cnt(j, buf, i, first=False, last_=False):
-            return (P4[0:48, 384:512], T.SM[:, 72 - 8 * j:120 - 8 * j], buf[:, 128 * i:128 * i + 128], first, last_)
-        mm(384, ("Ps", "RB"), "P4", cnt(0, T.Ps, 0, True), cnt(3, T.Ps, 1), cnt(4, T.Ps, 2), grp=("gcnt",))
-        mm(384, ("Ns", "RB"), "P4", cnt(1, T.Ns, 0), cnt(2, T.Ns, 1), cnt(5, T.Ns, 2, False, True), grp=("gcnt",))
-        act(T.B[0:48, :], P4[0:48, 384:512], AF.Sign, 128, (), ("B",), bias=-1.0, banks=("P4",))
-        mm(192, ("B", "M10", "M11", "M12", "M13", "hv", "I"), "P3", (P3[0:32, 0:128], T.SM[0:48, 0:32], T.B[0:48, :], True, True),
-           (P3[32:40, 0:128], T.hv[:], T.I[:], True, True))
-        act(T.XT[0:40, :], P3[0:40, 0:128], AF.Sign, 128, (), ("XT",), bias=-1.0, banks=("P3",))
-        mm(256, ("XT", "CO1", "CO2"), "P0", (P0[:, 0:128], T.CO1[0:40, :], T.XT[0:40, :], True, True),
-           (P0[:, 128:256], T.CO2[0:40, :], T.XT[0:40, :], True, True))
-        bt = "BT%d" % d
-        if t <= NST - 3:
-            tt(T.C[:], P0[:, 0:256], T[bt][:], OP.is_equal, 256, (bt,), ("C",), banks=("P0",), x=1.0)
-            tt(T.CD[:], T.C[:], P4[:, 0:256], OP.mult, 256, ("C",), ("CD",), banks=("P4",), x=1.0)
-        act(T.F[:], P0[:, 0:256], AF.Relu, 256, (), ("F",), scale=-1.0, banks=("P0",))
-        tt(T.FD[:], T.F[:], P4[:, 0:256], OP.mult, 256, ("F",), ("FD",), banks=("P4",), x=1.0)
-        mm(384, ("FD", k, "I"), "P0", (P0[:, 256:384], T.I[:], z, True, False), (P0[:, 256:384], T.I[:], T.FD[:, 0:128], False, False),
-           (P0[:, 256:384], T.I[:], T.FD[:, 128:256], False, True))
-        tt(T.nim[:], T.ivm[:], P0[:, 256:384], OP.max, 128, ("ivm",), ("nim",), banks=("P0",), x=1.0)
-        copy(T.IM[:, 0:1152].indirect(so), T.nim[:], 128, ("nim", sk_), ("IM",), x=3.5)
+        def row(j, buf, i):
+            return (T.SM[:, 48 - 8 * j:104 - 8 * j], buf[:, 128 * i:128 * i + 128])
+        mm("H GM0 GM1 GM2 GM3 P12 SM", "PW", acc(cnt, (GM, T.H[0:16, :]), row(0, T.P12, 0), row(2, T.P12, 1), stop=False), grp="gcnt")
+        mm("N12 SM", "PW", acc(cnt, row(1, T.N12, 0), row(4, T.N12, 1), start=False, stop=False), grp="gcnt")
+        mm("S21 SM", "PW", acc(cnt, row(3, T.S21, 0), row(5, T.S21, 1), start=False), grp="gcnt")
+        act(T.B[0:56, :], cnt, AF.Sign, "", "B", bias=-0.5, bank="PW")
+        mm("B M10 M11 M12 M13 M14", "PW", acc(PW[0:40, 384:512], (M1, T.B[0:56, :])))
+        act(T.XT[0:40, :], PW[0:40, 384:512], AF.Sign, "", "XT", bias=-5.0, bank="PW")
+        mm("XT CO0 CO1 CO2 CO3", "PR", [(PR[:, 128 * j:128 * j + 128], T.CO[0:40, 128 * j:128 * j + 128], T.XT[0:40, :], True, True) for j in range(4)])
+        tt(T.TD[:], PR[:, 0:256], D12[:], OP.mult, "D12", "TD", bank="PR")
+        tt(T.FD[:], PR[:, 256:512], T.TD[:], OP.mult, "TD", "FD", bank="PR")
+        half = [(T.hI[:], T.FD[:, 0:128]), (T.hI[:], T.FD[:, 128:256])]
+        cross = t <= NST - 3
+        if cross:
+            bu = T["Bu%d" % d][:]
+            mm(k + " I nREP TD Bu%d" % d, "PW", acc(PW[:, 0:128], (I, z), (T.nREP[:], bu), (I, T.TD[:, 0:128]), (I, T.TD[:, 128:256]), stop=False), grp="gm")
+            mm(k + " I nI hI REP FD Bu%d" % d, "PW", acc(PW[:, 0:128], (nI, T.FD[:, 0:128]), (nI, T.FD[:, 128:256]), start=False)
+               + acc(PW[:, 128:256], (I, z), (T.REP[:], bu), *half), grp="gm")
+            cr = T.CR[:, 256 * t:256 * t + 256]
+            act(cr, PW[:, 0:256], AF.Identity, "", "CR%d" % t, bias=-32.0, bank="PW")
+            send([cr[:, 0:128], cr[:, 128:256]], "CR%d" % t, 2, t + 2)
+        mm(k + " I nI hI ivm FD", "PR", acc(PR[:, 0:128], (I, z), (nI, T.ivm[:]), *half))
+        act(T.r[:], PR[:, 0:128], AF.Relu, "", "r", bank="PR")
+        tt(T.IM[:].indirect(so), T.ivm[:], T.r[:], OP.add, "ivm r " + sk_, "IM", x=SCAT)
         if last:
-            load(T.yimm[:], T.IM[:, 0:1024], ("yi",), 3500, r=("IM",))
-        if t <= NST - 3:
-            mm(384, ("CD", k, "I"), "P3", (P3[:, 256:384], T.I[:], z, True, False), (P3[:, 256:384], T.I[:], T.CD[:, 0:128], False, False),
-               (P3[:, 256:384], T.I[:], T.CD[:, 128:256], False, True))
-            cr = "CR%d" % t
-            act(cst("CR", t), P3[:, 256:384], AF.Copy, 128, (), (cr,), banks=("P3",))
-            send(cst("CR", t), cr, cores[(rank + 2) % nr], t + 2)
+            dma(T.yimm[:], T.IM[:, 0:1024], "IM", "yi", 3000)
 
-    send(T.ZB[:, 128:256], "ZB", cores[(rank + 1) % nr], 1)
+    send([T.ZB[:, 128:256]], "ZB", 1, 1)
     prep(0)
-    voff(0)
+    hosts(0)
     for t in range(NST):
         main(t)
     return ops
@@ -492,34 +459,36 @@ def build(g, T, topo, core):
 
 def depend(ops):
     lw, rd, bank, rdy, prev = {}, {}, {}, [], []
-    lastq = {}
+    lastdma = None
     for i, o in enumerate(ops):
         need, order = set(), set()
         for k in o["r"]:
             if k in lw:
-                need |= lw[k]
+                need.add(lw[k])
             rd.setdefault(k, []).append(i)
         for k in o["w"]:
             if k in lw:
-                need |= lw[k]
+                need.add(lw[k])
             need |= set(rd.get(k, ()))
         for k in o["w"]:
-            lw[k] = {i}
+            lw[k] = i
             rd[k] = []
-        for k in o["b"]:
-            h = bank.setdefault(k, [None, set(), set()])
+        if o["b"]:
+            h = bank.setdefault(o["b"], [None, set(), set(), None])
             if h[0] != o["q"]:
                 h[0], h[1], h[2] = o["q"], h[2], set()
+            elif o["q"] == "t":
+                order.add(h[3])
             need |= h[1]
             h[2].add(i)
+            h[3] = i
         if o["q"] == "s":
-            if o["q"] in lastq:
-                order.add(lastq[o["q"]])
-            lastq[o["q"]] = i
+            if lastdma is not None:
+                order.add(lastdma)
+            lastdma = i
         need.discard(i)
-        order.discard(i)
         rdy.append(need)
-        prev.append(order)
+        prev.append(order - need)
     return rdy, prev
 
 
@@ -565,7 +534,8 @@ def schedule(q, dur, nxt, cnt, key):
     return max(fin), seq, start, fin
 
 
-TRIES = 1500
+TRIES = 300
+WAKE = 60
 
 
 def improve(ops, need, order):
@@ -575,12 +545,15 @@ def improve(ops, need, order):
     nxt, prv = [[] for _ in range(n)], [[] for _ in range(n)]
     for i in range(n):
         for j in sorted(need[i] | order[i]):
-            lag = (40 if q[i] == q[j] else 80) if j in need[i] else 60 - dur[j]
+            if j in order[i]:
+                lag = 60 - dur[j] if q[i] == "s" else 0
+            else:
+                lag = 0 if q[i] == q[j] == "t" and not ops[i]["hard"] else WAKE
             nxt[j].append((i, lag))
             prv[i].append((j, lag))
     cur = [0.0] * n
     for i in range(n - 1, -1, -1):
-        cur[i] = dur[i] + max([cur[j] + 40 for j, _ in nxt[i]], default=0.0)
+        cur[i] = dur[i] + max([cur[j] + lag for j, lag in nxt[i]], default=0.0)
     best = None
     for _ in range(TRIES):
         r = schedule(q, dur, nxt, [len(x) for x in prv], cur)
@@ -617,7 +590,7 @@ def rank_program(g, core, T, topo):
         o = ops[i]
         q = o["q"]
         kn = known.setdefault(q, {}) if q != "n" else {}
-        for j in sorted(need[i], key=lambda x: -x):
+        for j in sorted(need[i], key=lambda x: -done[x][1]):
             s, v = done[j]
             if q == "t" and ops[j]["q"] == "t" and not o["hard"]:
                 continue

@@ -4,6 +4,10 @@ from concourse.mybir import AluOpType as OP, AxisListType, ActivationFunctionTyp
 
 NST = 5
 ND = 64
+NR = 64
+DIST = ((0, 128),)
+BT_ACT = ()
+SG_DVE = (1, 2, 3, 4)
 TW = 1280
 BIG = 2.0 ** 20
 
@@ -15,22 +19,21 @@ def _bufs(names, cols, dtype, where="sbuf"):
         SCRATCH[n] = (where, [128, cols], dtype)
 
 
-_bufs("G", 4096, "bfloat16")
+_bufs("G G2", 4096, "bfloat16")
 _bufs("X0 X1 AB", 2048, "bfloat16")
-_bufs("BKI bti", 1024, "int32")
+_bufs("BKI", 1024, "int32")
 _bufs("BK", TW, "float32")
 _bufs("IM", TW, "bfloat16")
 _bufs("BT EQ", 1024, "bfloat16")
 _bufs("zr0 zr1", 16 * ND, "bfloat16")
 _bufs("zr4", 4 * ND, "bfloat16")
 _bufs("CO", 512, "bfloat16")
-_bufs("SEL", 2048 - 16 * ND, "bfloat16")
 _bufs("CR", 768, "bfloat16")
 _bufs("THR", 272, "bfloat16")
-_bufs("ZB ROWS WE D12 P12 N12 S21 TD FD zz0 zz1", 256, "bfloat16")
+_bufs("ZB WE D12 P12 N12 S21 TD FD zz0 zz1", 256, "bfloat16")
 _bufs("KB", 144, "bfloat16")
 _bufs("GM", 56, "bfloat16")
-_bufs("Z1 Z2 Z3 Z4 ONES I nI hI KF D4 nI16 nI256 BO MK MK2 RS D8W BO8 REP nREP WH WL SM sm zT0 zT1 BD BE Bu0 Bu1 DM "
+_bufs("Z1 Z2 Z3 Z4 ONES I nI hI KF D4 nI16 nI256 BO MK MK2 RS D8W BO8 REP nREP WH WL SM sm ROWS BD BE Bu0 Bu1 DM "
       "qt Fs ivm Sg sk H W E1 wq S B XT r", 128, "bfloat16")
 _bufs("R8 G16 nG16", 8, "bfloat16")
 _bufs("ab", 288, "float32")
@@ -40,7 +43,6 @@ _bufs("c e2 t1 ns mU AL", 128, "float32")
 _bufs("pf tw", 64, "float32")
 _bufs("R8f iw y sq nwi hc", 8, "float32")
 _bufs("cg cm c8 bi bm", 128, "int32")
-_bufs("c7", 56, "int32")
 _bufs("pc vi vm0 vm1", 16, "int32")
 _bufs("WI", 1, "int32")
 _bufs("Ui u so", 8, "int32")
@@ -49,9 +51,13 @@ _bufs("go0 go1 oX", 16, "uint16")
 _bufs("sf0 sf1", 8, "uint16")
 _bufs("PK PQ PA PB PS PW PR PD", 512, "float32", "psum")
 
-SEMAPHORES = ["sv", "sa", "st", "sg", "ls"] + ["dm%d" % i for i in range(8)] + ["rz%d" % t for t in range(1, 5)]
+SEMAPHORES = ["sv", "sa", "st", "sg", "ls"] + ["dm%d" % i for i in range(9)] + ["rz%d" % t for t in range(1, 5)]
 CNT = {"v": "sv", "a": "sa", "t": "st", "g": "sg"}
 CY, GATH, SCAT = 0.83, 1.56, 3.8
+VFIX, AFIX, PCY = 40, 80, 0.42
+DFIX, DKIB = 1500, 2.56
+FIRST, RLAT = 5000, 1700
+WAKE, PLAT = 110, 150
 
 
 def build(g, T, topo, core):
@@ -62,7 +68,7 @@ def build(g, T, topo, core):
         ops.append({"q": q, "dur": dur, "r": reads.split(), "w": writes.split(), "f": fns, "b": bank, "sem": sem, "hard": hard})
 
     def dv(ap, x):
-        return 50 + max(64.0, ap.shape[1] * x) * CY
+        return VFIX + max(64.0, ap.shape[1] * x) * CY
 
     def copy(out, in_, r, w, bank=None, x=1.0):
         op("v", dv(in_, x), r, w, lambda: V.tensor_copy(out, in_), bank=bank)
@@ -86,7 +92,7 @@ def build(g, T, topo, core):
         op("v", dv(ap, 0.5), "", w, lambda: V.memset(ap, val))
 
     def act(out, in_, f, r, w, bias=0.0, scale=1.0, bank=None, x=1.0, accum=None):
-        d = 70 + max(64.0, out.shape[1] * x) * CY
+        d = AFIX + max(64.0, out.shape[1] * x) * CY
         if accum is None:
             op("a", d, r, w, lambda: S.activation(out, in_, f, bias, scale), bank=bank)
         else:
@@ -95,7 +101,7 @@ def build(g, T, topo, core):
     def mm(r, bank, calls, grp="", hard=False, x=1):
         def one(a):
             return lambda: PE.matmul(*a)
-        d = sum(10 + 0.45 * x * max(min(64, a[1].shape[1]), a[2].shape[1]) for a in calls)
+        d = sum(PCY * x * max(min(64, a[1].shape[1]), a[2].shape[1]) for a in calls)
         op("t", d, r, grp, *[one(a) for a in calls], bank=bank, hard=hard)
 
     def acc(out, *terms, start=True, stop=True):
@@ -117,16 +123,16 @@ def build(g, T, topo, core):
 
     nd = [0]
 
-    def dma(out, in_, r, w, dur):
+    def dma(out, in_, r, w, kib):
         s = "dm%d" % nd[0]
         nd[0] += 1
-        op("s", dur, r, w, lambda: g.sync.dma_start(out, in_), sem=(s, 16))
+        op("s", DFIX + kib * DKIB, r, w, lambda: g.sync.dma_start(out, in_), sem=(s, 16))
 
-    dma(T.WI[:], T.wt[:], "", "WI", 1900)
-    dma(T.ZB[:], T.bites[:], "", "ZB", 2200)
-    dma(T.BKI[:], T.bank[:], "", "BKI", 4500)
-    dma(T.G[:], T.geno[:], "", "G", 8000)
-    dma(T.IM[:, 0:1024], T.immun[:], "", "IM", 9000)
+    dma(T.WI[:], T.wt[:], "", "WI", 1)
+    dma(T.ZB[:], T.bites[:], "", "ZB", 64)
+    dma(T.BKI[:], T.bank[:], "", "BKI", 512)
+    dma(T.G[:], T.geno[:], "", "G", 1024)
+    dma(T.IM[:, 0:1024], T.immun[:], "", "IM", 256)
 
     rank = T.rank_of(core)
     cores = list(T.cores)
@@ -147,7 +153,7 @@ def build(g, T, topo, core):
             f = lambda: g.remote_dma_fused([RemoteDMATransfer(dst_ids=[DstId(rid=a[0], pnc=a[1])], dma_engine_mask=m, remote_sem=rs,
                                                               srcs=list(srcs), dsts=[zt[:]], alu_op=2)], local_sem=T.sem.ls)
         op("g", 300, key, "sent%d" % t, f, sem=("ls", len(e)))
-        op("n", 2300, "sent%d" % t, "Z%d" % t, sem=("rz%d" % t, len(engs(cores[(rank - hop) % nr], core))))
+        op("n", FIRST if t == 1 else RLAT, "sent%d" % t, "Z%d" % t, sem=("rz%d" % t, len(engs(cores[(rank - hop) % nr], core))))
 
     pc, pf, tw = T.pc, T.pf, T.tw
 
@@ -157,11 +163,12 @@ def build(g, T, topo, core):
     memset(T.ONES[:], 1.0, "ONES")
     iota(pc[:, 0:1], [[1, 1]], 0, 1, "pI")
     iota(T.cm[:], [[0, 8], [1, 16]], 0, 0, "cm")
-    for j, (s, o) in enumerate(((15, OP.bitwise_and), (7, OP.bitwise_and), (3, OP.logical_shift_right), (16, OP.bitwise_and))):
+    for j, (s, o) in enumerate(((15, OP.bitwise_and), (7, OP.bitwise_and), (3, OP.logical_shift_right), (16, OP.bitwise_and),
+                                (4, OP.logical_shift_right))):
         ts(pc[:, 1 + j:2 + j], pc[:, 0:1], s, o, "pI", "i%d" % j)
-    copy(col(0, 4), pc[:, 1:5], "i0 i1 i2 i3", "fp")
-    select(T.BO[:], T.ONES[:], [[-16, 8], [0, 16]], OP.is_ge, 0, 1, "ONES", "BO")
-    select(T.BO[:], T.BO[:], [[16, 8], [0, 16]], OP.is_ge, 15, -1, "BO", "BO")
+    copy(col(0, 5), pc[:, 1:6], "i0 i1 i2 i3 i4", "fp")
+    iota(T.cg[:], [[1, 8], [0, 16]], 0, 0, "cg")
+    ts(T.BO[:], T.cg[:], col(4), OP.is_equal, "cg fp", "BO")
     R8 = T.R8[:]
     act(R8, T.BO[:, 0::16], AF.Copy, "BO", "R8")
     act(T.R8f[:], T.BO[:, 0::16], AF.Copy, "BO", "R8f")
@@ -176,16 +183,9 @@ def build(g, T, topo, core):
         act(T[name][:], T.I[:], AF.Copy, "I", name, scale=val)
     act(T.G16[:], R8, AF.Copy, "R8", "G16", scale=16.0)
     act(T.nG16[:], R8, AF.Copy, "R8", "nG16", scale=-16.0)
-    memset(T.SEL[:], -1.0, "SEL")
-
-    def sel(e, lo=0, hi=128):
-        return T.SEL[lo:hi, 512 * e - 16 * ND:512 * e - 16 * ND + 512]
-    for e in range(ND // 32, 4):
-        select(sel(e), sel(e), [[-1, 32], [0, 16]], OP.is_equal, -32 * e, 1, "SEL", "SEL%d" % e)
     select(T.RS[:], T.ONES[:], [[0, 8], [1, 16]], OP.is_gt, 0, 0, "ONES", "RS")
-    iota(T.ROWS[0:2, 0:128], [[-32768, 8], [0, 16]], 8192 + 7 * 32768, 0, "row1", "", True)
-    iota(T.ROWS[0:2, 128:256], [[-512, 8], [0, 16]], 2336 + 7 * 512, 0, "row2", "", True)
-    iota(T.ROWS[0:1, :], [[0, 16], [-1, 16]], 15, 0, "row1 row2", "", True)
+    iota(T.ROWS[0:2, :], [[-32768, 8], [0, 16]], 8192 + 7 * 32768, 0, "ROWS", "", True)
+    iota(T.ROWS[0:1, :], [[0, 8], [-1, 16]], 15, 0, "ROWS", "", True)
     memset(T.THR[:], BIG, "THR")
     for o in (0, 144):
         iota(T.THR[:, o:o + 128:16], [[-32768, 8]], 16384 + 7 * 32768, 0, "THR%d" % o, "THR", True)
@@ -197,15 +197,14 @@ def build(g, T, topo, core):
         memset(T["zz%d" % d][:], 0.0, "zz%d" % d)
     iota(T.tw[:, 63:64], [[1, 1]], 0, 4, "p4", cast=True)
     act(T.D4[:], T.I[:], AF.Copy, "I p4", "D4", scale=tw[:, 63:64])
-    memset(tw[:, 0:16], 0.5, "tw0")
-    memset(tw[:, 16:32], 0.0, "tw1")
-    scan(tw[:, 32:48], tw[:, 0:16], tw[:, 16:32], 1024.0, OP.mult, OP.add, "tw0 tw1", "tw2")
-    tt(tw[:, 0:16], tw[:, 32:48], T.MK[:, 0:16], OP.mult, "tw2 MK", "tw0")
-    reduce_(col(10), tw[:, 0:16], "tw0", "f10")
-    iota(T.bti[:], [[1, 1024]], 0, 0, "bti")
-    ts(T.bti[:], T.bti[:], col(10), OP.mult, "bti f10", "bti")
-    ts(T.bti[:], T.bti[:], 512, OP.bitwise_and, "bti", "bti")
-    ts(T.BT[:], T.bti[:], 1.0 / 256, OP.mult, "bti", "BT", s2=-1.0, o2=OP.add)
+    ts(col(48, 10), T.MK[:, 0:10], -2.0, OP.mult, "MK", "flip", s2=1.0, o2=OP.add)
+    memset(T.BT[:, 0:1], -1.0, "BT")
+    for j in range(10):
+        if j in BT_ACT:
+            act(T.BT[:, 1 << j:2 << j], T.BT[:, 0:1 << j], AF.Copy, "BT flip", "BT", scale=col(48 + j))
+        else:
+            ts(T.BT[:, 1 << j:2 << j], T.BT[:, 0:1 << j], col(48 + j), OP.mult, "BT flip", "BT", x=0.5)
+    memset(tw[:, 16:24], 0.0, "tw1")
     ts(col(11), col(3), 1.0 / 16, OP.mult, "fp", "odd")
     ts(col(12), col(3), 0.0, OP.is_equal, "fp", "even")
     memset(tw[:, 48:56], 1.0 / 64, "tw3")
@@ -224,14 +223,12 @@ def build(g, T, topo, core):
     ts(col(16), col(0), 16.0, OP.mult, "fp", "f16")
     memset(T.KB[:], 0.0, "KB")
     act(T.KB[:, 15:143:16], R8, AF.Copy, "R8 fp KB", "KB", scale=col(0))
-    iota(T.cg[:], [[1, 8], [0, 16]], 0, 0, "cg")
-    iota(T.c7[:], [[0, 7], [1, 8]], 0, 0, "c7")
     iota(T.c8[:], [[0, 16], [1, 8]], 0, 0, "c8")
     ts(T.D8W[:], T.cg[:], col(1), OP.is_equal, "cg fp", "D8W")
     ts(col(17), col(2), 0.0, OP.is_equal, "fp", "f17", s2=2.0, o2=OP.mult)
     ts(col(18), col(17), -1.0, OP.add, "f17", "f18")
     D16, L1, L2, GM, M1 = T.sm[:, 40:56], T.sm[:, 56:72], T.sm[0:8, 72:88], T.GM[0:16, :], T.sm[0:56, 88:128]
-    ts(D16, T.c7[:, 0:16], col(1), OP.is_equal, "c7 fp f18", "D16", s2=col(18), o2=OP.mult)
+    ts(D16, T.c8[:, 0:16], col(1), OP.is_equal, "c8 fp f18", "D16", s2=col(18), o2=OP.mult)
     for j in range(2):
         act(T.sm[:, 56 + 8 * j:64 + 8 * j], R8, AF.Copy, "R8", "L1%d" % j, scale=-0.5)
     act(L2, T.sm[0:8, 40:56], AF.Copy, "D16", "L2", scale=-8.0)
@@ -244,7 +241,7 @@ def build(g, T, topo, core):
     act(T.GM[0:16, 32:48], T.sm[0:16, 40:56], AF.Copy, "D16", "GM2", scale=32.0)
     act(T.GM[0:16, 48:56], T.sm[0:16, 40:48], AF.Copy, "D16", "GM3", scale=0.375)
     E = 20
-    ts(col(E, 7), T.c7[:, 0:7], col(2), OP.is_equal, "c7 fp", "E")
+    ts(col(E, 7), T.cm[:, 0:7], col(2), OP.is_equal, "cm fp", "E")
     tt(col(28, 2), col(E, 2), col(E + 2, 2), OP.add, "E", "n01")
     tt(col(30), col(E + 4), col(E + 5), OP.add, "E", "n2")
     ts(col(31), col(E + 6), 4.0, OP.mult, "E", "g4")
@@ -284,8 +281,6 @@ def build(g, T, topo, core):
         tt(T.mU[:], PD[:, 0:128], T.MK[:], OP.mult, "MK", "mU", bank="PD")
         mm("mU R8f", "PD", acc(PD[:, 128:136], (T.mU[:], T.R8f[:])), x=4)
         copy(T.Ui[:], PD[:, 128:136], "", "Ui", bank="PD")
-        mm(k + " I", "PD", acc(PD[ND:128, 256:384], (z[:, ND:128], I)))
-        act(T["zT%d" % d][ND:128, :], PD[ND:128, 256:384], AF.Copy, "", "zT%d" % d, bank="PD")
         ts(T.u[:], T.Ui[:], 4095, OP.bitwise_and, "Ui", "u")
         ts(T.y[:], T.u[:], 1184.0, OP.add, "u", "y")
         tt(T.vi[:, 0:8] if t == 0 else T.sq[:], T.u[:], T.y[:], OP.mult, "u y", "vi" if t == 0 else "sq")
@@ -349,37 +344,45 @@ def build(g, T, topo, core):
             if e < nv:
                 tt(out, T.G[:].indirect(off), T["zr%d" % d][:, 512 * e:512 * e + 512], OP.subtract,
                    "G b16 " + " ".join("zr%d%d%d" % (d, e, j) for j in range(4)), xk + str(e), x=GATH)
-                ts(T.AB[:, 512 * e:512 * e + 512], out, 0.0, OP.max, xk + str(e), "AB%d" % e, s2=2.0, o2=OP.mult, x=0.5)
+                if 32 * e < NR:
+                    ts(T.AB[:, 512 * e:512 * e + 512], out, 0.0, OP.max, xk + str(e), "AB%d" % e, s2=2.0, o2=OP.mult, x=0.5)
+                else:
+                    act(T.AB[:, 512 * e:512 * e + 512], out, AF.Abs, xk + str(e), "AB%d" % e)
             else:
                 act(out, T.G[:].indirect(off), AF.Copy, "G b16", xk + str(e), x=GATH)
         act(T.Fs[:], T.qt[:], AF.Sign, "qt", "Fs", bias=-(131.5 + t))
         key = PK[:, 0:128]
-        mm("Fs KF row1 ONES", "PK", acc(key, (one2, T.ROWS[0:2, 0:128]), (T.Fs[:], T.KF[:]), stop=False), grp="gkey")
-        mm("qt nI16 row2 ONES", "PQ", acc(PQ[:, 128:256], (one2, T.ROWS[0:2, 128:256]), (T.qt[:], T.nI16[:])))
+        mm("Fs KF ROWS ONES", "PK", acc(key, (one2, T.ROWS[0:2, :]), (T.Fs[:], T.KF[:]), stop=False), grp="gkey")
+        mm("qt nI16 ROWS ONES", "PQ", acc(PQ[:, 128:256], (one2, T.ROWS[0:2, :]), (T.qt[:], T.nI16[:])))
 
         def dist(src, lo, hi, rhs, r, stop):
             mm(r, "PK", [(PK[lo:hi, kk:128:16], src[:, 16 * lo + kk:16 * hi:16], rhs, False, stop and kk == 15) for kk in range(16)], grp="gkey")
 
         def scalar_lanes(e):
             bank = "PA" if e % 2 else "PB"
-            mm("zT%d SEL%d" % (d, e), bank, acc(T[bank][:], (T["zT%d" % d][32 * e:32 * e + 32, :], sel(e, 32 * e, 32 * e + 32)), stop=False), grp="g" + bank)
+            mm(k + " nI", bank, [(T[bank][:, kk::16], nI, z[:, 32 * e:32 * e + 32], kk == 0, False) for kk in range(16)], grp="g" + bank)
             mm(xk + str(e) + " I", bank, acc(T[bank][:], (I, X[:, 512 * e:512 * e + 512]), start=False), grp="g" + bank)
             act(T.AB[:, 512 * e:512 * e + 512], T[bank][:], AF.Abs, "", "AB%d" % e, bank=bank)
-            dist(T.AB, 32 * e, 32 * e + 32, T.G16[:], "G16 AB%d" % e, True)
-        dist(X, 0, ND, T.nG16[:], "nG16 " + " ".join(xk + str(e) for e in range(nv)), False)
-        scalar_lanes(nv)
-        dist(T.AB, 0, ND, T.G16[:], "G16 " + " ".join("AB%d" % e for e in range(nv)), True)
-        for e in range(nv + 1, 4):
+        for e in range(nv, 4):
             scalar_lanes(e)
-        pcopy(T.G[:, t::32], z, k, "G")
+        if NR:
+            dist(X, 0, NR, T.nG16[:], "nG16 " + " ".join(xk + str(e) for e in range(NR // 32)), False)
+        for lo, hi in DIST:
+            dist(T.AB, lo, hi, T.G16[:], "G16 " + " ".join("AB%d" % e for e in range(lo // 32, hi // 32)), True)
+        if not last:
+            pcopy(T.G[:, t::32], z, k, "G")
+        pcopy(T.G2[:, t::32], z, k, "G2")
         if last:
-            dma(T.ygeno[:], T.G[:], "G", "yg", 7000)
+            dma(T.ygeno[:], T.G2[:], "G2", "yg", 1024)
         dups(t)
         act(T.ivm[:], T.IM[:, 0:1024].indirect(go), AF.Identity, "IM " + gk, "ivm", bias=-1.0, x=GATH)
-        mm(k + " ivm I nI", "PS", acc(PS[:, 0:128], (I, z), (nI, T.ivm[:])))
-        act(T.Sg[:], PS[:, 0:128], AF.Sign, "", "Sg", bias=-1.5, bank="PS")
+        if t in SG_DVE:
+            tt(T.Sg[:], T.IM[:, 0:1024].indirect(go), z, OP.is_lt, "IM %s %s" % (gk, k), "Sg", x=GATH)
+        else:
+            mm(k + " ivm I nI", "PS", acc(PS[:, 0:128], (I, z), (nI, T.ivm[:])))
+            act(T.Sg[:], PS[:, 0:128], AF.Sign, "", "Sg", bias=-1.5, bank="PS")
         mm("Sg R8", "PS", acc(PS[0:8, 128:256], (R8, T.Sg[:])))
-        act(T.sk[0:8, :], PS[0:8, 128:256], AF.Sign, "", "sk", bias=-1.0, bank="PS")
+        act(T.sk[0:8, :], PS[0:8, 128:256], AF.Sign, "", "sk", bias=-8.5 if t in SG_DVE else -1.0, bank="PS")
         mm("Fs sk L10 L11 L2", "PS", acc(PS[0:16, 256:384], (L1, T.Fs[:]), (L2, T.sk[0:8, :])))
         act(T.H[0:16, :], PS[0:16, 256:384], AF.Relu, "f17", "H hc", bias=pf[0:16, 17:18], bank="PS", accum=None if last else T.hc[0:16, 0:1])
         if not last:
@@ -407,7 +410,7 @@ def build(g, T, topo, core):
         so, sk_ = T["sf%d" % d][:], "sf%d" % d
         tt(T.BK[:].indirect(so), T.t1[:], T.ns[:], OP.max, "t1 ns " + sk_, "BK", x=SCAT)
         if last:
-            dma(T.ybank[:], win, "BK", "yb", 4000)
+            dma(T.ybank[:], win, "BK", "yb", 512)
         mm("W E1 I nI", "PW", acc(PW[:, 0:128], (T.E1[:], I)) + acc(PW[:, 128:256], (T.W[:], I), (T.E1[:], nI)))
         act(T.WE[:], PW[:, 0:256], AF.Copy, "", "WE", bank="PW")
         mm("WE KB ONES rowC", "PW", acc(PW[:, 256:272], (one1, rowC), *[(T.KB[:, 15 - j:143 - j], T.WE[:, j::16]) for j in range(16)]))
@@ -420,36 +423,42 @@ def build(g, T, topo, core):
         ts(T.P12[:], D12[:], 0.0, OP.is_gt, "D12", "P12", s2=0.5, o2=OP.subtract, x=0.5)
         ts(T.N12[:], D12[:], 0.0, OP.is_lt, "D12", "N12", s2=0.5, o2=OP.subtract, x=0.5)
         act(T.S21[:], PW[:, 0:256], AF.Sign, "", "S21", bias=-0.5, bank="PW")
-        cnt = PW[0:56, 256:384]
+        cnt = PR[0:56, 256:384]
 
         def row(j, buf, i):
             return (T.SM[:, 48 - 8 * j:104 - 8 * j], buf[:, 128 * i:128 * i + 128])
-        mm("H GM0 GM1 GM2 GM3 P12 SM", "PW", acc(cnt, (GM, T.H[0:16, :]), row(0, T.P12, 0), row(2, T.P12, 1), stop=False), grp="gcnt")
-        mm("N12 SM", "PW", acc(cnt, row(1, T.N12, 0), row(4, T.N12, 1), start=False, stop=False), grp="gcnt")
-        mm("S21 SM", "PW", acc(cnt, row(3, T.S21, 0), row(5, T.S21, 1), start=False), grp="gcnt")
-        act(T.B[0:56, :], cnt, AF.Sign, "", "B", bias=-0.5, bank="PW")
+        mm("H GM0 GM1 GM2 GM3 P12 SM", "PR", acc(cnt, (GM, T.H[0:16, :]), row(0, T.P12, 0), row(2, T.P12, 1), stop=False), grp="gcnt")
+        mm("N12 SM", "PR", acc(cnt, row(1, T.N12, 0), row(4, T.N12, 1), start=False, stop=False), grp="gcnt")
+        mm("S21 SM", "PR", acc(cnt, row(3, T.S21, 0), row(5, T.S21, 1), start=False), grp="gcnt")
+        act(T.B[0:56, :], cnt, AF.Sign, "", "B", bias=-0.5, bank="PR")
         mm("B M10 M11 M12 M13 M14", "PW", acc(PW[0:40, 384:512], (M1, T.B[0:56, :])))
         act(T.XT[0:40, :], PW[0:40, 384:512], AF.Sign, "", "XT", bias=-5.0, bank="PW")
-        mm("XT CO0 CO1 CO2 CO3", "PR", [(PR[:, 128 * j:128 * j + 128], T.CO[0:40, 128 * j:128 * j + 128], T.XT[0:40, :], True, True) for j in range(4)])
+
+        def ranks(out, js):
+            return [(out[:, 128 * i:128 * i + 128], T.CO[0:40, 128 * j:128 * j + 128], T.XT[0:40, :], True, True) for i, j in enumerate(js)]
+        mm("XT CO0 CO1", "PR", ranks(PR, (0, 1)))
+        mm("XT CO2 CO3", "PW", ranks(PW, (2, 3)))
         tt(T.TD[:], PR[:, 0:256], D12[:], OP.mult, "D12", "TD", bank="PR")
-        tt(T.FD[:], PR[:, 256:512], T.TD[:], OP.mult, "TD", "FD", bank="PR")
+        tt(T.FD[:], PW[:, 0:256], T.TD[:], OP.mult, "TD", "FD", bank="PW")
         half = [(T.hI[:], T.FD[:, 0:128]), (T.hI[:], T.FD[:, 128:256])]
-        cross = t <= NST - 3
-        if cross:
+        mm(k + " I nI ivm", "PS", acc(PS[:, 0:128], (I, z), (nI, T.ivm[:]), stop=False), grp="gn")
+        if t <= NST - 3:
             bu = T["Bu%d" % d][:]
-            mm(k + " I nREP TD Bu%d" % d, "PW", acc(PW[:, 0:128], (I, z), (T.nREP[:], bu), (I, T.TD[:, 0:128]), (I, T.TD[:, 128:256]), stop=False), grp="gm")
-            mm(k + " I nI hI REP FD Bu%d" % d, "PW", acc(PW[:, 0:128], (nI, T.FD[:, 0:128]), (nI, T.FD[:, 128:256]), start=False)
-               + acc(PW[:, 128:256], (I, z), (T.REP[:], bu), *half), grp="gm")
             cr = T.CR[:, 256 * t:256 * t + 256]
-            act(cr, PW[:, 0:256], AF.Identity, "", "CR%d" % t, bias=-32.0, bank="PW")
-            send([cr[:, 0:128], cr[:, 128:256]], "CR%d" % t, 2, t + 2)
-        mm(k + " I nI hI ivm FD", "PR", acc(PR[:, 0:128], (I, z), (nI, T.ivm[:]), *half))
-        act(T.r[:], PR[:, 0:128], AF.Relu, "", "r", bank="PR")
+            mm(k + " I nREP TD Bu%d" % d, "PR", acc(PR[:, 0:128], (I, z), (T.nREP[:], bu), (I, T.TD[:, 0:128]), (I, T.TD[:, 128:256]), stop=False), grp="gm")
+            mm("nI FD", "PR", acc(PR[:, 0:128], (nI, T.FD[:, 0:128]), (nI, T.FD[:, 128:256]), start=False), grp="gm")
+            act(cr[:, 0:128], PR[:, 0:128], AF.Identity, "", "CM%d" % t, bias=-32.0, bank="PR")
+            mm(k + " I hI REP FD Bu%d" % d, "PW", acc(PW[:, 256:384], (I, z), (T.REP[:], bu), *half))
+            act(cr[:, 128:256], PW[:, 256:384], AF.Identity, "", "CF%d" % t, bias=-32.0, bank="PW")
+            send([cr[:, 0:128], cr[:, 128:256]], "CM%d CF%d" % (t, t), 2, t + 2)
+        mm("hI FD", "PS", acc(PS[:, 0:128], *half, start=False), grp="gn")
+        act(T.r[:], PS[:, 0:128], AF.Relu, "", "r", bank="PS")
         tt(T.IM[:].indirect(so), T.ivm[:], T.r[:], OP.add, "ivm r " + sk_, "IM", x=SCAT)
         if last:
-            dma(T.yimm[:], T.IM[:, 0:1024], "IM", "yi", 3000)
+            dma(T.yimm[:], T.IM[:, 0:1024], "IM", "yi", 256)
 
     send([T.ZB[:, 128:256]], "ZB", 1, 1)
+    dma(T.G2[:], T.geno[:], "Z1", "G2", 1024)
     prep(0)
     hosts(0)
     for t in range(NST):
@@ -535,7 +544,15 @@ def schedule(q, dur, nxt, cnt, key):
 
 
 TRIES = 300
-WAKE = 60
+
+
+def lag_of(ops, i, j, ordered):
+    a, b = ops[j], ops[i]
+    if ordered:
+        return 50 - DFIX if b["q"] == "s" else 0
+    if a["q"] == "t":
+        return 0 if b["q"] == "t" and not b["hard"] else WAKE + PLAT
+    return WAKE
 
 
 def improve(ops, need, order):
@@ -545,10 +562,7 @@ def improve(ops, need, order):
     nxt, prv = [[] for _ in range(n)], [[] for _ in range(n)]
     for i in range(n):
         for j in sorted(need[i] | order[i]):
-            if j in order[i]:
-                lag = 60 - dur[j] if q[i] == "s" else 0
-            else:
-                lag = 0 if q[i] == q[j] == "t" and not ops[i]["hard"] else WAKE
+            lag = lag_of(ops, i, j, j in order[i])
             nxt[j].append((i, lag))
             prv[i].append((j, lag))
     cur = [0.0] * n

import numpy as np
from concourse.bass import DstId, RemoteDMATransfer
from concourse.mybir import AluOpType as OP, AxisListType, ActivationFunctionType as AF

NST = 5
ND = 64
NR = 64
DIST = ((0, 128),)
BT_ACT = ()
SG_DVE = (1, 2, 3, 4)
TW = 1280
BIG = 2.0 ** 20

SCRATCH = {}


def _bufs(names, cols, dtype, where="sbuf"):
    for n in names.split():
        SCRATCH[n] = (where, [128, cols], dtype)


_bufs("G G2", 4096, "bfloat16")
_bufs("X0 X1 AB", 2048, "bfloat16")
_bufs("BKI", 1024, "int32")
_bufs("BK", TW, "float32")
_bufs("IM", TW, "bfloat16")
_bufs("BT EQ", 1024, "bfloat16")
_bufs("zr0 zr1", 16 * ND, "bfloat16")
_bufs("zr4", 4 * ND, "bfloat16")
_bufs("CO", 512, "bfloat16")
_bufs("CR", 768, "bfloat16")
_bufs("THR", 272, "bfloat16")
_bufs("ZB WE D12 P12 N12 S21 TD FD zz0 zz1", 256, "bfloat16")
_bufs("KB", 144, "bfloat16")
_bufs("GM", 56, "bfloat16")
_bufs("Z1 Z2 Z3 Z4 ONES I nI hI KF D4 nI16 nI256 BO MK MK2 RS D8W BO8 REP nREP WH WL SM sm ROWS BD BE Bu0 Bu1 DM "
      "qt Fs ivm Sg sk H W E1 wq S B XT r", 128, "bfloat16")
_bufs("R8 G16 nG16", 8, "bfloat16")
_bufs("ab", 288, "float32")
_bufs("hb", 272, "float32")
_bufs("s3", 144, "float32")
_bufs("c e2 t1 ns mU AL", 128, "float32")
_bufs("pf tw", 64, "float32")
_bufs("R8f iw y sq nwi hc", 8, "float32")
_bufs("cg cm c8 bi bm", 128, "int32")
_bufs("pc vi vm0 vm1", 16, "int32")
_bufs("WI", 1, "int32")
_bufs("Ui u so", 8, "int32")
_bufs("b16", 128, "uint16")
_bufs("go0 go1 oX", 16, "uint16")
_bufs("sf0 sf1", 8, "uint16")
_bufs("PK PQ PA PB PS PW PR PD", 512, "float32", "psum")

SEMAPHORES = ["sv", "sa", "st", "sg", "ls"] + ["dm%d" % i for i in range(9)] + ["rz%d" % t for t in range(1, 5)]
CNT = {"v": "sv", "a": "sa", "t": "st", "g": "sg"}
CY, GATH, SCAT = 0.83, 1.56, 3.8
VFIX, AFIX, PCY = 40, 80, 0.42
DFIX, DKIB = 1500, 2.56
FIRST, RLAT = 5000, 1700
WAKE, PLAT = 110, 150


def build(g, T, topo, core):
    ops = []
    V, S, PE = g.vector, g.scalar, g.tensor

    def op(q, dur, reads, writes, *fns, bank=None, sem=None, hard=False):
        ops.append({"q": q, "dur": dur, "r": reads.split(), "w": writes.split(), "f": fns, "b": bank, "sem": sem, "hard": hard})

    def dv(ap, x):
        return VFIX + max(64.0, ap.shape[1] * x) * CY

    def copy(out, in_, r, w, bank=None, x=1.0):
        op("v", dv(in_, x), r, w, lambda: V.tensor_copy(out, in_), bank=bank)

    def tt(out, in0, in1, o, r, w, bank=None, x=None):
        op("v", dv(in1, x or (1.0 if bank else 2.0)), r, w, lambda: V.tensor_tensor(out, in0, in1, o), bank=bank)

    def ts(out, in0, s1, o1, r, w, s2=None, o2=None, bank=None, x=1.0):
        if o2 is None:
            op("v", dv(out, x), r, w, lambda: V.tensor_scalar(out, in0, s1, None, o1), bank=bank)
        else:
            op("v", dv(out, x), r, w, lambda: V.tensor_scalar(out, in0, s1, s2, o1, o2), bank=bank)

    def scan(out, d0, d1, init, o0, o1, r, w, bank=None):
        op("v", dv(out, 1.0), r, w, lambda: V.tensor_tensor_scan(out, d0, d1, init, o0, o1), bank=bank)

    def reduce_(out, in_, r, w):
        op("v", dv(in_, 1.0), r, w, lambda: V.tensor_reduce(out, in_, AxisListType.X, OP.add))

    def memset(ap, val, w):
        op("v", dv(ap, 0.5), "", w, lambda: V.memset(ap, val))

    def act(out, in_, f, r, w, bias=0.0, scale=1.0, bank=None, x=1.0, accum=None):
        d = AFIX + max(64.0, out.shape[1] * x) * CY
        if accum is None:
            op("a", d, r, w, lambda: S.activation(out, in_, f, bias, scale), bank=bank)
        else:
            op("a", d + 20, r, w, lambda: S.activation(out, in_, f, bias, scale, accum_out=accum), bank=bank)

    def mm(r, bank, calls, grp="", hard=False, x=1):
        def one(a):
            return lambda: PE.matmul(*a)
        d = sum(PCY * x * max(min(64, a[1].shape[1]), a[2].shape[1]) for a in calls)
        op("t", d, r, grp, *[one(a) for a in calls], bank=bank, hard=hard)

    def acc(out, *terms, start=True, stop=True):
        n = len(terms)
        return [(out, a, b, start and i == 0, stop and i == n - 1) for i, (a, b) in enumerate(terms)]

    def select(out, in_, pattern, cmp_, base, cm, r, w):
        op("g", 170 + 2 * CY * out.shape[1], r, w, lambda: g.affine_select(out, in_, pattern, cmp_, 0.0, base, cm))

    def pcopy(out, in_, r, w):
        select(out, in_, [[1, in_.shape[1]]], OP.is_ge, 0, 0, r, w)

    def iota(out, pattern, base, cm, w, r="", cast=False):
        d = 130 + 2 * CY * out.shape[1]
        if cast:
            op("g", d, r, w, lambda: g.iota(out, pattern, base, cm, allow_small_or_imprecise_dtypes=True))
        else:
            op("g", d, r, w, lambda: g.iota(out, pattern, base, cm))

    nd = [0]

    def dma(out, in_, r, w, kib):
        s = "dm%d" % nd[0]
        nd[0] += 1
        op("s", DFIX + kib * DKIB, r, w, lambda: g.sync.dma_start(out, in_), sem=(s, 16))

    dma(T.WI[:], T.wt[:], "", "WI", 1)
    dma(T.ZB[:], T.bites[:], "", "ZB", 64)
    dma(T.BKI[:], T.bank[:], "", "BKI", 512)
    dma(T.G[:], T.geno[:], "", "G", 1024)
    dma(T.IM[:, 0:1024], T.immun[:], "", "IM", 256)

    rank = T.rank_of(core)
    cores = list(T.cores)
    nr = len(cores)

    def engs(src, dst):
        return topo.engines(src, dst)[:8]

    def send(srcs, key, hop, t):
        dst = cores[(rank + hop) % nr]
        e = engs(core, dst)
        m = sum(1 << x for x in e)
        a = topo.addr(dst)
        zt, rs = T["Z%d" % t], T.sem["rz%d" % t]
        if len(srcs) == 1:
            f = lambda: g.remote_dma(zt[:], srcs[0], rs, T.sem.ls, a[1], a[0], m)
        else:
            f = lambda: g.remote_dma_fused([RemoteDMATransfer(dst_ids=[DstId(rid=a[0], pnc=a[1])], dma_engine_mask=m, remote_sem=rs,
                                                              srcs=list(srcs), dsts=[zt[:]], alu_op=2)], local_sem=T.sem.ls)
        op("g", 300, key, "sent%d" % t, f, sem=("ls", len(e)))
        op("n", FIRST if t == 1 else RLAT, "sent%d" % t, "Z%d" % t, sem=("rz%d" % t, len(engs(cores[(rank - hop) % nr], core))))

    pc, pf, tw = T.pc, T.pf, T.tw

    def col(i, n=1):
        return pf[:, i:i + n]

    memset(T.ONES[:], 1.0, "ONES")
    iota(pc[:, 0:1], [[1, 1]], 0, 1, "pI")
    iota(T.cm[:], [[0, 8], [1, 16]], 0, 0, "cm")
    for j, (s, o) in enumerate(((15, OP.bitwise_and), (7, OP.bitwise_and), (3, OP.logical_shift_right), (16, OP.bitwise_and),
                                (4, OP.logical_shift_right))):
        ts(pc[:, 1 + j:2 + j], pc[:, 0:1], s, o, "pI", "i%d" % j)
    copy(col(0, 5), pc[:, 1:6], "i0 i1 i2 i3 i4", "fp")
    iota(T.cg[:], [[1, 8], [0, 16]], 0, 0, "cg")
    ts(T.BO[:], T.cg[:], col(4), OP.is_equal, "cg fp", "BO")
    R8 = T.R8[:]
    act(R8, T.BO[:, 0::16], AF.Copy, "BO", "R8")
    act(T.R8f[:], T.BO[:, 0::16], AF.Copy, "BO", "R8f")
    ts(T.MK[:], T.cm[:], col(0), OP.is_equal, "cm fp", "MK")
    ts(pc[:, 8:9], T.WI[:], 4032, OP.bitwise_and, "WI", "i8")
    ts(pc[:, 9:10], T.WI[:], 63, OP.bitwise_and, "WI", "i9")
    copy(col(8, 2), pc[:, 8:10], "i8 i9", "fw")
    act(T.WH[:], T.BO[:], AF.Copy, "BO fw", "WH", scale=col(8))
    act(T.WL[:], T.BO[:], AF.Copy, "BO fw", "WL", scale=col(9))
    select(T.I[:], T.ONES[:], [[-1, 128]], OP.is_equal, 0, 1, "ONES", "I")
    for name, val in (("nI", -1.0), ("KF", 8192.0), ("nI16", -16.0), ("nI256", -256.0), ("hI", 0.5)):
        act(T[name][:], T.I[:], AF.Copy, "I", name, scale=val)
    act(T.G16[:], R8, AF.Copy, "R8", "G16", scale=16.0)
    act(T.nG16[:], R8, AF.Copy, "R8", "nG16", scale=-16.0)
    select(T.RS[:], T.ONES[:], [[0, 8], [1, 16]], OP.is_gt, 0, 0, "ONES", "RS")
    iota(T.ROWS[0:2, :], [[-32768, 8], [0, 16]], 8192 + 7 * 32768, 0, "ROWS", "", True)
    iota(T.ROWS[0:1, :], [[0, 8], [-1, 16]], 15, 0, "ROWS", "", True)
    memset(T.THR[:], BIG, "THR")
    for o in (0, 144):
        iota(T.THR[:, o:o + 128:16], [[-32768, 8]], 16384 + 7 * 32768, 0, "THR%d" % o, "THR", True)
    memset(T.ab[:, 128:288], 0.0, "abp")
    memset(T.ab[:, 143:144], BIG, "abp")
    memset(T.c[:, 0:1], 0.0, "c")
    memset(T.s3[:, 128:144], 0.0, "s3p")
    for d in range(2):
        memset(T["zz%d" % d][:], 0.0, "zz%d" % d)
    iota(T.tw[:, 63:64], [[1, 1]], 0, 4, "p4", cast=True)
    act(T.D4[:], T.I[:], AF.Copy, "I p4", "D4", scale=tw[:, 63:64])
    ts(col(48, 10), T.MK[:, 0:10], -2.0, OP.mult, "MK", "flip", s2=1.0, o2=OP.add)
    memset(T.BT[:, 0:1], -1.0, "BT")
    for j in range(10):
        if j in BT_ACT:
            act(T.BT[:, 1 << j:2 << j], T.BT[:, 0:1 << j], AF.Copy, "BT flip", "BT", scale=col(48 + j))
        else:
            ts(T.BT[:, 1 << j:2 << j], T.BT[:, 0:1 << j], col(48 + j), OP.mult, "BT flip", "BT", x=0.5)
    memset(tw[:, 16:24], 0.0, "tw1")
    ts(col(11), col(3), 1.0 / 16, OP.mult, "fp", "odd")
    ts(col(12), col(3), 0.0, OP.is_equal, "fp", "even")
    memset(tw[:, 48:56], 1.0 / 64, "tw3")
    scan(tw[:, 32:40], tw[:, 48:56], tw[:, 16:24], 64.0, OP.mult, OP.add, "tw3 tw1", "tw2")
    tt(tw[:, 48:56], tw[:, 32:40], R8, OP.mult, "tw2 R8", "tw3")
    reduce_(col(13), tw[:, 48:56], "tw3", "f13")
    op("v", 250, "f13", "f14", lambda: V.reciprocal(col(14), col(13)))
    ts(col(15), col(14), 8192.0, OP.mult, "f14", "f15")
    ts(tw[:, 0:16], T.cm[:, 0:16], col(0), OP.is_gt, "cm fp", "tw0", s2=1.9375, o2=OP.mult)
    WT, rowC, rowN = T.sm[:, 0:16], T.sm[0:1, 16:32], T.sm[0:1, 32:40]
    ts(WT, tw[:, 0:16], 0.0625, OP.add, "tw0 f13", "WT", s2=col(13), o2=OP.mult)
    act(T.MK2[:], T.MK[:], AF.Copy, "MK f15", "MK2", scale=col(15))
    memset(rowN, -14336.0, "rowN")
    iota(T.iw[:], [[16, 8]], 1024, 1, "iw", cast=True)
    iota(rowC, [[0, 2], [256, 8]], 0, 0, "rowC", cast=True)
    ts(col(16), col(0), 16.0, OP.mult, "fp", "f16")
    memset(T.KB[:], 0.0, "KB")
    act(T.KB[:, 15:143:16], R8, AF.Copy, "R8 fp KB", "KB", scale=col(0))
    iota(T.c8[:], [[0, 16], [1, 8]], 0, 0, "c8")
    ts(T.D8W[:], T.cg[:], col(1), OP.is_equal, "cg fp", "D8W")
    ts(col(17), col(2), 0.0, OP.is_equal, "fp", "f17", s2=2.0, o2=OP.mult)
    ts(col(18), col(17), -1.0, OP.add, "f17", "f18")
    D16, L1, L2, GM, M1 = T.sm[:, 40:56], T.sm[:, 56:72], T.sm[0:8, 72:88], T.GM[0:16, :], T.sm[0:56, 88:128]
    ts(D16, T.c8[:, 0:16], col(1), OP.is_equal, "c8 fp f18", "D16", s2=col(18), o2=OP.mult)
    for j in range(2):
        act(T.sm[:, 56 + 8 * j:64 + 8 * j], R8, AF.Copy, "R8", "L1%d" % j, scale=-0.5)
    act(L2, T.sm[0:8, 40:56], AF.Copy, "D16", "L2", scale=-8.0)
    act(T.BO8[0:8, :], T.D8W[0:8, :], AF.Copy, "D8W", "BO8", scale=-256.0)
    ts(T.AL[0:16, :], T.ONES[0:16, :], pf[0:16, 18:19], OP.mult, "ONES f18", "AL", s2=-32.0, o2=OP.mult)
    memset(T.SM[:], 0.0, "SM")
    act(T.SM[:, 48:56], R8, AF.Copy, "R8 SM", "SM")
    memset(T.GM[0:16, 0:16], 0.0, "GM0")
    act(T.GM[0:16, 16:32], T.sm[0:16, 40:56], AF.Copy, "D16", "GM1", scale=-32.0)
    act(T.GM[0:16, 32:48], T.sm[0:16, 40:56], AF.Copy, "D16", "GM2", scale=32.0)
    act(T.GM[0:16, 48:56], T.sm[0:16, 40:48], AF.Copy, "D16", "GM3", scale=0.375)
    E = 20
    ts(col(E, 7), T.cm[:, 0:7], col(2), OP.is_equal, "cm fp", "E")
    tt(col(28, 2), col(E, 2), col(E + 2, 2), OP.add, "E", "n01")
    tt(col(30), col(E + 4), col(E + 5), OP.add, "E", "n2")
    ts(col(31), col(E + 6), 4.0, OP.mult, "E", "g4")
    ts(col(32, 2), col(29, 2), col(31), OP.add, "n01 n2 g4", "ng")
    ts(col(34, 2), col(32, 2), -1.0, OP.mult, "ng n01", "s01", s2=col(28), o2=OP.add)
    tt(col(36), col(29), col(33), OP.subtract, "n01 ng", "s2")
    ts(col(37), col(E + 6), 8.0, OP.mult, "E", "s3c")
    for j in range(4):
        act(T.sm[:, 88 + 8 * j:96 + 8 * j], T.D8W[:, 0::16], AF.Copy, "D8W s01 s2 s3c", "M1%d" % j, scale=col(34 + j))
    memset(T.sm[:, 120:128], 0.0, "M14")
    tt(col(38), col(E + 2), col(E + 3), OP.add, "E", "k0")
    tt(col(39), col(E), col(38), OP.subtract, "E k0", "k1")
    tt(col(40), col(E + 1), col(E + 2), OP.add, "E", "k2")
    ts(col(41), col(39), col(E + 4), OP.subtract, "k1 E", "co0", s2=0.5, o2=OP.mult)
    ts(col(42), col(40), 0.5, OP.mult, "k2 E", "co1", s2=col(E + 4), o2=OP.subtract)
    ts(col(43), col(39), col(E + 4), OP.add, "k1 E", "co2", s2=0.5, o2=OP.mult)
    ts(col(44), col(40), 0.5, OP.mult, "k2", "co3")
    for j in range(4):
        act(T.CO[:, 128 * j:128 * j + 128], T.D8W[:], AF.Copy, "D8W co%d" % j, "CO%d" % j, scale=col(41 + j))
    ts(T.nREP[:], T.c8[:], col(0), OP.is_equal, "c8 fp", "nREP", s2=32.0, o2=OP.mult)
    tt(T.REP[:], T.nREP[:], T.BO[:], OP.mult, "nREP BO", "REP")
    act(T.nREP[:], T.REP[:], AF.Copy, "REP", "nREP", scale=-1.0)

    PK, PQ, PS, PW, PR, PD = T.PK, T.PQ, T.PS, T.PW, T.PR, T.PD
    I, nI, RS = T.I[:], T.nI[:], T.RS[:]
    one1, one2 = T.ONES[0:1, :], T.ONES[0:2, :]

    def zap(t):
        return T.ZB[:, 0:128] if t == 0 else T["Z%d" % t][:]

    def zk(t):
        return "ZB" if t == 0 else "Z%d" % t

    def prep(t):
        z, k, d = zap(t), zk(t), t % 2
        mm(k + " WH WL", "PD", acc(PD[:, 0:128], (z, T.WH[:]), (z, T.WL[:])))
        tt(T.mU[:], PD[:, 0:128], T.MK[:], OP.mult, "MK", "mU", bank="PD")
        mm("mU R8f", "PD", acc(PD[:, 128:136], (T.mU[:], T.R8f[:])), x=4)
        copy(T.Ui[:], PD[:, 128:136], "", "Ui", bank="PD")
        ts(T.u[:], T.Ui[:], 4095, OP.bitwise_and, "Ui", "u")
        ts(T.y[:], T.u[:], 1184.0, OP.add, "u", "y")
        tt(T.vi[:, 0:8] if t == 0 else T.sq[:], T.u[:], T.y[:], OP.mult, "u y", "vi" if t == 0 else "sq")
        if t <= NST - 3:
            ts(T.vi[:, 8:16], T.u[:], 32.0, OP.mult, "u", "vu")
        for j in range(4):
            pcopy(T.zr4[:, j::4], z[:, 0:ND], k, "zr4%d" % j)
        for h in range(ND // 32):
            for j in range(4):
                pcopy(T["zr%d" % d][:, 512 * h + j:512 * h + 512:4], T.zr4[:, 128 * h:128 * h + 128], "zr40 zr41 zr42 zr43", "zr%d%d%d" % (d, h, j))
        for j in range(2):
            pcopy(T["zz%d" % d][:, 128 * j + ND:128 * j + 128], z[:, ND:128], k + " zz%d" % d, "zz%d%d" % (d, j))

    def hosts(t):
        d, n = t % 2, 16 if t <= NST - 3 else 8
        if t:
            ts(T.vi[:, 0:8], T.sq[:], PS[:, 384:385], OP.add, "sq", "vi", s2=65536.0, o2=OP.add, bank="PS")
        ts(T["vm%d" % d][:, 0:n], T.vi[:, 0:n], 5, OP.logical_shift_right, "vi vu", "vm%d" % d, s2=1023, o2=OP.bitwise_and)
        copy(T["go%d" % d][:, 0:n], T["vm%d" % d][:, 0:n], "vm%d" % d, "go%d" % d)

    def dups(t):
        d = t % 2
        go, gk = T["go%d" % d][:, 0:8], "go%d" % d
        act(T.BD[:], T.BT[:].indirect(go), AF.Copy, "BT odd " + gk, "BD", scale=col(11), x=GATH)
        act(T.BE[:], T.BT[:].indirect(go), AF.Copy, "BT even " + gk, "BE", scale=col(12), x=GATH)
        for h in range(2):
            for j in range(2):
                calls = []
                for i in range(2):
                    bx = (T.BD if i else T.BE)[64 * h + 32 * j:64 * h + 32 * j + 32, :]
                    calls.append((PD[:, 256 * j + 128 * i:256 * j + 128 * i + 128], bx, bx, True, True))
                mm("BD BE", "PD", calls, grp="gdup", hard=bool(j))
            act(T.EQ[:, 512 * h:512 * h + 512], PD[:], AF.Relu, "", "EQ%d" % h, bias=-15.0, bank="PD")
        mm("EQ0 EQ1 WT", "PD", [(PD[:, 16 * j:16 * j + 16], T.EQ[:, 128 * j:128 * j + 128], WT, True, True) for j in range(8)])
        tt(T.DM[:], PD[:, 0:128], T.MK2[:], OP.mult, "MK2", "DM", bank="PD")
        mm("DM R8 ONES rowN", "PD", acc(PD[:, 128:136], (one1, rowN), (T.DM[:], R8)))
        tt(T.nwi[:], PD[:, 128:136], T.iw[:], OP.min, "iw", "nwi", bank="PD")
        tt(T.so[:], T["vm%d" % d][:, 0:8], T.nwi[:], OP.max, "nwi vm%d" % d, "so")
        copy(T["sf%d" % d][:], T.so[:], "so", "sf%d" % d)
        if t <= NST - 3:
            act(T["Bu%d" % d][:], T.BT[:].indirect(T["go%d" % d][:, 8:16]), AF.Copy, "BT " + gk, "Bu%d" % d, x=GATH)

    def main(t):
        d = t % 2
        z, k = zap(t), zk(t)
        last = t == NST - 1
        go, gk = T["go%d" % d][:, 0:8], "go%d" % d
        X, xk = T["X%d" % d], "X%d" % d
        win = T.BK[:, 0:1024]
        if t == 0:
            copy(T.bi[:], T.BKI[:].indirect(go), "BKI " + gk, "bi", x=GATH)
            copy(win, T.BKI[:], "BKI", "BK")
        else:
            copy(T.bi[:], win.indirect(go), "BK " + gk, "bi", x=GATH)
        ts(T.bm[:], T.bi[:], 4095, OP.bitwise_and, "bi", "bm")
        copy(T.b16[:], T.bm[:], "bm", "b16")
        act(T.qt[:], win.indirect(go), AF.Identity, "BK " + gk, "qt", bias=129.5 + 2.0 ** -14, scale=1.0 / 4096, x=GATH)
        nv = ND // 32
        for e in range(4):
            off, out = T.b16[:, 32 * e:32 * e + 32], X[:, 512 * e:512 * e + 512]
            if e < nv:
                tt(out, T.G[:].indirect(off), T["zr%d" % d][:, 512 * e:512 * e + 512], OP.subtract,
                   "G b16 " + " ".join("zr%d%d%d" % (d, e, j) for j in range(4)), xk + str(e), x=GATH)
                if 32 * e < NR:
                    ts(T.AB[:, 512 * e:512 * e + 512], out, 0.0, OP.max, xk + str(e), "AB%d" % e, s2=2.0, o2=OP.mult, x=0.5)
                else:
                    act(T.AB[:, 512 * e:512 * e + 512], out, AF.Abs, xk + str(e), "AB%d" % e)
            else:
                act(out, T.G[:].indirect(off), AF.Copy, "G b16", xk + str(e), x=GATH)
        act(T.Fs[:], T.qt[:], AF.Sign, "qt", "Fs", bias=-(131.5 + t))
        key = PK[:, 0:128]
        mm("Fs KF ROWS ONES", "PK", acc(key, (one2, T.ROWS[0:2, :]), (T.Fs[:], T.KF[:]), stop=False), grp="gkey")
        mm("qt nI16 ROWS ONES", "PQ", acc(PQ[:, 128:256], (one2, T.ROWS[0:2, :]), (T.qt[:], T.nI16[:])))

        def dist(src, lo, hi, rhs, r, stop):
            mm(r, "PK", [(PK[lo:hi, kk:128:16], src[:, 16 * lo + kk:16 * hi:16], rhs, False, stop and kk == 15) for kk in range(16)], grp="gkey")

        def scalar_lanes(e):
            bank = "PA" if e % 2 else "PB"
            mm(k + " nI", bank, [(T[bank][:, kk::16], nI, z[:, 32 * e:32 * e + 32], kk == 0, False) for kk in range(16)], grp="g" + bank)
            mm(xk + str(e) + " I", bank, acc(T[bank][:], (I, X[:, 512 * e:512 * e + 512]), start=False), grp="g" + bank)
            act(T.AB[:, 512 * e:512 * e + 512], T[bank][:], AF.Abs, "", "AB%d" % e, bank=bank)
        for e in range(nv, 4):
            scalar_lanes(e)
        if NR:
            dist(X, 0, NR, T.nG16[:], "nG16 " + " ".join(xk + str(e) for e in range(NR // 32)), False)
        for lo, hi in DIST:
            dist(T.AB, lo, hi, T.G16[:], "G16 " + " ".join("AB%d" % e for e in range(lo // 32, hi // 32)), True)
        if not last:
            pcopy(T.G[:, t::32], z, k, "G")
        pcopy(T.G2[:, t::32], z, k, "G2")
        if last:
            dma(T.ygeno[:], T.G2[:], "G2", "yg", 1024)
        dups(t)
        act(T.ivm[:], T.IM[:, 0:1024].indirect(go), AF.Identity, "IM " + gk, "ivm", bias=-1.0, x=GATH)
        if t in SG_DVE:
            tt(T.Sg[:], T.IM[:, 0:1024].indirect(go), z, OP.is_lt, "IM %s %s" % (gk, k), "Sg", x=GATH)
        else:
            mm(k + " ivm I nI", "PS", acc(PS[:, 0:128], (I, z), (nI, T.ivm[:])))
            act(T.Sg[:], PS[:, 0:128], AF.Sign, "", "Sg", bias=-1.5, bank="PS")
        mm("Sg R8", "PS", acc(PS[0:8, 128:256], (R8, T.Sg[:])))
        act(T.sk[0:8, :], PS[0:8, 128:256], AF.Sign, "", "sk", bias=-8.5 if t in SG_DVE else -1.0, bank="PS")
        mm("Fs sk L10 L11 L2", "PS", acc(PS[0:16, 256:384], (L1, T.Fs[:]), (L2, T.sk[0:8, :])))
        act(T.H[0:16, :], PS[0:16, 256:384], AF.Relu, "f17", "H hc", bias=pf[0:16, 17:18], bank="PS", accum=None if last else T.hc[0:16, 0:1])
        if not last:
            mm("hc AL", "PS", acc(PS[:, 384:385], (T.AL[0:16, :], T.hc[0:16, 0:1])), x=4)
            prep(t + 1)
            hosts(t + 1)
        mm("qt sk nI16 BO8", "PQ", acc(PQ[:, 0:128], (T.qt[:], T.nI16[:]), (T.sk[0:8, :], T.BO8[0:8, :])))
        act(PQ[:, 0:128], PQ[:, 0:128], AF.Relu, "", "", bias=-2336.0, scale=-1.0, bank="PQ")
        ab, hb = T.ab, T.hb
        scan(ab[:, 0:128], RS, key, 0.0, OP.mult, OP.max, "RS", "a", bank="PK")
        tt(T.c[:, 1:128], ab[:, 0:127], PK[:, 1:128], OP.min, "a", "c", bank="PK")
        scan(ab[:, 144:272], T.c[:], RS, 0.0, OP.max, OP.mult, "c RS", "b")
        scan(hb[:], T.THR[:], ab[:, 15:287], BIG, OP.min, OP.max, "a b abp THR THR0 THR144", "hb")
        tt(T.W[:], key, hb[:, 144:272], OP.is_ge, "hb", "W", bank="PK")
        tt(T.E1[:], key, hb[:, 0:128], OP.is_ge, "hb", "E1", bank="PK")
        tt(T.wq[:], PQ[:, 0:128], T.W[:], OP.mult, "W", "wq", bank="PQ")
        tt(T.e2[:], PQ[:, 128:256], T.wq[:], OP.add, "wq", "e2", bank="PQ")
        scan(T.s3[:, 0:128], RS, T.e2[:], 0.0, OP.mult, OP.max, "e2 RS", "s3")
        scan(PK[:, 128:256], RS, T.s3[:, 15:143], 0.0, OP.mult, OP.max, "s3 s3p RS", "hb3", bank="PK")
        tt(T.S[:], T.e2[:], PK[:, 128:256], OP.is_equal, "e2 hb3", "S", bank="PK")
        mm("wq nI256", "PQ", acc(PQ[:, 256:384], (T.wq[:], T.nI256[:])))
        tt(T.t1[:], T.bi[:], PQ[:, 256:384], OP.add, "bi", "t1", bank="PQ")
        mm("S D4 KF", "PK", acc(PK[:, 256:384], (T.S[:], T.D4[:]), (T.S[:], T.KF[:])))
        act(T.ns[:], PK[:, 256:384], AF.Identity, "", "ns", scale=8.0, bias=float(t + 4096 * (8 + t) - 65536), bank="PK")
        so, sk_ = T["sf%d" % d][:], "sf%d" % d
        tt(T.BK[:].indirect(so), T.t1[:], T.ns[:], OP.max, "t1 ns " + sk_, "BK", x=SCAT)
        if last:
            dma(T.ybank[:], win, "BK", "yb", 512)
        mm("W E1 I nI", "PW", acc(PW[:, 0:128], (T.E1[:], I)) + acc(PW[:, 128:256], (T.W[:], I), (T.E1[:], nI)))
        act(T.WE[:], PW[:, 0:256], AF.Copy, "", "WE", bank="PW")
        mm("WE KB ONES rowC", "PW", acc(PW[:, 256:272], (one1, rowC), *[(T.KB[:, 15 - j:143 - j], T.WE[:, j::16]) for j in range(16)]))
        ts(T.oX[:], PW[:, 256:272], col(16), OP.add, "f16", "oX", bank="PW")
        D12 = T.D12
        tt(D12[:], X[:].indirect(T.oX[:]), T["zz%d" % d][:], OP.subtract,
           "oX zz%d0 zz%d1 " % (d, d) + " ".join(xk + str(e) for e in range(4)), "D12", x=GATH)
        d1, d2 = D12[:, 0:128], D12[:, 128:256]
        mm("D12 I nI", "PW", acc(PW[:, 0:128], (I, d2), (nI, d1)) + acc(PW[:, 128:256], (I, d1), (nI, d2)))
        ts(T.P12[:], D12[:], 0.0, OP.is_gt, "D12", "P12", s2=0.5, o2=OP.subtract, x=0.5)
        ts(T.N12[:], D12[:], 0.0, OP.is_lt, "D12", "N12", s2=0.5, o2=OP.subtract, x=0.5)
        act(T.S21[:], PW[:, 0:256], AF.Sign, "", "S21", bias=-0.5, bank="PW")
        cnt = PR[0:56, 256:384]

        def row(j, buf, i):
            return (T.SM[:, 48 - 8 * j:104 - 8 * j], buf[:, 128 * i:128 * i + 128])
        mm("H GM0 GM1 GM2 GM3 P12 SM", "PR", acc(cnt, (GM, T.H[0:16, :]), row(0, T.P12, 0), row(2, T.P12, 1), stop=False), grp="gcnt")
        mm("N12 SM", "PR", acc(cnt, row(1, T.N12, 0), row(4, T.N12, 1), start=False, stop=False), grp="gcnt")
        mm("S21 SM", "PR", acc(cnt, row(3, T.S21, 0), row(5, T.S21, 1), start=False), grp="gcnt")
        act(T.B[0:56, :], cnt, AF.Sign, "", "B", bias=-0.5, bank="PR")
        mm("B M10 M11 M12 M13 M14", "PW", acc(PW[0:40, 384:512], (M1, T.B[0:56, :])))
        act(T.XT[0:40, :], PW[0:40, 384:512], AF.Sign, "", "XT", bias=-5.0, bank="PW")

        def ranks(out, js):
            return [(out[:, 128 * i:128 * i + 128], T.CO[0:40, 128 * j:128 * j + 128], T.XT[0:40, :], True, True) for i, j in enumerate(js)]
        mm("XT CO0 CO1", "PR", ranks(PR, (0, 1)))
        mm("XT CO2 CO3", "PW", ranks(PW, (2, 3)))
        tt(T.TD[:], PR[:, 0:256], D12[:], OP.mult, "D12", "TD", bank="PR")
        tt(T.FD[:], PW[:, 0:256], T.TD[:], OP.mult, "TD", "FD", bank="PW")
        half = [(T.hI[:], T.FD[:, 0:128]), (T.hI[:], T.FD[:, 128:256])]
        mm(k + " I nI ivm", "PS", acc(PS[:, 0:128], (I, z), (nI, T.ivm[:]), stop=False), grp="gn")
        if t <= NST - 3:
            bu = T["Bu%d" % d][:]
            cr = T.CR[:, 256 * t:256 * t + 256]
            mm(k + " I nREP TD Bu%d" % d, "PR", acc(PR[:, 0:128], (I, z), (T.nREP[:], bu), (I, T.TD[:, 0:128]), (I, T.TD[:, 128:256]), stop=False), grp="gm")
            mm("nI FD", "PR", acc(PR[:, 0:128], (nI, T.FD[:, 0:128]), (nI, T.FD[:, 128:256]), start=False), grp="gm")
            act(cr[:, 0:128], PR[:, 0:128], AF.Identity, "", "CM%d" % t, bias=-32.0, bank="PR")
            mm(k + " I hI REP FD Bu%d" % d, "PW", acc(PW[:, 256:384], (I, z), (T.REP[:], bu), *half))
            act(cr[:, 128:256], PW[:, 256:384], AF.Identity, "", "CF%d" % t, bias=-32.0, bank="PW")
            send([cr[:, 0:128], cr[:, 128:256]], "CM%d CF%d" % (t, t), 2, t + 2)
        mm("hI FD", "PS", acc(PS[:, 0:128], *half, start=False), grp="gn")
        act(T.r[:], PS[:, 0:128], AF.Relu, "", "r", bank="PS")
        tt(T.IM[:].indirect(so), T.ivm[:], T.r[:], OP.add, "ivm r " + sk_, "IM", x=SCAT)
        if last:
            dma(T.yimm[:], T.IM[:, 0:1024], "IM", "yi", 256)

    send([T.ZB[:, 128:256]], "ZB", 1, 1)
    dma(T.G2[:], T.geno[:], "Z1", "G2", 1024)
    prep(0)
    hosts(0)
    for t in range(NST):
        main(t)
    return ops


def depend(ops):
    lw, rd, bank, rdy, prev = {}, {}, {}, [], []
    lastdma = None
    for i, o in enumerate(ops):
        need, order = set(), set()
        for k in o["r"]:
            if k in lw:
                need.add(lw[k])
            rd.setdefault(k, []).append(i)
        for k in o["w"]:
            if k in lw:
                need.add(lw[k])
            need |= set(rd.get(k, ()))
        for k in o["w"]:
            lw[k] = i
            rd[k] = []
        if o["b"]:
            h = bank.setdefault(o["b"], [None, set(), set(), None])
            if h[0] != o["q"]:
                h[0], h[1], h[2] = o["q"], h[2], set()
            elif o["q"] == "t":
                order.add(h[3])
            need |= h[1]
            h[2].add(i)
            h[3] = i
        if o["q"] == "s":
            if lastdma is not None:
                order.add(lastdma)
            lastdma = i
        need.discard(i)
        rdy.append(need)
        prev.append(order - need)
    return rdy, prev


def schedule(q, dur, nxt, cnt, key):
    n = len(q)
    left = cnt[:]
    avail, start, fin, seq = [0.0] * n, [0.0] * n, [0.0] * n, []
    ready = {k: [] for k in "vatgsn"}
    free = dict.fromkeys("vatgsn", 0.0)
    for i in range(n):
        if left[i] == 0:
            ready[q[i]].append(i)
    best, dirty = {}, list("vatgsn")
    while len(seq) < n:
        for k in dirty:
            r = ready[k]
            if not r:
                best.pop(k, None)
                continue
            f = free[k]
            t0 = max(f, min([avail[i] for i in r]))
            bi, bp = -1, -1e18
            for i in r:
                if avail[i] <= t0 and key[i] > bp:
                    bp, bi = key[i], i
            best[k] = (t0, bi)
        k = min(best, key=lambda x: best[x])
        st, i = best[k]
        ready[k].remove(i)
        seq.append(i)
        start[i], fin[i] = st, st + dur[i]
        free[k] = st + 60 if k == "s" else (0.0 if k == "n" else fin[i])
        dirty = [k]
        for j, lag in nxt[i]:
            av = fin[i] + lag
            if av > avail[j]:
                avail[j] = av
            left[j] -= 1
            if left[j] == 0:
                ready[q[j]].append(j)
                if q[j] not in dirty:
                    dirty.append(q[j])
    return max(fin), seq, start, fin


TRIES = 300


def lag_of(ops, i, j, ordered):
    a, b = ops[j], ops[i]
    if ordered:
        return 50 - DFIX if b["q"] == "s" else 0
    if a["q"] == "t":
        return 0 if b["q"] == "t" and not b["hard"] else WAKE + PLAT
    return WAKE


def improve(ops, need, order):
    rnd = np.random.RandomState(3)
    n = len(ops)
    q, dur = [o["q"] for o in ops], [o["dur"] for o in ops]
    nxt, prv = [[] for _ in range(n)], [[] for _ in range(n)]
    for i in range(n):
        for j in sorted(need[i] | order[i]):
            lag = lag_of(ops, i, j, j in order[i])
            nxt[j].append((i, lag))
            prv[i].append((j, lag))
    cur = [0.0] * n
    for i in range(n - 1, -1, -1):
        cur[i] = dur[i] + max([cur[j] + lag for j, lag in nxt[i]], default=0.0)
    best = None
    for _ in range(TRIES):
        r = schedule(q, dur, nxt, [len(x) for x in prv], cur)
        for _ in range(4):
            key = schedule(q, dur, prv, [len(x) for x in nxt], r[3])[3]
            r2 = schedule(q, dur, nxt, [len(x) for x in prv], key)
            if best is None or min(r, r2)[0] < best[0]:
                best = r2 if r2[0] < r[0] else r
            if r2[0] >= r[0] - 1:
                break
            r = r2
        key = schedule(q, dur, prv, [len(x) for x in nxt], best[3])[3]
        sg = (100.0, 400.0, 1500.0)[int(rnd.randint(3))]
        cur = [key[i] + sg * float(x) for i, x in enumerate(rnd.normal(size=n))]
    return best


PLAN = {}


def rank_program(g, core, T, topo):
    rank = T.rank_of(core)
    if rank is None:
        return
    ops = build(g, T, topo, core)
    if "seq" not in PLAN:
        need, order = depend(ops)
        PLAN["need"] = need
        PLAN["end"], PLAN["seq"], PLAN["start"], PLAN["fin"] = improve(ops, need, order)
    need, seq = PLAN["need"], PLAN["seq"]
    queue = {"v": g.vector, "a": g.scalar, "t": g.tensor, "g": g, "s": g.sync}
    count, done, known, clock = {}, {}, {}, {}
    for i in seq:
        o = ops[i]
        q = o["q"]
        kn = known.setdefault(q, {}) if q != "n" else {}
        for j in sorted(need[i], key=lambda x: -done[x][1]):
            s, v = done[j]
            if q == "t" and ops[j]["q"] == "t" and not o["hard"]:
                continue
            if kn.get(s, 0) >= v:
                continue
            if q != "n":
                queue[q].wait_ge(T.sem[s], v)
            for s2, v2 in clock[j].items():
                kn[s2] = max(kn.get(s2, 0), v2)
            kn[s] = max(kn.get(s, 0), v)
        ins = None
        for f in o["f"]:
            ins = f()
        if o["sem"] is None:
            s = CNT[q]
            count[s] = count.get(s, 0) + 1
            ins.then_inc(T.sem[s], 1)
        else:
            s, v = o["sem"]
            count[s] = count.get(s, 0) + v
            if q == "s":
                ins.then_inc(T.sem[s], v)
        done[i] = (s, count[s])
        clock[i] = {} if q == "n" else dict(kn)
    kn = known["g"]
    for s in count:
        if kn.get(s, 0) < count[s]:
            g.wait_ge(T.sem[s], count[s])
